import numpy as np, ml_dtypes
CORES = [16,18,20,22]
N = 4
BF = ml_dtypes.bfloat16
def gentries(a):
    return np.ascontiguousarray(a.reshape(8, 16, -1).transpose(0, 2, 1)).reshape(8, -1)
def gtable(e):
    e = np.asarray(e); return np.ascontiguousarray(e.reshape(8, -1, 16).transpose(0, 2, 1)).reshape(128, -1).astype(np.int32)
W, S, L, RO, RW, BC, BR = 4096, 16, 256, 4, 2, 2, 3
def people(rng, street, fame, one):
    sh = (N, 8, 16, W); col = np.arange(W) % S
    a = np.where(rng.random(sh) < street, S * rng.integers(0, L, sh) + col, rng.integers(0, W, sh))
    st = rng.integers(0, L, (N * 8, 24)); star = S * np.take_along_axis(st, rng.integers(0, 24, (N * 8, 16 * W)), 1).reshape(sh) + col
    a = np.where(rng.random(sh) < fame, star, a)
    return np.where(rng.random((N, 8, 1, W)) < one, a[:, :, :1], a)
def strangers(rng, *sh):
    return S * rng.integers(0, L, sh + (W,)) + (np.arange(W) + rng.integers(1, S, sh + (W,))) % S
def pack(x, a, tt):
    return {"x": np.ascontiguousarray(np.reshape(x, (N, 128, W))).astype(np.float32).astype(BF), "aq": np.ascontiguousarray(np.reshape(a, (N, 128, W))).astype(np.int32),
            "tg": np.stack([gtable(b) for b in tt])}
def mixed(rng):
    return people(rng, rng.choice(np.array([0.3, 0.5, 0.7]), (N, 8, 1, 1)), rng.choice(np.array([0.0, 0.05, 0.15]), (N, 8, 1, 1)), 0.02)
def setup_inputs(rng):
    return pack(rng.integers(0, 256, (N, 8, 16, W)), mixed(rng), rng.integers(0, W, (N, 8, W)))
def setup_inputs_ties(rng):
    x = 127 * rng.integers(0, 3, (N, 8, 16, W)); a = mixed(rng)
    x[:, 0] = 255 * rng.integers(0, 2, (N, 1, W)); x[:, 1] = rng.integers(0, 2, (N, 16, W)); x[:, 3] = rng.integers(0, 256, (N, 16, 1))
    x[:, 5] = rng.integers(0, 256, (16, 4))[:, rng.integers(0, 4, (N, W))].transpose(1, 0, 2)
    a[:, 6, 8:] = a[:, 6, :8]; a[:, 7, 1:] = a[:, 7, :15]
    return pack(x, a, rng.integers(0, W, (N, 8, W)))
def setup_inputs_stars(rng):
    a = np.zeros((N, 8, 16, W), np.int64); ev = a[:, ::2].shape
    a[:, ::2] = S * rng.choice(np.array([0, 1, 2, 3, 4, 5, L - 8, L - 1]), ev) + np.arange(W) % S
    a[:, 1::2] = rng.choice(np.array([0, 1, W // 2, W - 2, W - 1]), ev)
    a = np.where(rng.random((N, 8, 1, W)) < 0.2, a[:, :, :1], a)
    return pack(rng.integers(0, 256, (N, 8, 16, W)), a, rng.choice(np.array([0, 1, W // 2, W - 2, W - 1, W // 4]), (N, 8, W)))
def setup_inputs_free(rng):
    a = mixed(rng); a[:, ::2] = strangers(rng, N, 4, 16)
    x = rng.integers(0, 256, (N, 8, 16, W)); x[:, :4] = x[:, :4] & 1; x[:, 4:6] = x[:, 4:6] & 63
    share = np.zeros((N, 6, 1, 1)); share[1::2, :2] = 1.0; share[:, 2:4] = 0.5; share[:, 4:6] = 0.03
    x[:, :6] = np.where(rng.random((N, 6, 1, W)) < share, 255 - x[:, :6], x[:, :6])
    return pack(x, a, rng.integers(0, W, (N, 8, W)))
def setup_inputs_chains(rng):
    a = mixed(rng); a[:, ::2] = strangers(rng, N, 4, 16)
    i = np.arange(L); bl = i[(i % 8 > RW) & (i % 8 <= RW + BC)]; n = len(bl)
    for q in range(N):
        for g in range(8):
            for t in range(RO):
                o = rng.permutation(bl); c = rng.integers(0, 6, n)
                nx = np.where(c == 0, rng.integers(0, L, n), np.where(c == 1, o, np.roll(o, -1)))
                nx[0] = o[0]; nx[1] = o[2]; nx[2] = o[1]; nx[3:10] = o[4:11]
                town = a[q, g]; town[:, S * o + t] = S * nx + t
    return pack(rng.integers(0, 256, (N, 8, 16, W)), a, rng.integers(0, W, (N, 8, W)))
def setup_inputs_spread(rng):
    x = np.minimum((np.exp2(8 * rng.random((N, 8, 1, W))) * rng.random((N, 8, 16, W))).astype(np.int64), 255)
    e = rng.choice(np.array([1.0, 2.0, 4.0]), (N, 8, 1, 1)); sh = (N, 8, 16, W)
    a = np.minimum((W * np.power(rng.random(sh), e)).astype(np.int64), W - 1)
    s = S * np.minimum((L * np.power(rng.random(sh), e)).astype(np.int64), L - 1) + np.arange(W) % S
    a = np.where(rng.random(sh) < rng.random((N, 8, 1, 1)), s, a)
    return pack(x, a, np.minimum((W * np.power(rng.random((N, 8, W)), e[:, :, 0])).astype(np.int64), W - 1))
def check_inputs(d):
    bad = []; xf = np.asarray(d["x"]).astype(np.float32)
    if not np.all((xf >= 0) & (xf <= 255) & (xf == np.floor(xf))): bad.append("whole numbers and range of x")
    for k in ("aq", "tg"):
        if np.min(d[k]) < 0 or np.max(d[k]) > W - 1: bad.append("range of " + k)
    return bad
def reference(x, aq, tg):
    xs = x.astype(np.float32).astype(np.int32).reshape(N, 8, 16, W); aw = aq.astype(np.int64).reshape(N, 8, 16, W)
    tt = np.stack([gentries(a) for a in tg]).astype(np.int64)
    lane = np.arange(L); role = lane % 8; ri = np.arange(N)[:, None]; gi = np.arange(8)[None, :]
    blk = (role > RW) & (role <= RW + BC)
    yx = np.zeros((N, 8, 16, RO, L), np.float32); ym = np.zeros((N, 8, RO, L), np.float32)
    for t in range(RO):
        v = S * lane + t; xv = xs[..., v]; own = aw[..., v]
        near = np.take_along_axis(xs, own.reshape(N, 8, 1, 16 * L), 3).reshape(N, 8, 16, 16, L)
        c = np.add.reduce(np.abs(near - xv[:, :, :, None, :]), axis=2); k = np.argmax(c, axis=2)
        tt[:, :, v] = np.take_along_axis(own, k[:, :, None, :], 2)[:, :, 0]
        uu = np.take_along_axis(own, ((k + 1) % 16)[:, :, None, :], 2)[:, :, 0]
        p = tt[:, :, v][..., 0::8]; o = uu[..., 0::8]; D = p.shape[-1]
        meet = (p[..., None] == p[:, :, None, :]) | (p[..., None] == o[:, :, None, :]) | (o[..., None] == p[:, :, None, :]) | (o[..., None] == o[:, :, None, :])
        void = (p == o) | np.any(meet & (np.tri(D, D, -1) > 0), axis=-1)
        s = np.zeros((N, 8, W), np.int64) + np.arange(W)
        q, g, i = np.nonzero(~void); s[q, g, p[q, g, i]] = o[q, g, i]; s[q, g, o[q, g, i]] = p[q, g, i]
        tt = np.take_along_axis(s, tt, 2); uu = np.take_along_axis(s, uu, 2)
        for w in range(1, RW + 1):
            place = tt[:, :, v][..., w::8]; val = uu[..., w::8]
            for i in range(place.shape[-1] - 1, -1, -1):
                tt[ri, gi, place[..., i]] = val[..., i]
        tv = tt[:, :, v]; bt = tv[..., blk]; b = np.zeros((N, 8, W), bool)
        for rnd in range(BR):
            q, g, i = np.nonzero(~b[:, :, v[blk]]); b = np.zeros((N, 8, W), bool); b[q, g, bt[q, g, i]] = True
        free = ~b[:, :, v]
        nx = []; nm = []
        for r in range(N):
            h = (r + 1 + t % (N - 1)) % N; a = tv[r]
            al = np.take_along_axis(aw[h], a[:, None, :], 2)
            far = np.take_along_axis(xs[h], al.reshape(8, 1, 16 * L), 2).reshape(8, 16, 16, L)
            e = np.add.reduce(np.abs(far - xv[r][:, :, None, :]), axis=1); k = np.argmin(e, axis=1)
            m = np.take_along_axis(al, k[:, None, :], 1)[:, 0]; xa = np.take_along_axis(xs[h], a[:, None, :], 2)
            nx.append(np.where(free[r][:, None, :], (xv[r] + xa) >> 1, xv[r])); nm.append(np.where(free[r], m, own[r, :, t]))
        nx = np.stack(nx); nm = np.stack(nm)
        xs[..., v] = nx; aw[:, :, t, v] = nm; yx[:, :, :, t] = nx; ym[:, :, t] = nm
    return {"yx": yx.reshape(N, 128, RO * L).astype(BF), "ym": ym.reshape(N, 8, RO * L).astype(np.float32), "yt": tt.astype(np.float32)}

@@ -1,0 +1,624 @@
+import numpy as np
+from concourse.bass import DstId, RemoteDMATransfer
+from concourse.mybir import AluOpType, ActivationFunctionType
+
+W, L, RO, N = 4096, 256, 4, 4
+WD = W + 64
+KF = 8192.0
+
+F32, BF, F16, I32, U16 = "float32", "bfloat16", "float16", "int32", "uint16"
+SB = {
+    BF: {"xA": W, "xB": W, "rep1": W, "rep2": W, "rep3": W, "near": W, "mc": W, "far": W, "xvc": RO * L, "xvin": RO * L, "nxc": RO * L,
+         "updin": 6 * L, "nev": L, "nsc": L, "new": 128, "wsc": 128, "at1": L, "a2": L, "at3": 4 * L, "idrow": 64, "lanerow": L,
+         "farp": L, "mvp": L, "xa": L, "hey": 128, "nhey": 128, "half": L, "z32": 144, "zm16": 144, "z16": 144, "eye": 128,
+         "neye": 128, "bo": 128, "oh": 48, "rst": L, "cvoid": L, "cwave": 64},
+    F16: {"ownh": RO * L, "nown": RO * L, "nownin": RO * L, "alh": L, "selv": L, "zh": 144, "boh": 128, "bok": 432},
+    I32: {"aqs": W, "tgs": L, "ki": 16, "kj": 16, "vi": 16, "vj": 16, "hx": L, "pi": 2, "ri": 2},
+    U16: {"tgu": L, "ownu": RO * L, "alist": RO * 16, "alin": RO * 16, "alu": L, "plist": 16, "ku": 16, "vu": 16, "ulist": RO * 8,
+          "tlist": 16, "soff": RO * 4, "woff": RO * 4, "prm": 64, "prr": 64},
+    F32: {"stab": WD, "tw": WD, "yy": WD, "dout": RO * L, "din": RO * L, "ymc": RO * L, "ksc": L, "vsc": L, "lsta": 16,
+          "rowpo": 96, "urow": RO * 128, "st1": 64, "zcol": 4, "asc": L, "ub": 64, "bsc": 64, "ucol": 4, "tm": 64, "swp": 64, "b2": L,
+          "vall": 3 * L, "nrow": L, "m16": L, "g16": 128, "m64": L, "vv": L, "act": L, "vw": 64, "actw": 64, "col": 16, "pf": 64,
+          "idf": 4, "idcol": 4, "ndum": 4, "nrm": 4, "kct": 4, "kcm": 4, "cfz": L, "cf2": L, "cmax": L, "cmin": L, "prow": L, "psc": L},
+}
+SCRATCH = {k: ("sbuf", [128, n], d) for d in SB for k, n in SB[d].items()}
+SCRATCH["mv"] = ("sbuf", [128, L, 16], BF)
+SCRATCH["sel"] = ("sbuf", [128, 2, L], F16)
+SCRATCH.update({"B%d" % b: ("psum", [128, 512], F32) for b in range(8)})
+UPD = [(0, 1), (0, 2), (1, 1), (1, 3), (2, 1)]
+SEMAPHORES = (["eV", "eS", "eP", "eG", "ldx", "ldq", "ldb", "ldt", "outs", "lsm", "lr1", "lr2", "lr3", "rr1", "rr2", "rr3"]
+              + ["rx%d" % t for t in range(RO)] + ["ra%d" % t for t in range(RO)] + ["rd%d" % t for t in range(RO)]
+              + ["ru%d" % k for k in range(len(UPD))])
+COSTS = [(1.56, 3.8, 0.5, 150.0), (1.15, 2.2, 0.45, 110.0), (1.95, 5.4, 0.65, 210.0)]
+CFG = {
+    "cg": ["SSVSSSSS"] * RO,
+    "mp": [0, 96, 160, 256],
+    "vg": ["SSSS", "SSSS", "SSSS", "VSVV"],
+    "yg": "SVSVSVSV", "bonus": 1500.0, "tries": 9000, "seed": 2, "temp": 50.0,
+}
+A = AluOpType
+AF = ActivationFunctionType
+
+
+def build(g, T, topo, rank, cost):
+    ops = []
+    V, S, P = g.vector, g.scalar, g.tensor
+    core = T.cores[rank]
+    GA, SCA, PE = cost[:3]
+
+    def op(eng, fns, dur, R, Wr, banks=(), kind="c", sem=None, lsem=None, cnt=0, lat=0.0, bulk=False):
+        ops.append(dict(e=eng, f=fns, d=float(dur), R=list(R), W=list(Wr), b=list(banks), k=kind, sem=sem, lsem=lsem,
+                        cnt=cnt, lat=lat, bulk=bulk))
+
+    def ts(out, in0, s1, s2, o0, o1, n, R, Wr, banks=()):
+        if o1 is None:
+            op("V", [lambda: V.tensor_scalar(out, in0, s1, None, o0)], max(64, n), R, Wr, banks)
+        else:
+            op("V", [lambda: V.tensor_scalar(out, in0, s1, s2, o0, o1)], max(64, n), R, Wr, banks)
+
+    def tt(out, a, b, o, n, R, Wr, banks=(), bulk=False):
+        op("V", [lambda: V.tensor_tensor(out, a, b, o)], max(64, n), R, Wr, banks, bulk=bulk)
+
+    def cp(out, a, n, R, Wr, banks=()):
+        op("V", [lambda: V.tensor_copy(out, a)], max(64, n), R, Wr, banks)
+
+    def ac(out, a, fn, n, R, Wr, banks=()):
+        op("S", [lambda: S.activation(out, a, fn)], max(64, n), R, Wr, banks, bulk=True)
+
+    def gcp(out, a, n, R, Wr):
+        op("G", [lambda: g.affine_select(out, a, [[0, n]], A.is_gt, 0.0, 1, 0)], 205 + 2 * n, R, Wr)
+
+    def scan(out, d0, d1, o0, o1, n, R, Wr, banks=()):
+        op("V", [lambda: V.tensor_tensor_scan(out, d0, d1, 0.0, o0, o1)], max(64, n), R, Wr, banks)
+
+    def mm(lst, R, Wr, banks, per=4, bulk=False):
+        for i in range(0, len(lst), per):
+            part = lst[i:i + per]
+            op("P", [(lambda m=m: P.matmul(m[0], m[1], m[2], m[3], m[4])) for m in part], sum(max(64, m[5]) for m in part) * PE + 15,
+               R, Wr, banks, bulk=bulk)
+
+    def gat(eng, out, win, off, n, R, Wr):
+        if eng == "V":
+            op("V", [lambda: V.tensor_copy(out, win.indirect(off))], 60 + GA * n, R, Wr, bulk=n > 256)
+        else:
+            op("S", [lambda: S.activation(out, win.indirect(off), AF.Copy)], 80 + GA * n, R, Wr, bulk=n > 256)
+
+    def sca(win, off, a, n, R, Wr):
+        op("V", [lambda: V.tensor_copy(win.indirect(off), a)], 60 + SCA * n, R, Wr)
+
+    def iota(out, pat, base, cm, n, Wr, fl=True):
+        if fl:
+            op("G", [lambda: g.iota(out, pat, base, cm, allow_small_or_imprecise_dtypes=True)], 160 + 2 * n, [], Wr)
+        else:
+            op("G", [lambda: g.iota(out, pat, base, cm)], 160 + 2 * n, [], Wr)
+
+    def dma(eng, out, a, sem, R, Wr, lat):
+        q = g.sync if eng == "Y" else g.scalar
+        op(eng, [lambda: q.dma_start(out, a)], 100, R, Wr, kind="d", sem=sem, cnt=16, lat=lat)
+
+    def send(dist, pairs, sem, lsem, R, Wr, lat):
+        dst = T.cores[(rank + dist) % N]
+        rid, pid, _ = topo.addr(dst)
+        eng = topo.engines(core, dst)
+        per = len(eng) // len(pairs)
+        masks = [sum(1 << e for e in eng[i * per:(i + 1) * per]) for i in range(len(pairs))]
+        if len(pairs) == 1:
+            fn = lambda: g.remote_dma(pairs[0][0], pairs[0][1], T.sem[sem], T.sem[lsem], pid, rid, masks[0])
+        else:
+            fn = lambda: g.remote_dma_fused([RemoteDMATransfer(dst_ids=[DstId(rid=rid, pnc=pid)], dma_engine_mask=masks[i], remote_sem=T.sem[sem],
+                                                               src=pairs[i][1], dst=pairs[i][0]) for i in range(len(pairs))], local_sem=T.sem[lsem])
+        op("G", [fn], 600, R, Wr, kind="r", sem=sem, lsem=lsem, cnt=per * len(pairs), lat=lat)
+
+    def nt(buf, t, w=L):
+        return buf[:, t * w:(t + 1) * w]
+
+    def runs(word, unit):
+        out, i = [], 0
+        while i < len(word):
+            j = i + 2 if (unit == 32 and i + 1 < len(word) and word[i + 1] == word[i]) else i + 1
+            out.append((i * unit, j * unit, word[i]))
+            i = j
+        return out
+
+    mp = CFG["mp"]
+    parts = [(mp[n], mp[n + 1]) for n in range(len(mp) - 1)]
+    aqw = T.aqs[:, 0:W]
+    dma("Y", T.xA[:], T.x[:], "ldx", [], ["xA"], 6500)
+    dma("S", T.aqs[:], T.aq[:], "ldq", [], ["aq"], 11000)
+    dma("Y", T.xB[:], T.x[:], "ldb", ["aq"], ["xB"], 6000)
+    dma("Y", T.tgs[:], T.tg[:], "ldt", ["aq"], ["tgs"], 7000)
+
+    col = T.col
+    rc, pc, gc15, gc0, r128, kc, r1, c15, cu, cv, t0 = [col[:, i:i + 1] for i in range(11)]
+    iota(T.pi[:], [[0, 2]], 0, 1, 2, ["pi"], False)
+    iota(T.nrow[:], [[1, L]], 0, 0, L, ["nrow"])
+    iota(T.m16[:], [[0, 16], [1, 16]], 0, 0, L, ["m16"])
+    for a, b in parts:
+        iota(T.prow[:, a:b], [[128, 16], [16, (b - a) // 32], [2048, 2]], a // 2, 0, b - a, ["prow%d" % a])
+    iota(T.pf[:], [[1, 4], [16, 8], [2048, 2]], 0, 0, 64, ["pf"])
+    iota(T.g16[:], [[16, 8], [0, 16]], 0, 0, 128, ["g16"])
+    iota(T.vv[:], [[-16, 2], [0, 4], [1, 32]], 0, 0, L, ["vv"])
+    iota(T.vw[:], [[-16, 2], [1, 32]], 0, 0, 64, ["vw"])
+    iota(T.m64[:], [[0, 4], [1, 64]], 0, 0, L, ["m64"])
+    iota(T.idrow[:], [[16, 2], [128, 32]], 48, 0, 64, ["idrow"])
+    iota(T.idf[:], [[16, 2], [2048, 2]], 48, 0, 4, ["idf"])
+    for h in range(4):
+        iota(T.stab[:, h * 1040:(h + 1) * 1040], [[1, 1040]], h * 1040, 0, 1040, ["stab%d" % h])
+    STAB0 = ["stab%d" % h for h in range(4)]
+    ts(T.ri[:], T.pi[:], 15, None, A.bitwise_and, None, 2, ["pi"], ["ri"])
+    cp(rc, T.ri[:, 0:1], 1, ["ri"], ["rc"])
+    cp(pc, T.pi[:, 0:1], 1, ["pi"], ["pc"])
+    tt(gc0, pc, rc, A.subtract, 1, ["pc", "rc"], ["gc0"])
+    ts(gc15, gc0, 15.0, None, A.add, None, 1, ["gc0"], ["gc15"])
+    ts(r128, rc, 128.0, None, A.mult, None, 1, ["rc"], ["r128"])
+    ts(T.prm[:], T.pf[:], r128, None, A.add, None, 64, ["pf", "r128"], ["prm"])
+    ts(T.idcol[:], T.idf[:], r128, None, A.add, None, 4, ["idf", "r128"], ["idcol"])
+    ts(kc, rc, 15.0, KF, A.is_lt, A.mult, 1, ["rc"], ["kc"])
+    ts(T.kct[:], T.nrow[:, 0:4], kc, None, A.add, None, 4, ["nrow", "kc"], ["kct"])
+    ts(T.kcm[:], T.nrow[:, 0:4], kc, None, A.subtract, None, 4, ["nrow", "kc"], ["kcm"])
+    ts(T.nrm[:], T.nrow[:, 0:4], rc, -1.0, A.is_equal, A.mult, 4, ["nrow", "rc"], ["nrm"])
+    ts(r1, rc, 1.0, None, A.add, None, 1, ["rc"], ["r1"])
+    ts(c15, rc, -1.0, 15.0, A.mult, A.add, 1, ["rc"], ["c15"])
+    ts(t0, rc, 0.0, -16.0, A.is_equal, A.mult, 1, ["rc"], ["t0"])
+    ts(cu, c15, 1.0, t0, A.add, A.add, 1, ["c15", "t0"], ["cu"])
+    ts(cv, rc, 15.0, r1, A.is_lt, A.mult, 1, ["rc", "r1"], ["cv"])
+    for i, (c, key) in enumerate(((c15, "c15"), (cu, "cu"), (cv, "cv"))):
+        ts(T.oh[:, 16 * i:16 * i + 16], T.nrow[:, 0:16], c, None, A.is_equal, None, 16, ["nrow", key], ["oh%d" % i])
+    for buf, sc, key in ((T.z32, 32.0, "z32"), (T.zm16, -16.0, "zm16"), (T.z16, 16.0, "z16"), (T.zh, 1.0, "zh")):
+        ts(buf[:], T.nrow[:, 0:144], gc15, sc, A.is_equal, A.mult, 144, ["nrow", "gc15"], [key])
+    for buf, sc, key in ((T.eye, 1.0, "eye"), (T.neye, -1.0, "neye"), (T.hey, 0.5, "hey"), (T.nhey, -0.5, "nhey")):
+        ts(buf[:], T.nrow[:, 0:128], pc, sc, A.is_equal, A.mult, 128, ["nrow", "pc"], [key])
+    ts(T.half[:], T.nrow[:], 0.0, 0.5, A.mult, A.add, L, ["nrow"], ["half"])
+    ts(T.bo[:], T.g16[:], gc0, KF, A.is_equal, A.mult, 128, ["g16", "gc0"], ["bo"])
+    ts(T.boh[:], T.g16[:], gc0, None, A.is_equal, None, 128, ["g16", "gc0"], ["boh"])
+    for t in range(RO - 1):
+        ts(nt(T.bok, t, 144), T.zh[:], T.nrm[:, t:t + 1], -1.0, A.mult, A.mult, 72, ["zh", "nrm"], ["bok%d" % t])
+    ts(T.cmax[:], T.m16[:], 0.0, -1000000.0, A.is_equal, A.mult, L, ["m16"], ["cmax"])
+    ts(T.cmax[:], T.cmax[:], 1.0, None, A.add, None, L, ["cmax"], ["cmax"])
+    ts(T.cmin[:], T.cmax[:], -1.0, None, A.mult, None, L, ["cmax"], ["cmin"])
+    ts(T.cfz[:], T.m16[:], rc, -20000.0, A.is_equal, A.mult, L, ["m16", "rc"], ["cfz"])
+    ts(T.cf2[:], T.m16[:], r1, KF, A.is_equal, A.mult, L, ["m16", "r1"], ["cf2"])
+    tt(T.cfz[:], T.cfz[:], T.cf2[:], A.add, 2 * L, ["cfz", "cf2"], ["cfz"])
+    scan(T.psc[:], T.cfz[:], T.prow[:], A.add, A.max, L, ["cfz"] + ["prow%d" % a for a, b in parts], ["psc"])
+    for t in range(RO):
+        ts(nt(T.prr, t, 16), T.psc[:, 15:L:16], T.kcm[:, t:t + 1], None, A.add, None, 16, ["psc", "kcm"], ["prr%d" % t])
+    ts(T.rst[:], T.m64[:], 0.0, None, A.is_gt, None, L, ["m64"], ["rst"])
+    ts(T.lanerow[:], T.nrow[:], 16.0, None, A.mult, None, L, ["nrow"], ["lanerow"])
+    ts(T.ndum[:], T.nrow[:, 0:64:16], rc, float(W), A.add, A.add, 4, ["nrow", "rc"], ["ndum"])
+    ts(T.ndum[:], T.ndum[:], -1.0, None, A.mult, None, 4, ["ndum"], ["ndum"])
+    for c1 in range(2):
+        a = 128 * c1 + 32
+        ts(T.vv[:, a:a + 32], T.vv[:, a:a + 32], -1.0, None, A.add, None, 32, ["vv"], ["vv"])
+    ts(T.act[:], T.vv[:], rc, None, A.is_lt, None, L, ["vv", "rc"], ["act"])
+    tt(T.cvoid[:, 1:L], T.act[:, 1:L], T.act[:, 0:L - 1], A.subtract, 2 * L, ["act"], ["cvoid"])
+    ts(T.cvoid[:, 0:L:128], T.act[:, 0:2], 0.0, 5.0, A.mult, A.add, 2, ["act", "cvoid"], ["cvoid"])
+    ts(T.actw[:], T.vw[:], rc, None, A.is_lt, None, 64, ["vw", "rc"], ["actw"])
+    tt(T.cwave[:, 1:64], T.actw[:, 1:64], T.actw[:, 0:63], A.subtract, 128, ["actw"], ["cwave"])
+    ts(T.cwave[:, 0:64:32], T.actw[:, 0:2], 0.0, 5.0, A.mult, A.add, 2, ["actw", "cwave"], ["cwave"])
+
+    def Z(buf, r):
+        return buf[:, 15 - r:143 - r]
+
+    send(-1, [(T.rep1[:], T.xA[:])], "rr1", "lr1", ["xA", "aq"], ["rep1"], 7000)
+    for t in range(RO):
+        gat("V", nt(T.ownu, t), aqw, nt(T.prr, t, 16), L, ["aq", "prr%d" % t], ["ownu%d" % t])
+        ts(nt(T.ownh, t), aqw.indirect(nt(T.prm, t, 16)), -2048.0, None, A.add, None, 60 + GA * L, ["aq", "prm"], ["ownh%d" % t])
+        if t == 0:
+            cp(nt(T.xvc, t), T.xA[:, t:W:16], 128, ["xA"], ["xvc%d" % t])
+        else:
+            gcp(nt(T.xvc, t), T.xA[:, t:W:16], L, ["xA"], ["xvc%d" % t])
+        ts(nt(T.nown, t), T.aqs[:, t:W:16], -2048.0, T.nrm[:, t:t + 1], A.add, A.mult, L, ["aq", "nrm"], ["nown%d" % t])
+        send(1 + t % 3, [(nt(T.xvin, t), nt(T.xvc, t)), (nt(T.nownin, t), nt(T.nown, t))], "rx%d" % t, "lsm",
+             ["xvc%d" % t, "nown%d" % t], ["xvin%d" % t, "nownin%d" % t], 3000)
+    cp(T.tgu[:], T.tgs[:], L, ["tgs"], ["tgu"])
+
+    def wave_offsets(t, w, zrow, zkey):
+        h = w - 1
+        st = T.st1[:, 32 * h:32 * h + 32]
+        scan(st, T.cfz[:, 0:32], zrow, A.add, A.max, 32, ["cfz", zkey], ["st1%d" % h])
+        for c1 in range(2):
+            o = 64 * h + 32 * c1
+            ts(T.new[:, o:o + 32], zrow, kc, T.st1[:, 32 * h + 16 * c1 + 15:32 * h + 16 * c1 + 16], A.add, A.not_equal, 32,
+               [zkey, "st1%d" % h, "kc"], ["new%d" % o])
+        ts(T.zcol[:, 2 * h:2 * h + 2], T.st1[:, 32 * h + 15:32 * h + 32:16], kc, None, A.subtract, None, 2, ["st1%d" % h, "kc"], ["zcol%d" % h])
+        scan(nt(T.wsc, h, 64), T.cwave[:], nt(T.new, h, 64), A.add, A.min, 32, ["cwave", "new%d" % (64 * h), "new%d" % (64 * h + 32)], ["wsc%d" % h])
+        for c1 in range(2):
+            o = 4 * t + 2 * h + c1
+            e = 64 * h + 32 * c1 + 31
+            ts(T.woff[:, o:o + 1], T.wsc[:, e:e + 1], T.ndum[:, c1:c1 + 1], T.zcol[:, 2 * h + c1:2 * h + c1 + 1],
+               A.mult, A.max, 1, ["wsc%d" % h, "ndum", "zcol%d" % h], ["woff%d" % o])
+
+    def redirect(win, key, t, w, more=()):
+        o = 4 * t + 2 * (w - 1)
+        sca(win, T.woff[:, o:o + 2], T.urow[:, 128 * t + 32 * (w - 1):128 * t + 32 * w], 32,
+            ["woff%d" % o, "woff%d" % (o + 1), "urow%d" % t] + list(more), [key])
+
+    def night(t):
+        s = str(t)
+        lst = []
+        for a, b in parts:
+            nc = (b - a) // 16
+            for c in range(a // 16, b // 16):
+                o = t * L + 128 * (c % 2) + c // 2
+                lst.append((T.B0[:, a + c - a // 16:b:nc], T.eye[:], T.xvc[:, o:o + 121:8], True, True, 16))
+        mm(lst, ["eye", "xvc" + s], ["xvP"], ["B0"])
+        for a, b, e in runs(CFG["cg"][t], 32):
+            gat(e, T.near[:, 16 * a:16 * b], T.xA[:, 0:W], T.ownu[:, t * L + a:t * L + b], 16 * (b - a), ["xA", "ownu" + s],
+                ["near%d" % u for u in range(a // 32, b // 32)])
+        for n, (a, b) in enumerate(parts):
+            nk = ["near%d" % u for u in range(a // 32, b // 32)]
+            w = b - a
+            for k in range(16):
+                tt(T.mc[:, 16 * a + k:16 * b:16], T.near[:, 16 * a + k:16 * b:16], T.B0[:, a:b], A.max, w, nk + ["xvP"], ["mc%d_%d" % (n, k)], ["B0"], True)
+            kb, kk, out = ("B4", "cnt3", T.B4[:, L:L + b]) if a == 0 else ("B2", "key", T.B2[:, a:b])
+            mm([(out, Z(T.zm16, r), T.near[:, 16 * a + w * r:16 * a + w * (r + 1)], r == 0, False, w) for r in range(16)], nk + ["zm16"], [kk], [kb])
+            mm([(out, Z(T.z32, r), T.mc[:, 16 * a + w * r:16 * a + w * (r + 1)], False, r == 15, w) for r in range(16)],
+               ["mc%d_%d" % (n, k) for k in range(16)] + ["z32"], [kk], [kb])
+            if b not in (96, L):
+                continue
+            a = 0 if b == 96 else 96
+            ca, cb, h = a // 16, b // 16, "A" if a == 0 else "B"
+            scan(T.ksc[:, a:b], T.cmax[:, a:b], out if a == 0 else T.B2[:, a:b], A.add, A.max, b - a, ["cmax", kk], ["ksc" + h], [kb])
+            cp(T.ki[:, ca:cb], T.ksc[:, a + 15:b:16], 1, ["ksc" + h], ["ki" + h])
+            ts(T.kj[:, ca:cb], T.ki[:, ca:cb], 15, None, A.bitwise_and, None, 1, ["ki" + h], ["kj" + h])
+            cp(T.ku[:, ca:cb], T.kj[:, ca:cb], 1, ["kj" + h], ["ku" + h])
+            for u in ((1, 0) if a == 0 else (1,)):
+                tt(T.sel[:, u, a:b], T.oh[:, 16 - 16 * u:32 - 16 * u].indirect(T.ku[:, ca:cb]), T.ownh[:, t * L + a:t * L + b], A.mult,
+                   60 + GA * (b - a), ["ku" + h, "oh%d" % (1 - u), "ownh" + s], ["sel%s%d" % (h, u)])
+            if a == 0:
+                mm([(T.B4[:, 0:12], Z(T.zh, r), T.sel[:, :, r:96:16], r == 0, r == 15, 12) for r in range(16)]
+                   + [(T.B4[:, 16:80], T.boh[:], T.sel[:, :, 0:32], True, True, 64), (T.B4[:, 80:112], T.boh[:], T.sel[:, 0, 0:32], True, True, 32)],
+                   ["selA0", "selA1", "zh", "boh"], ["lstP"], ["B4"], 18)
+                for c1 in range(2):
+                    for po in range(2):
+                        o = 128 * c1 + 64 * po
+                        ts(T.nev[:, o:o + 64], T.B4[:, 16:80], T.B4[:, 6 * po + c1:6 * po + c1 + 1], None, A.not_equal, None, 64,
+                           ["lstP"], ["nev%d" % o], ["B4"])
+                ts(T.lsta[:, 0:12], T.B4[:, 0:12], 2048.0, None, A.add, None, 12, ["lstP"], ["lsta"], ["B4"])
+                ts(T.rowpo[:], T.B4[:, 16:112], 2048.0, None, A.add, None, 96, ["lstP"], ["rowpo"], ["B4"])
+                ts(nt(T.ulist, t, 8), T.B4[:, 2:10], 2048.0, None, A.add, None, 8, ["lstP"], ["ulist" + s], ["B4"])
+                scan(T.nsc[:], T.cvoid[:], T.nev[:], A.add, A.min, 128, ["cvoid", "nev0", "nev64", "nev128", "nev192"], ["nsc"])
+                for po in range(2):
+                    for c1 in range(2):
+                        e = 2 * po + c1
+                        ts(T.soff[:, 4 * t + e:4 * t + e + 1], T.nsc[:, 128 * c1 + 127:128 * c1 + 128], T.ndum[:, e:e + 1],
+                           T.lsta[:, 6 * po + c1:6 * po + c1 + 1], A.mult, A.max, 1, ["nsc", "ndum", "lsta"], ["soff%d_%d" % (t, e)])
+                so = ["soff%d_%d" % (t, e) for e in range(4)]
+                sca(T.stab[:, 0:WD], nt(T.soff, t, 4), T.rowpo[:, 32:96], 64, so + ["rowpo"] + STAB0, ["stab"])
+                gat("V", nt(T.urow, t, 128), T.stab[:, 0:WD], nt(T.ulist, t, 8), 128, ["stab", "ulist" + s], ["urow" + s])
+                wave_offsets(t, 1, T.urow[:, 128 * t + 96:128 * t + 128], "urow" + s)
+            else:
+                mm([(T.B0[:, L:L + 16], Z(T.zh, r), T.sel[:, 1, 32 * (r % 8) + r // 8:32 * (r % 8) + 32:2], r == 0, r == 15, 16) for r in range(16)],
+                   ["selA1", "selB1", "zh"], ["lstT"], ["B0"], 16)
+                ts(T.tlist[:], T.B0[:, L:L + 16], 2048.0, None, A.add, None, 16, ["lstT"], ["tlist"], ["B0"])
+                gat("V", T.tw[:, t:W:16], T.stab[:, 0:WD], T.tlist[:], L, ["stab", "tlist"], ["tw"])
+        if t < RO - 1:
+            sca(T.stab[:, 0:WD], nt(T.soff, t, 4), T.rowpo[:, 0:64], 64, ["soff%d_%d" % (t, e) for e in range(4)] + ["rowpo"], ["stab"])
+        redirect(T.tw[:, 0:WD], "tw", t, 1)
+        wave_offsets(t, 2, T.tw[:, 32 + t:W:128], "tw")
+        redirect(T.tw[:, 0:WD], "tw", t, 2)
+        kt = T.kct[:, t:t + 1]
+        for o in range(2):
+            scan(T.bsc[:, 32 * o:32 * o + 32], T.cfz[:, 0:32], T.tw[:, 16 * (3 + o) + t:W:128], A.add, A.max, 32, ["cfz", "tw"], ["bsc%d" % o])
+        for c in range(4):
+            ts(T.at1[:, 64 * c:64 * c + 64], T.idrow[:], kt, T.bsc[:, 16 * c + 15:16 * c + 16], A.add, A.is_equal, 64,
+               ["idrow", "kct", "bsc%d" % (c // 2)], ["at1%d" % c])
+        for o in range(2):
+            ts(T.ub[:, 32 * o:32 * o + 32], T.tw[:, 16 * (3 + o) + t:W:128], float(-t), None, A.add, None, 32, ["tw"], ["ub%d" % o])
+        ts(T.ucol[:], T.bsc[:, 15:64:16], kt, None, A.subtract, None, 4, ["bsc0", "bsc1", "kct"], ["ucol"])
+        for c in range(4):
+            mm([(T.B4[:, 128:192], T.bo[:], T.at1[:, 64 * c:64 * c + 64], c == 0, c == 3, 64)], ["bo", "at1%d" % c], ["cnt1"], ["B4"])
+        scan(T.asc[:], T.cfz[:], T.tw[:, t:W:16], A.add, A.max, L, ["cfz", "tw"], ["asc"])
+        ts(nt(T.alist, t, 16), T.asc[:, 15:L:16], kc, None, A.subtract, None, 16, ["asc", "kc"], ["alist" + s])
+        send(1 + t % 3, [(nt(T.alin, t, 16), nt(T.alist, t, 16))], "ra" + s, "lsm", ["alist" + s], ["alin" + s], 2500)
+        if t == 0:
+            send(-2, [(T.rep2[:], T.xB[:])], "rr2", "lr2", ["xB", "alist0"], ["rep2"], 7000)
+        tt(T.tm[:], T.ub[:], T.B4[:, 128:192], A.add, 64, ["ub0", "ub1", "cnt1"], ["tm"], ["B4"])
+        for c in range(4):
+            ts(T.a2[:, 64 * c:64 * c + 64], T.tm[:], T.idcol[:, c:c + 1], None, A.is_equal, None, 64, ["tm", "idcol"], ["a2%d" % c])
+        scan(T.b2[:], T.rst[:], T.a2[:], A.mult, A.max, L, ["rst"] + ["a2%d" % c for c in range(4)], ["b2"])
+        for c in range(4):
+            ts(nt(T.at3, c), T.lanerow[:], T.ucol[:, c:c + 1], T.b2[:, 64 * c + 63:64 * c + 64], A.is_equal, A.is_gt, 128,
+               ["lanerow", "ucol", "b2"], ["at3%d" % c])
+            mm([(T.B4[:, L:2 * L], T.bo[:], nt(T.at3, c), c == 0, c == 3, L)], ["bo", "at3%d" % c], ["cnt3"], ["B4"])
+        free = nt(T.B5, t % 2)
+        fk = "free%d" % (t % 2)
+        ts(free, T.B4[:, L:2 * L], 0.0, None, A.is_equal, None, L, ["cnt3"], [fk], ["B4", "B5"])
+        d = 1 + t % 3
+        gat("S", T.xa[:], T["rep%d" % d][:, 0:W], nt(T.alist, t, 16), L, ["rep%d" % d, "alist" + s], ["xa"])
+        o = T.B2[:, L:2 * L]
+        mm([(o, T.nhey[:], nt(T.xvc, t), True, False, L), (o, T.nhey[:], T.half[:], False, False, L)], ["nhey", "half", "xvc" + s], ["dx"], ["B2"])
+        mm([(o, T.hey[:], T.xa[:], False, True, L)], ["hey", "xa"], ["dx"], ["B2"])
+        cp(T.hx[:], o, L, ["dx"], ["hx"], ["B2"])
+        tt(T.B4[:, L:2 * L], T.hx[:], free, A.mult, L, ["hx", fk], ["cnt3"], ["B4", "B5"])
+        if t < RO - 1:
+            tt(T.xA[:, t:W:16], nt(T.xvc, t), T.B4[:, L:2 * L], A.add, L, ["xvc" + s, "cnt3"], ["xA"], ["B4"])
+            gcp(nt(T.nxc, t), T.xA[:, t:W:16], L, ["xA"], ["nxc" + s])
+        else:
+            tt(nt(T.nxc, t), nt(T.xvc, t), T.B4[:, L:2 * L], A.add, L, ["xvc" + s, "cnt3"], ["nxc" + s], ["B4"])
+        dma("Y", T.yx[:, t * L:(t + 1) * L], nt(T.nxc, t), "outs", ["nxc" + s], [], 2500)
+        for k, (tu, du) in enumerate(UPD):
+            if tu == t:
+                send(-du, [(nt(T.updin, k), nt(T.nxc, t))], "ru%d" % k, "lsm", ["nxc" + s], ["updin%d" % k], 2500)
+                gcp(T["rep%d" % du][:, t:W:16], nt(T.updin, k), L, ["updin%d" % k], ["rep%d" % du])
+
+    def visit(t):
+        s = str(t)
+        gat("V", T.alu[:], aqw, nt(T.alin, t, 16), L, ["aq", "alin" + s], ["alu"])
+        if t == 0:
+            ts(T.alh[:], T.alu[:], -2048.0, None, A.add, None, 128, ["alu"], ["alh"])
+        else:
+            back(t - 1)
+            ts(T.alh[:], aqw.indirect(nt(T.alin, t, 16)), -2048.0, None, A.add, None, 60 + GA * L, ["aq", "alin" + s], ["alh"])
+        for a, b, e in runs(CFG["vg"][t], 64):
+            gat(e, T.far[:, 16 * a:16 * b], T.xB[:, 0:W], T.alu[:, a:b], 16 * (b - a), ["xB", "alu"], ["far%d" % (a // 64)])
+        for hf in range(2):
+            a, b = 128 * hf, 128 * hf + 128
+            fk = ["far%d" % (2 * hf), "far%d" % (2 * hf + 1)]
+            mk = ["mv%d_%d" % (hf, k) for k in range(16)]
+            xv = T.xvin[:, t * L + a:t * L + b]
+            for kq in range(4):
+                bn = "B%d" % (6 + kq % 2)
+                lst = []
+                ks = [kk for kk in range(4) if 4 * kq + kk != t - 1]
+                for kk in ks:
+                    o = nt(T[bn], kk, 128)
+                    lst += [(o, T.eye[:], T.far[:, 16 * a + 4 * kq + kk:16 * b:16], True, False, 128), (o, T.neye[:], xv, False, True, 128)]
+                mm(lst, fk + ["eye", "neye", "xvin" + s], [bn], [bn], 4, True)
+                for kk in ks:
+                    ac(T.mv[:, a:b, 4 * kq + kk], nt(T[bn], kk, 128), AF.Abs, 128, [bn], [mk[4 * kq + kk]], [bn])
+            mm([(T.B3[:, a:b], Z(T.z16, r), T.mv[:, a + r:b:16, :], r == 0, r == 15, 128) for r in range(16)], ["z16"] + mk, ["keyV"], ["B3"], 4, True)
+        if t > 0:
+            o = 144 * (t - 1) + 15
+            mm([(T.B1[:, L:L + 16], T.bok[:, o - r:o + 128 - r], T.alh[:, r:L:16], r == 0, r == 15, 16) for r in range(16)],
+               ["bok%d" % (t - 1), "alh"], ["eP"], ["B1"])
+            ts(T.plist[:], T.B1[:, L:L + 16], 2048.0, None, A.add, None, 16, ["eP"], ["plist"], ["B1"])
+            gat("S", T.farp[:], T.xB[:, 0:W], T.plist[:], L, ["xB", "plist"], ["farp"])
+            mm([(T.B6[:, 0:L], T.eye[:], T.farp[:], True, False, L), (T.B6[:, 0:L], T.neye[:], nt(T.xvin, t), False, True, L)],
+               ["farp", "eye", "neye", "xvin" + s], ["B6"], ["B6"])
+            ac(T.mvp[:], T.B6[:, 0:L], AF.Abs, L, ["B6"], ["mvp"], ["B6"])
+            mm([(T.B3[:, t - 1:L:16], Z(T.z16, r), T.mvp[:, r:L:16], r == 0, r == 15, 16) for r in range(16)], ["z16", "mvp"], ["keyV"], ["B3"])
+        if t < RO - 1:
+            gcp(T.xB[:, t:W:16], nt(T.nxc, t), L, ["nxc" + s], ["xB"])
+        if t == 0:
+            send(-3, [(T.rep3[:], T.xB[:])], "rr3", "lr3", ["xB"], ["rep3"], 7000)
+        scan(T.vsc[:], T.cmin[:], T.B3[:, 0:L], A.add, A.min, L, ["cmin", "keyV"], ["vsc"], ["B3"])
+        cp(T.vi[:], T.vsc[:, 15:L:16], 16, ["vsc"], ["vi"])
+        ts(T.vj[:], T.vi[:], 15, None, A.bitwise_and, None, 16, ["vi"], ["vj"])
+        cp(T.vu[:], T.vj[:], 16, ["vj"], ["vu"])
+        tt(T.selv[:], T.oh[:, 32:48].indirect(T.vu[:]), T.alh[:], A.mult, 60 + GA * L, ["vu", "oh2", "alh"], ["selv"])
+        mm([(T.B1[:, 0:L], Z(T.zh, t), nt(T.nownin, t), True, False, L)], ["zh", "nownin" + s], ["dP"], ["B1"])
+        mm([(T.B1[:, 0:L], Z(T.zh, t), T.selv[:], False, True, L)], ["zh", "selv"], ["dP"], ["B1"])
+        ac(nt(T.dout, t), T.B1[:, 0:L], AF.Copy, L, ["dP"], ["dout" + s], ["B1"])
+        send(-1 - t % 3, [(nt(T.din, t), nt(T.dout, t))], "rd" + s, "lsm", ["dout" + s], ["din" + s], 2800)
+
+    def back(t):
+        s = str(t)
+        tt(T.B1[:, L:2 * L], nt(T.din, t), nt(T.B5, t % 2), A.mult, L, ["din" + s, "free%d" % (t % 2)], ["eP"], ["B1", "B5"])
+        if t < RO - 1:
+            tt(T.aqs[:, t:W:16], T.aqs[:, t:W:16], T.B1[:, L:2 * L], A.add, L, ["aq", "eP"], ["aq"], ["B1"])
+            cp(nt(T.ymc, t), T.aqs[:, t:W:16], L, ["aq"], ["ymc" + s])
+        else:
+            tt(nt(T.ymc, t), T.aqs[:, t:W:16], T.B1[:, L:2 * L], A.add, L, ["aq", "eP"], ["ymc" + s], ["B1"])
+        dma("Y", T.ym[:, t * L:(t + 1) * L], T.ymc[t:128:16, t * L:(t + 1) * L], "outs", ["ymc" + s], [], 2500)
+
+    def targets():
+        st = T.stab[:, 0:WD]
+        for t in (2, 1, 0):
+            so = ["soff%d_%d" % (t, e) for e in range(4)]
+            gat("S", nt(T.vall, t), st, nt(T.alist, t, 16), L, ["stab", "alist%d" % t], ["vall%d" % t])
+            gat("V", T.swp[:, 0:32], st, T.soff[:, 4 * t + 2:4 * t + 4], 32, ["stab"] + so, ["swp0"])
+            gat("V", T.swp[:, 32:64], st, T.soff[:, 4 * t:4 * t + 2], 32, ["stab"] + so, ["swp1"])
+            sca(st, nt(T.soff, t, 4), T.swp[:], 64, so + ["swp0", "swp1"], ["stab"])
+            gat("S", T.urow[:, 128 * t:128 * t + 64], st, T.ulist[:, 8 * t:8 * t + 4], 64, ["stab", "ulist%d" % t], ["urow%d" % t])
+        q = 32
+        for n in range(L // q):
+            gat(CFG["yg"][n], T.yy[:, 16 * q * n:16 * q * (n + 1)], st, T.tgu[:, q * n:q * (n + 1)], 16 * q, ["stab", "tgu"], ["yy%d" % n])
+        for t in range(RO):
+            redirect(T.yy[:, 0:WD], "yy", t, 1, ["yy%d" % n for n in range(L // q)] if t == 0 else [])
+            redirect(T.yy[:, 0:WD], "yy", t, 2)
+            if t < RO - 1:
+                cp(T.yy[:, t:W:16], nt(T.vall, t), L, ["vall%d" % t], ["yy"])
+            else:
+                cp(T.yy[:, t:W:16], T.tw[:, t:W:16], L, ["tw"], ["yy"])
+        dma("Y", T.yt[:, :], T.yy[0:128:16, 0:W], "outs", ["yy"], [], 3000)
+
+    for t in range(RO):
+        night(t)
+        if t == RO - 1:
+            targets()
+        visit(t)
+    back(RO - 1)
+    return ops
+
+
+def depend(ops):
+    last, readers, epoch = {}, {}, {}
+    for i, o in enumerate(ops):
+        dep = {}
+
+        def add(j, how):
+            dep[(j, how)] = not (o["e"] == "P" and ops[j]["e"] == "P")
+        for k in o["R"]:
+            if k in last:
+                add(last[k], "w")
+        for k in o["W"]:
+            if k in last:
+                add(last[k], "w")
+            for j in readers.get(k, []):
+                if j != i:
+                    add(j, "r")
+        for b in o["b"]:
+            eng, cur, prev = epoch.get(b, (None, [], []))
+            if eng == o["e"]:
+                cur.append(i)
+            else:
+                eng, cur, prev = o["e"], [i], cur
+            for j in prev:
+                add(j, "w")
+            epoch[b] = (eng, cur, prev)
+        for k in o["R"]:
+            readers.setdefault(k, []).append(i)
+        for k in o["W"]:
+            last[k] = i
+            readers[k] = []
+        o["dep"] = [(j, how, wt) for (j, how), wt in dep.items()]
+
+
+def place(eng, dur, pred, prio):
+    n = len(eng)
+    p = list(prio)
+    for i in range(n):
+        for j, lt in pred[i]:
+            if p[j] >= p[i]:
+                p[i] = p[j] + 0.001
+    lo = {e: [] for e in "VSPGY"}
+    hi = {e: [] for e in "VSPGY"}
+    start = [0.0] * n
+    for i in sorted(range(n), key=lambda k: p[k]):
+        t = 0.0
+        for j, lt in pred[i]:
+            x = start[j] + dur[j] + lt
+            if x > t:
+                t = x
+        a, b, d = lo[eng[i]], hi[eng[i]], dur[i]
+        k = len(a)
+        while k > 0 and b[k - 1] > t:
+            k -= 1
+        while k < len(a) and a[k] < t + d:
+            t = max(t, b[k])
+            k += 1
+        a.insert(k, t)
+        b.insert(k, t + d)
+        start[i] = t
+    return start
+
+
+def replay(eng, dur, pred, tail, order):
+    fin, why, free, last = [0.0] * len(eng), [None] * len(eng), {e: 0.0 for e in "VSPGY"}, {e: None for e in "VSPGY"}
+    for i in order:
+        t, w = free[eng[i]], (last[eng[i]], True)
+        for j, lt in pred[i]:
+            if fin[j] + lt >= t:
+                t, w = fin[j] + lt, (j, False)
+        fin[i] = free[eng[i]] = t + dur[i]
+        why[i], last[eng[i]] = w, i
+    i = max(range(len(eng)), key=lambda k: fin[k] + tail[k])
+    end, pairs = fin[i] + tail[i], []
+    while i is not None:
+        if why[i][1] and why[i][0] is not None:
+            pairs.append((why[i][0], i))
+        i = why[i][0]
+    return end, pairs
+
+
+def schedule(sets):
+    ops = sets[0]
+    n = len(ops)
+    eng = [o["e"] for o in ops]
+    tail = [o["lat"] for o in ops]
+    durs = [[o["d"] for o in s] for s in sets]
+    preds = [[[(j, ops[j]["lat"] + (c[3] if wt else 0.0)) for j, how, wt in o["dep"]] for o in ops] for c in COSTS]
+    level = [durs[0][i] + tail[i] for i in range(n)]
+    last = list(level)
+    for i in range(n - 1, -1, -1):
+        for j, lt in preds[0][i]:
+            level[j] = max(level[j], durs[0][j] + lt + level[i])
+    group, names, count = [], {}, 0
+    for i, o in enumerate(ops):
+        key = (o["e"], (o["W"] + ["-"])[0].split("_")[0])
+        if key not in names or names[key][1] < i - 40:
+            names[key] = [count, i]
+            count += 1
+        names[key][1] = i
+        group.append(names[key][0])
+    group = np.array(group)
+    rs = np.random.RandomState(CFG["seed"])
+
+    def score(prio, bound=1e18):
+        st = place(eng, durs[0], preds[0], prio)
+        if max(st[k] + last[k] for k in range(n)) > bound:
+            return None
+        order = sorted(range(n), key=lambda k: (st[k], k))
+        res = [replay(eng, durs[m], preds[m], tail, order) for m in range(len(sets))]
+        return sum(x[0] for x in res) / len(res), np.array(st), order, res
+    top = best = score([-(level[i] + (0.0 if ops[i]["bulk"] else CFG["bonus"])) for i in range(n)])
+    for it in range(CFG["tries"]):
+        p = best[1].copy()
+        if it % 4:
+            pairs = best[3][rs.randint(len(sets))][1]
+            a, b = pairs[rs.randint(len(pairs))]
+            kind = rs.randint(4)
+            if kind == 0:
+                p[b] = p[a] - 1.0
+            elif kind == 1:
+                p[a] = p[b] + 1.0
+            elif kind == 2:
+                p[group == group[b]] -= p[b] - p[group == group[a]].min() + 1.0
+            else:
+                p[group == group[a]] += p[group == group[b]].max() - p[a] + 1.0
+        else:
+            near = np.unique(group[np.abs(p - rs.uniform(8000, p.max())) < 3000])
+            if len(near) == 0:
+                continue
+            for x in rs.choice(near, rs.randint(1, 4)):
+                p[group == x] += rs.normal() * rs.choice([300.0, 1200.0, 4000.0])
+        cand = score(p.tolist(), best[3][0][0] + 300.0)
+        if cand is not None and cand[0] <= best[0] + CFG["temp"] * (1.0 - it / CFG["tries"]) * rs.exponential():
+            best = cand
+        if best[0] < top[0]:
+            top = best
+    for i in range(n):
+        ops[i]["t"] = float(top[1][i])
+    return top[2], [x[0] for x in top[3]]
+
+
+MEMO = {}
+
+
+def rank_program(g, core, T, topo):
+    rank = T.rank_of(core)
+    if rank is None:
+        return
+    sets = [build(g, T, topo, rank, c) for c in (COSTS if "order" not in MEMO else COSTS[:1])]
+    ops = sets[0]
+    depend(ops)
+    if "order" not in MEMO:
+        MEMO["order"] = schedule(sets)[0]
+    order = MEMO["order"]
+    queue = {"V": g.vector, "S": g.scalar, "P": g.tensor, "G": g, "Y": g.sync}
+    total = {}
+    for i in order:
+        o = ops[i]
+        if o["k"] == "c":
+            sm = "e" + o["e"]
+            total[sm] = total.get(sm, 0) + len(o["f"])
+            o["tw"] = o["tr"] = (sm, total[sm])
+        else:
+            total[o["sem"]] = total.get(o["sem"], 0) + o["cnt"]
+            o["tw"] = o["tr"] = (o["sem"], total[o["sem"]])
+            if o["k"] == "r":
+                total[o["lsem"]] = total.get(o["lsem"], 0) + o["cnt"]
+                o["tr"] = (o["lsem"], total[o["lsem"]])
+    seen = {e: {} for e in queue}
+    for i in order:
+        o = ops[i]
+        q = queue[o["e"]]
+        need = {}
+        for j, how, wt in o["dep"]:
+            if wt:
+                sm, c = ops[j]["t" + how]
+                need[sm] = max(need.get(sm, 0), c)
+        for sm, c in need.items():
+            if seen[o["e"]].get(sm, 0) < c:
+                q.wait_ge(T.sem[sm], c)
+                seen[o["e"]][sm] = c
+        for f in o["f"]:
+            ins = f()
+            if o["k"] == "c":
+                ins.then_inc(T.sem["e" + o["e"]], 1)
+            elif o["k"] == "d":
+                ins.then_inc(T.sem[o["sem"]], 16)
+    for sm, c in total.items():
+        if max(seen[e].get(sm, 0) for e in seen) < c:
+            g.wait_ge(T.sem[sm], c)

@@ -3,67 +3,100 @@ from concourse.bass import DstId, RemoteDMATransfer
 from concourse.mybir import AluOpType, ActivationFunctionType
 
 W, L, RO, N = 4096, 256, 4, 4
-WD = W + 64
+WD = W + 256
 KF = 8192.0
+MAGIC = 12582912.0
 
 F32, BF, F16, I32, U16 = "float32", "bfloat16", "float16", "int32", "uint16"
 SB = {
-    BF: {"xA": W, "xB": W, "rep1": W, "rep2": W, "rep3": W, "near": W, "mc": W, "far": W, "xvc": RO * L, "xvin": RO * L, "nxc": RO * L,
-         "updin": 6 * L, "nev": L, "nsc": L, "new": 128, "wsc": 128, "at1": L, "a2": L, "at3": 4 * L, "idrow": 64, "lanerow": L,
-         "farp": L, "mvp": L, "xa": L, "hey": 128, "nhey": 128, "half": L, "z32": 144, "zm16": 144, "z16": 144, "eye": 128,
-         "neye": 128, "bo": 128, "oh": 48, "rst": L, "cvoid": L, "cwave": 64},
-    F16: {"ownh": RO * L, "nown": RO * L, "nownin": RO * L, "alh": L, "selv": L, "zh": 144, "boh": 128, "bok": 432},
-    I32: {"aqs": W, "tgs": L, "ki": 16, "kj": 16, "vi": 16, "vj": 16, "hx": L, "pi": 2, "ri": 2},
-    U16: {"tgu": L, "ownu": RO * L, "alist": RO * 16, "alin": RO * 16, "alu": L, "plist": 16, "ku": 16, "vu": 16, "ulist": RO * 8,
-          "tlist": 16, "soff": RO * 4, "woff": RO * 4, "prm": 64, "prr": 64},
-    F32: {"stab": WD, "tw": WD, "yy": WD, "dout": RO * L, "din": RO * L, "ymc": RO * L, "ksc": L, "vsc": L, "lsta": 16,
-          "rowpo": 96, "urow": RO * 128, "st1": 64, "zcol": 4, "asc": L, "ub": 64, "bsc": 64, "ucol": 4, "tm": 64, "swp": 64, "b2": L,
-          "vall": 3 * L, "nrow": L, "m16": L, "g16": 128, "m64": L, "vv": L, "act": L, "vw": 64, "actw": 64, "col": 16, "pf": 64,
-          "idf": 4, "idcol": 4, "ndum": 4, "nrm": 4, "kct": 4, "kcm": 4, "cfz": L, "cf2": L, "cmax": L, "cmin": L, "prow": L, "psc": L},
+    BF: {"xA": W, "rep1": W, "rep2": W, "rep3": W, "near": W, "far": W, "xvc": RO * L, "xvq": RO * L, "nxc": RO * L, "updin": 6 * L, "at1": L,
+         "a2": L, "at3": 4 * L, "idrow": 64, "lanerow": L, "farp": L, "mvp": L, "xa": L, "mh": L, "free": RO * L, "nbo": 128, "hey": 128, "nhey": 128,
+         "half": L, "z32": 144, "zm16": 144, "z16": 144, "eye": 128, "neye": 128, "bo": 128, "oh": 48, "rst": L},
+    F16: {"ownh": RO * L, "nown": RO * L, "alh": L, "selv": L, "zh": 144, "boh": 128, "bok": 432, "c128": 144, "eqd": 264,
+          "cvoid": 264, "nsc": 264},
+    I32: {"aqs": W, "aqr1": W, "aqr2": W, "aqr3": W, "tgs": L, "ki": 16, "kj": 16, "vi": 16, "vj": 16, "pi": 2, "ri": 2},
+    U16: {"tgu": L, "ownu": RO * L, "alist": RO * 16, "alu": L, "plist": 16, "ku": 16, "vu": 16, "ulist": RO * 10, "tlist": 16, "soff": RO * 4,
+          "woff": RO * 4, "repl": WD // 16, "prm": RO * 16, "prr": RO * 16},
+    F32: {"stab": WD, "tw": WD, "yy": WD, "ymc": RO * L, "ymin": 6 * L, "ksc": L, "vsc": L, "rowpo": 96, "st1": 64, "zcol": 2, "asc": L,
+          "ub": 64, "bsc": 64, "ucol": 4, "tm": 64, "swp": 64, "vall": 3 * L, "nrow": L, "urow": RO * 64, "zr1": 32, "b2": L, "kcm": 4,
+          "cwave": 68, "eqw": 136, "wsc": 136, "col": 16, "idf": 4, "idcol": 4, "dum": 2, "nrm": 8, "cfz": L, "cmax": L, "cmin": L},
 }
 SCRATCH = {k: ("sbuf", [128, n], d) for d in SB for k, n in SB[d].items()}
-SCRATCH["mv"] = ("sbuf", [128, L, 16], BF)
+SCRATCH.update({k: ("sbuf", [128, L, 16], BF) for k in ("mc", "mv")})
 SCRATCH["sel"] = ("sbuf", [128, 2, L], F16)
 SCRATCH.update({"B%d" % b: ("psum", [128, 512], F32) for b in range(8)})
-UPD = [(0, 1), (0, 2), (1, 1), (1, 3), (2, 1)]
-SEMAPHORES = (["eV", "eS", "eP", "eG", "ldx", "ldq", "ldb", "ldt", "outs", "lsm", "lr1", "lr2", "lr3", "rr1", "rr2", "rr3"]
-              + ["rx%d" % t for t in range(RO)] + ["ra%d" % t for t in range(RO)] + ["rd%d" % t for t in range(RO)]
-              + ["ru%d" % k for k in range(len(UPD))])
-COSTS = [(1.56, 3.8, 0.5, 150.0), (1.15, 2.2, 0.45, 110.0), (1.95, 5.4, 0.65, 210.0)]
+UPD = [(0, 2), (0, 3), (0, 1), (1, 3), (1, 1), (2, 1)]
+PIECES = 4
+SEMAPHORES = (["eV", "eS", "eP", "eG", "ldx", "ldt", "outs", "lsm"] + ["ldq%d" % p for p in range(PIECES)]
+              + ["lx1", "lx2", "lx3", "lq1", "lq3", "rx1", "rx2", "rx3", "rq0", "rq1", "rq2", "rq3", "hq0", "hq1", "hl"] + ["u%s%d" % (a, k) for a in "xq" for k in range(len(UPD))])
+COSTS = [(1.56, 3.8, 0.5, 150.0, 3000.0, 2200.0), (1.15, 2.2, 0.45, 110.0, 4500.0, 2800.0), (1.95, 5.4, 0.65, 210.0, 3600.0, 2500.0)]
 CFG = {
-    "cg": ["SSVSSSSS"] * RO,
-    "mp": [0, 96, 160, 256],
-    "vg": ["SSSS", "SSSS", "SSSS", "VSVV"],
-    "yg": "SVSVSVSV", "bonus": 1500.0, "tries": 9000, "seed": 2, "temp": 50.0,
+    "cg": ["S64 V64 S64 V64"] + ["F32 S64 S64 S48 F48"] * 3,
+    "cn": ["A64 M64 A64 M64"] + ["R32 M64 M64 M48 R48"] * 3,
+    "parts": "P32 P64 P64 P96", "clamp": 1, "split": 1, "per": 8,
+    "vg": ["S64 S64 S64 S64"] * 3 + ["V64 S64 V64 V64"],
+    "yg": "SVSVSVSV", "xa": "S", "free": "V", "redo": 1, "patch": [1, 2, 3], "reset": "G", "renew": "G",
+    "bonus": [0.0, 700.0, 1500.0, 3000.0], "lead": [0.0, 1000.0, 2000.0, 4000.0, 8000.0, 16000.0], "tries": 10000, "seed": 2, "temp": 50.0, "pull": 0.05, "turn": 100, "mg": 2,
 }
+FIRST = 96
+
+
+def spans(word):
+    out, a = [], 0
+    for w in word.split():
+        out.append((a, a + int(w[1:]), w[0]))
+        a = out[-1][1]
+    return out
+
+
 A = AluOpType
 AF = ActivationFunctionType
 
 
+def helpers(T, topo):
+    out = []
+    for c in T.cores:
+        out.append([x for x in topo.cores_of(c) if x not in T.cores and x not in out and topo.die(x) == topo.die(c)][0])
+    return out
+
+
 def build(g, T, topo, rank, cost):
-    ops = []
+    ops, phase = [], ["s"]
     V, S, P = g.vector, g.scalar, g.tensor
-    core = T.cores[rank]
+    core, helper = T.cores[rank], helpers(T, topo)[rank]
+    mate = [r for r in range(N) if r != rank and topo.die(T.cores[r]) == topo.die(core)][0]
     GA, SCA, PE = cost[:3]
 
-    def op(eng, fns, dur, R, Wr, banks=(), kind="c", sem=None, lsem=None, cnt=0, lat=0.0, bulk=False):
+    def op(eng, fns, dur, R, Wr, banks=(), kind="c", sem=None, lsem=None, cnt=0, mib=0.0, hint=0.0, bulk=False):
         ops.append(dict(e=eng, f=fns, d=float(dur), R=list(R), W=list(Wr), b=list(banks), k=kind, sem=sem, lsem=lsem,
-                        cnt=cnt, lat=lat, bulk=bulk))
+                        cnt=cnt, mib=mib, hint=hint, bulk=bulk, ph=phase[0]))
 
-    def ts(out, in0, s1, s2, o0, o1, n, R, Wr, banks=()):
+    def join(k):
+        last = ops[-k:]
+        del ops[-k:]
+        op(last[0]["e"], [f for o in last for f in o["f"]], sum(o["d"] for o in last), sorted({x for o in last for x in o["R"]}),
+           sorted({x for o in last for x in o["W"]}), last[0]["b"], bulk=last[0]["bulk"])
+
+    def ts(out, in0, s1, s2, o0, o1, n, R, Wr, banks=(), bulk=False):
         if o1 is None:
-            op("V", [lambda: V.tensor_scalar(out, in0, s1, None, o0)], max(64, n), R, Wr, banks)
+            op("V", [lambda: V.tensor_scalar(out, in0, s1, None, o0)], max(64, n), R, Wr, banks, bulk=bulk)
         else:
-            op("V", [lambda: V.tensor_scalar(out, in0, s1, s2, o0, o1)], max(64, n), R, Wr, banks)
+            op("V", [lambda: V.tensor_scalar(out, in0, s1, s2, o0, o1)], max(64, n), R, Wr, banks, bulk=bulk)
+
+    def fill(out, n, c, R, Wr):
+        ts(out, T.nrow[:, 0:n], 0.0, c, A.mult, A.add, n, ["nrow"] + R, Wr)
 
     def tt(out, a, b, o, n, R, Wr, banks=(), bulk=False):
         op("V", [lambda: V.tensor_tensor(out, a, b, o)], max(64, n), R, Wr, banks, bulk=bulk)
 
-    def cp(out, a, n, R, Wr, banks=()):
-        op("V", [lambda: V.tensor_copy(out, a)], max(64, n), R, Wr, banks)
+    def cp(out, a, n, R, Wr, banks=(), eng="V"):
+        if eng == "V":
+            op("V", [lambda: V.tensor_copy(out, a)], max(64, n), R, Wr, banks)
+        else:
+            ac(out, a, AF.Copy, n, R, Wr, banks, False)
 
-    def ac(out, a, fn, n, R, Wr, banks=()):
-        op("S", [lambda: S.activation(out, a, fn)], max(64, n), R, Wr, banks, bulk=True)
+    def ac(out, a, fn, n, R, Wr, banks=(), bulk=True):
+        op("S", [lambda: S.activation(out, a, fn)], max(64, n), R, Wr, banks, bulk=bulk)
 
     def gcp(out, a, n, R, Wr):
         op("G", [lambda: g.affine_select(out, a, [[0, n]], A.is_gt, 0.0, 1, 0)], 205 + 2 * n, R, Wr)
@@ -77,11 +110,11 @@ def build(g, T, topo, rank, cost):
             op("P", [(lambda m=m: P.matmul(m[0], m[1], m[2], m[3], m[4])) for m in part], sum(max(64, m[5]) for m in part) * PE + 15,
                R, Wr, banks, bulk=bulk)
 
-    def gat(eng, out, win, off, n, R, Wr):
-        if eng == "V":
-            op("V", [lambda: V.tensor_copy(out, win.indirect(off))], 60 + GA * n, R, Wr, bulk=n > 256)
-        else:
-            op("S", [lambda: S.activation(out, win.indirect(off), AF.Copy)], 80 + GA * n, R, Wr, bulk=n > 256)
+    def gat(eng, out, win, off, n, R, Wr, free=True):
+        both = {"V": ([lambda: V.tensor_copy(out, win.indirect(off))], 60 + GA * n), "S": ([lambda: S.activation(out, win.indirect(off), AF.Copy)], 80 + GA * n)}
+        op(eng, both[eng][0], both[eng][1], R, Wr, bulk=n > 256)
+        if free:
+            ops[-1]["alt"] = both
 
     def sca(win, off, a, n, R, Wr):
         op("V", [lambda: V.tensor_copy(win.indirect(off), a)], 60 + SCA * n, R, Wr)
@@ -92,343 +125,472 @@ def build(g, T, topo, rank, cost):
         else:
             op("G", [lambda: g.iota(out, pat, base, cm)], 160 + 2 * n, [], Wr)
 
-    def dma(eng, out, a, sem, R, Wr, lat):
-        q = g.sync if eng == "Y" else g.scalar
-        op(eng, [lambda: q.dma_start(out, a)], 100, R, Wr, kind="d", sem=sem, cnt=16, lat=lat)
+    def dma(out, a, sem, R, Wr, mib, hint=0.0):
+        op("Y", [lambda: g.sync.dma_start(out, a)], 100, R, Wr, kind="d", sem=[sem], cnt=16, mib=mib, hint=hint)
 
-    def send(dist, pairs, sem, lsem, R, Wr, lat):
-        dst = T.cores[(rank + dist) % N]
-        rid, pid, _ = topo.addr(dst)
-        eng = topo.engines(core, dst)
-        per = len(eng) // len(pairs)
-        masks = [sum(1 << e for e in eng[i * per:(i + 1) * per]) for i in range(len(pairs))]
-        if len(pairs) == 1:
-            fn = lambda: g.remote_dma(pairs[0][0], pairs[0][1], T.sem[sem], T.sem[lsem], pid, rid, masks[0])
+    def send(items, lsem, R, Wr, mib, hint=0.0, by="G"):
+        trs, per = [], 0
+        for i, (dist, out, a, sem) in enumerate(items):
+            dst = helper if dist is None else T.cores[(rank - dist) % N]
+            rid, pid, _ = topo.addr(dst)
+            eng = topo.engines(core if by == "G" else helper, dst)
+            per = len(eng) // (1 if len(items) == 1 else 2 if len(items) == 2 else 4)
+            mask = sum(1 << e for e in eng[i * per:(i + 1) * per])
+            trs.append((out, a, T.sem[sem], pid, rid, mask))
+        if len(items) == 1:
+            o, a, sm, pid, rid, mask = trs[0]
+            fn = lambda: g.remote_dma(o, a, sm, T.sem[lsem], pid, rid, mask)
         else:
-            fn = lambda: g.remote_dma_fused([RemoteDMATransfer(dst_ids=[DstId(rid=rid, pnc=pid)], dma_engine_mask=masks[i], remote_sem=T.sem[sem],
-                                                               src=pairs[i][1], dst=pairs[i][0]) for i in range(len(pairs))], local_sem=T.sem[lsem])
-        op("G", [fn], 600, R, Wr, kind="r", sem=sem, lsem=lsem, cnt=per * len(pairs), lat=lat)
+            fn = lambda: g.remote_dma_fused([RemoteDMATransfer(dst_ids=[DstId(rid=rid, pnc=pid)], dma_engine_mask=mask, remote_sem=sm, src=a, dst=o)
+                                             for o, a, sm, pid, rid, mask in trs], local_sem=T.sem[lsem])
+        op(by, [fn], 600, R, Wr, kind="r", sem=[x[3] for x in items], lsem=lsem, cnt=per, mib=mib, hint=hint)
 
     def nt(buf, t, w=L):
         return buf[:, t * w:(t + 1) * w]
 
-    def runs(word, unit):
-        out, i = [], 0
-        while i < len(word):
-            j = i + 2 if (unit == 32 and i + 1 < len(word) and word[i + 1] == word[i]) else i + 1
-            out.append((i * unit, j * unit, word[i]))
-            i = j
-        return out
-
-    mp = CFG["mp"]
-    parts = [(mp[n], mp[n + 1]) for n in range(len(mp) - 1)]
+    q = W // PIECES
+    AQ = ["aq%d" % p for p in range(PIECES)]
     aqw = T.aqs[:, 0:W]
-    dma("Y", T.xA[:], T.x[:], "ldx", [], ["xA"], 6500)
-    dma("S", T.aqs[:], T.aq[:], "ldq", [], ["aq"], 11000)
-    dma("Y", T.xB[:], T.x[:], "ldb", ["aq"], ["xB"], 6000)
-    dma("Y", T.tgs[:], T.tg[:], "ldt", ["aq"], ["tgs"], 7000)
+    for p in range(PIECES):
+        dma(T.aqs[:, p * q:(p + 1) * q], T.aq[:, p * q:(p + 1) * q], "ldq%d" % p, ["ld"], [AQ[p], "ld"], 2.0 / PIECES, 0 if p == 0 else 3000 + 6000 * p / PIECES)
+        if p == 0:
+            dma(T.xA[:], T.x[:], "ldx", ["ld"], ["xA", "ld"], 1.0, 6000 / PIECES)
+    dma(T.tgs[:], T.tg[:], "ldt", ["ld"], ["tgs", "ld"], 0.125, 9000)
 
     col = T.col
-    rc, pc, gc15, gc0, r128, kc, r1, c15, cu, cv, t0 = [col[:, i:i + 1] for i in range(11)]
+    rc, pc, gc15, gc0, r128, kc, r1, c15, cu, cv, t0, r4 = [col[:, i:i + 1] for i in range(12)]
     iota(T.pi[:], [[0, 2]], 0, 1, 2, ["pi"], False)
     iota(T.nrow[:], [[1, L]], 0, 0, L, ["nrow"])
-    iota(T.m16[:], [[0, 16], [1, 16]], 0, 0, L, ["m16"])
-    for a, b in parts:
-        iota(T.prow[:, a:b], [[128, 16], [16, (b - a) // 32], [2048, 2]], a // 2, 0, b - a, ["prow%d" % a])
-    iota(T.pf[:], [[1, 4], [16, 8], [2048, 2]], 0, 0, 64, ["pf"])
-    iota(T.g16[:], [[16, 8], [0, 16]], 0, 0, 128, ["g16"])
-    iota(T.vv[:], [[-16, 2], [0, 4], [1, 32]], 0, 0, L, ["vv"])
-    iota(T.vw[:], [[-16, 2], [1, 32]], 0, 0, 64, ["vw"])
-    iota(T.m64[:], [[0, 4], [1, 64]], 0, 0, L, ["m64"])
+    iota(T.ksc[:], [[0, 16], [1, 16]], 0, 0, L, ["ksc"])
+    ina, g16, vw, inw = T.ymc[:, 0:264], T.ymc[:, 272:400], T.ymc[:, 400:464], T.ymc[:, 464:532]
+    prow, psc, pf = T.vall[:, 0:L], T.vall[:, L:2 * L], T.vall[:, 2 * L:2 * L + 64]
+    iota(g16, [[16, 8], [0, 16]], 0, 0, 128, ["g16"])
+    iota(T.asc[:], [[-16, 2], [0, 4], [1, 32]], 0, 0, L, ["asc"])
+    iota(vw, [[-16, 2], [1, 32]], 0, 0, 64, ["vw"])
+    iota(T.vsc[:], [[0, 4], [1, 64]], 0, 0, L, ["vsc"])
+    parts = spans(CFG["parts"])
+    for a, b, kind in parts:
+        iota(prow[:, a:b], [[128, 16], [16, (b - a) // 32], [2048, 2]], a // 2, 0, b - a, ["prow%d" % a])
+    iota(pf, [[1, 4], [16, 8], [2048, 2]], 0, 0, 64, ["pf"])
     iota(T.idrow[:], [[16, 2], [128, 32]], 48, 0, 64, ["idrow"])
     iota(T.idf[:], [[16, 2], [2048, 2]], 48, 0, 4, ["idf"])
-    for h in range(4):
-        iota(T.stab[:, h * 1040:(h + 1) * 1040], [[1, 1040]], h * 1040, 0, 1040, ["stab%d" % h])
-    STAB0 = ["stab%d" % h for h in range(4)]
+    for h in range(8):
+        iota(nt(T.stab, h, WD // 8), [[1, WD // 8]], h * WD // 8, 0, WD // 8, ["stab%d" % h])
+    STAB0 = ["stab%d" % h for h in range(8)]
     ts(T.ri[:], T.pi[:], 15, None, A.bitwise_and, None, 2, ["pi"], ["ri"])
     cp(rc, T.ri[:, 0:1], 1, ["ri"], ["rc"])
     cp(pc, T.pi[:, 0:1], 1, ["pi"], ["pc"])
     tt(gc0, pc, rc, A.subtract, 1, ["pc", "rc"], ["gc0"])
     ts(gc15, gc0, 15.0, None, A.add, None, 1, ["gc0"], ["gc15"])
     ts(r128, rc, 128.0, None, A.mult, None, 1, ["rc"], ["r128"])
-    ts(T.prm[:], T.pf[:], r128, None, A.add, None, 64, ["pf", "r128"], ["prm"])
     ts(T.idcol[:], T.idf[:], r128, None, A.add, None, 4, ["idf", "r128"], ["idcol"])
     ts(kc, rc, 15.0, KF, A.is_lt, A.mult, 1, ["rc"], ["kc"])
-    ts(T.kct[:], T.nrow[:, 0:4], kc, None, A.add, None, 4, ["nrow", "kc"], ["kct"])
-    ts(T.kcm[:], T.nrow[:, 0:4], kc, None, A.subtract, None, 4, ["nrow", "kc"], ["kcm"])
-    ts(T.nrm[:], T.nrow[:, 0:4], rc, -1.0, A.is_equal, A.mult, 4, ["nrow", "rc"], ["nrm"])
+    ts(T.nrm[:, 0:4], T.nrow[:, 0:4], rc, None, A.is_equal, None, 4, ["nrow", "rc"], ["nrm"])
+    ts(T.nrm[:, 4:8], T.nrow[:, 0:4], rc, -1.0, A.is_equal, A.mult, 4, ["nrow", "rc"], ["nrn"])
     ts(r1, rc, 1.0, None, A.add, None, 1, ["rc"], ["r1"])
     ts(c15, rc, -1.0, 15.0, A.mult, A.add, 1, ["rc"], ["c15"])
     ts(t0, rc, 0.0, -16.0, A.is_equal, A.mult, 1, ["rc"], ["t0"])
     ts(cu, c15, 1.0, t0, A.add, A.add, 1, ["c15", "t0"], ["cu"])
     ts(cv, rc, 15.0, r1, A.is_lt, A.mult, 1, ["rc", "r1"], ["cv"])
+    ts(r4, rc, 4.0, W + 128.0, A.mult, A.add, 1, ["rc"], ["r4"])
+    ts(T.dum[:], T.nrow[:, 0:128:64], r4, None, A.add, None, 2, ["nrow", "r4"], ["dum"])
     for i, (c, key) in enumerate(((c15, "c15"), (cu, "cu"), (cv, "cv"))):
         ts(T.oh[:, 16 * i:16 * i + 16], T.nrow[:, 0:16], c, None, A.is_equal, None, 16, ["nrow", key], ["oh%d" % i])
     for buf, sc, key in ((T.z32, 32.0, "z32"), (T.zm16, -16.0, "zm16"), (T.z16, 16.0, "z16"), (T.zh, 1.0, "zh")):
         ts(buf[:], T.nrow[:, 0:144], gc15, sc, A.is_equal, A.mult, 144, ["nrow", "gc15"], [key])
     for buf, sc, key in ((T.eye, 1.0, "eye"), (T.neye, -1.0, "neye"), (T.hey, 0.5, "hey"), (T.nhey, -0.5, "nhey")):
         ts(buf[:], T.nrow[:, 0:128], pc, sc, A.is_equal, A.mult, 128, ["nrow", "pc"], [key])
-    ts(T.half[:], T.nrow[:], 0.0, 0.5, A.mult, A.add, L, ["nrow"], ["half"])
-    ts(T.bo[:], T.g16[:], gc0, KF, A.is_equal, A.mult, 128, ["g16", "gc0"], ["bo"])
-    ts(T.boh[:], T.g16[:], gc0, None, A.is_equal, None, 128, ["g16", "gc0"], ["boh"])
+    fill(T.half[:], L, 0.5, [], ["half"])
+    fill(T.c128[:], 144, 128.0, [], ["c128"])
+    ts(T.bo[:], g16, gc0, KF, A.is_equal, A.mult, 128, ["g16", "gc0"], ["bo"])
+    ts(T.boh[:], g16, gc0, None, A.is_equal, None, 128, ["g16", "gc0"], ["boh"])
+    ts(T.prm[:], pf, r128, None, A.add, None, 64, ["pf", "r128"], ["prm"])
+    ts(T.kcm[:], T.nrow[:, 0:4], kc, None, A.subtract, None, 4, ["nrow", "kc"], ["kcm"])
+    ts(T.nbo[:], g16, gc0, -KF, A.is_equal, A.mult, 128, ["g16", "gc0"], ["nbo"])
     for t in range(RO - 1):
-        ts(nt(T.bok, t, 144), T.zh[:], T.nrm[:, t:t + 1], -1.0, A.mult, A.mult, 72, ["zh", "nrm"], ["bok%d" % t])
-    ts(T.cmax[:], T.m16[:], 0.0, -1000000.0, A.is_equal, A.mult, L, ["m16"], ["cmax"])
+        ts(nt(T.bok, t, 144), T.zh[:], T.nrm[:, t:t + 1], None, A.mult, None, 72, ["zh", "nrm"], ["bok%d" % t])
+    ts(T.cmax[:], T.ksc[:], 0.0, -1000000.0, A.is_equal, A.mult, L, ["ksc"], ["cmax"])
     ts(T.cmax[:], T.cmax[:], 1.0, None, A.add, None, L, ["cmax"], ["cmax"])
+    ts(T.cfz[:], T.ksc[:], rc, -20000.0, A.is_equal, A.mult, L, ["ksc", "rc"], ["cfz"])
+    ts(T.cmin[:], T.ksc[:], r1, KF, A.is_equal, A.mult, L, ["ksc", "r1"], ["cmin"])
+    tt(T.cfz[:], T.cfz[:], T.cmin[:], A.add, 2 * L, ["cfz", "cmin"], ["cfz"])
     ts(T.cmin[:], T.cmax[:], -1.0, None, A.mult, None, L, ["cmax"], ["cmin"])
-    ts(T.cfz[:], T.m16[:], rc, -20000.0, A.is_equal, A.mult, L, ["m16", "rc"], ["cfz"])
-    ts(T.cf2[:], T.m16[:], r1, KF, A.is_equal, A.mult, L, ["m16", "r1"], ["cf2"])
-    tt(T.cfz[:], T.cfz[:], T.cf2[:], A.add, 2 * L, ["cfz", "cf2"], ["cfz"])
-    scan(T.psc[:], T.cfz[:], T.prow[:], A.add, A.max, L, ["cfz"] + ["prow%d" % a for a, b in parts], ["psc"])
-    for t in range(RO):
-        ts(nt(T.prr, t, 16), T.psc[:, 15:L:16], T.kcm[:, t:t + 1], None, A.add, None, 16, ["psc", "kcm"], ["prr%d" % t])
-    ts(T.rst[:], T.m64[:], 0.0, None, A.is_gt, None, L, ["m64"], ["rst"])
+    ts(T.rst[:], T.vsc[:], 0.0, None, A.is_gt, None, L, ["vsc"], ["rst"])
     ts(T.lanerow[:], T.nrow[:], 16.0, None, A.mult, None, L, ["nrow"], ["lanerow"])
-    ts(T.ndum[:], T.nrow[:, 0:64:16], rc, float(W), A.add, A.add, 4, ["nrow", "rc"], ["ndum"])
-    ts(T.ndum[:], T.ndum[:], -1.0, None, A.mult, None, 4, ["ndum"], ["ndum"])
     for c1 in range(2):
         a = 128 * c1 + 32
-        ts(T.vv[:, a:a + 32], T.vv[:, a:a + 32], -1.0, None, A.add, None, 32, ["vv"], ["vv"])
-    ts(T.act[:], T.vv[:], rc, None, A.is_lt, None, L, ["vv", "rc"], ["act"])
-    tt(T.cvoid[:, 1:L], T.act[:, 1:L], T.act[:, 0:L - 1], A.subtract, 2 * L, ["act"], ["cvoid"])
-    ts(T.cvoid[:, 0:L:128], T.act[:, 0:2], 0.0, 5.0, A.mult, A.add, 2, ["act", "cvoid"], ["cvoid"])
-    ts(T.actw[:], T.vw[:], rc, None, A.is_lt, None, 64, ["vw", "rc"], ["actw"])
-    tt(T.cwave[:, 1:64], T.actw[:, 1:64], T.actw[:, 0:63], A.subtract, 128, ["actw"], ["cwave"])
-    ts(T.cwave[:, 0:64:32], T.actw[:, 0:2], 0.0, 5.0, A.mult, A.add, 2, ["actw", "cwave"], ["cwave"])
+        ts(T.asc[:, a:a + 32], T.asc[:, a:a + 32], -1.0, None, A.add, None, 32, ["asc"], ["asc"])
+    for h in range(2):
+        fill(nt(ina, h, 132), 132, 0.0, [], ["ina"])
+        fill(nt(T.eqd, h, 132), 132, 0.0, [], ["eqd0", "eqd1", "eqd2", "eqd3"])
+        ts(ina[:, 132 * h + 2:132 * h + 130], nt(T.asc, h, 128), rc, KF, A.is_ge, A.mult, 128, ["asc", "rc"], ["ina"])
+    tt(T.cvoid[:, 1:264], ina[:, 1:264], ina[:, 0:263], A.subtract, 528, ["ina"], ["cvoid"])
+    fill(T.cvoid[:, 0:264:132], 2, -30000.0, ["cvoid"], ["cvoid"])
+    fill(T.cvoid[:, 131:264:132], 2, -128.0, ["cvoid"], ["cvoid"])
+    fill(inw, 68, 0.0, [], ["inw"])
+    fill(T.eqw[:], 136, 0.0, [], ["eqw0", "eqw1", "eqw2", "eqw3"])
+    for h in range(2):
+        ts(inw[:, 34 * h + 1:34 * h + 33], nt(vw, h, 32), rc, KF, A.is_ge, A.mult, 32, ["vw", "rc"], ["inw"])
+    tt(T.cwave[:, 1:68], inw[:, 1:68], inw[:, 0:67], A.subtract, 136, ["inw"], ["cwave"])
+    fill(T.cwave[:, 0:68:34], 2, -30000.0, ["cwave"], ["cwave"])
+    scan(psc, T.cfz[:], prow, A.add, A.max, L, ["cfz"] + ["prow%d" % a for a, b, kind in parts], ["psc"])
+    for t in range(1, RO):
+        ts(nt(T.prr, t, 16), psc[:, 15:L:16], T.kcm[:, t:t + 1], None, A.add, None, 16, ["psc", "kcm"], ["prr%d" % t])
+    TMP = ["ina", "g16", "vw", "inw", "psc", "pf"] + ["prow%d" % a for a, b, kind in parts]
 
     def Z(buf, r):
         return buf[:, 15 - r:143 - r]
 
-    send(-1, [(T.rep1[:], T.xA[:])], "rr1", "lr1", ["xA", "aq"], ["rep1"], 7000)
+    lo, hi = nt(T.aqs, 0, W // 2), nt(T.aqs, 1, W // 2)
+    send([(None, lo, lo, "hq0")], "lq1", AQ[:-1] + ["rs"], ["hq0", "rs"], 1.0)
+    send([(1, T.rep1[:], T.xA[:], "rx1")], "lx1", ["xA", "rs"], ["rep1", "rs"], 1.0, 2400)
+    send([(1, nt(T.aqr1, 1, W // 2), hi, "rq1")], "lq1", AQ + ["rs"], ["aqr1b", "rs"], 1.0, 4800)
+    send([(None, hi, hi, "hq1")], "lq1", AQ + ["rs"], ["hq1", "rs"], 1.0, 7200)
+    send([(1, nt(T.aqr1, 0, W // 2), lo, "rq0")], "hl", ["hq0", "hs"], ["aqr1", "hs"], 1.0, by="H")
+    send([(2, T.aqr2[:], T.aqs[:], "rq2")], "hl", ["hq0", "hq1", "hs"], ["aqr2", "hs"], 2.0, 3000, by="H")
+    send([(1, T.rep2[:], T.rep1[:], "rx2")], "lx2", ["rep1", "rs"], ["rep2", "rs"], 1.0, 3000)
     for t in range(RO):
-        gat("V", nt(T.ownu, t), aqw, nt(T.prr, t, 16), L, ["aq", "prr%d" % t], ["ownu%d" % t])
-        ts(nt(T.ownh, t), aqw.indirect(nt(T.prm, t, 16)), -2048.0, None, A.add, None, 60 + GA * L, ["aq", "prm"], ["ownh%d" % t])
         if t == 0:
+            for p in range(PIECES):
+                cp(T.ownu[:, p * q // 16:(p + 1) * q // 16], T.aqs[:, p * q:(p + 1) * q:16], q // 16, [AQ[p]], ["ownu0_%d" % p])
             cp(nt(T.xvc, t), T.xA[:, t:W:16], 128, ["xA"], ["xvc%d" % t])
         else:
+            gat("V", nt(T.ownu, t), aqw, nt(T.prr, t, 16), L, AQ + ["prr%d" % t], ["ownu%d_%d" % (t, p) for p in range(PIECES)], False)
             gcp(nt(T.xvc, t), T.xA[:, t:W:16], L, ["xA"], ["xvc%d" % t])
-        ts(nt(T.nown, t), T.aqs[:, t:W:16], -2048.0, T.nrm[:, t:t + 1], A.add, A.mult, L, ["aq", "nrm"], ["nown%d" % t])
-        send(1 + t % 3, [(nt(T.xvin, t), nt(T.xvc, t)), (nt(T.nownin, t), nt(T.nown, t))], "rx%d" % t, "lsm",
-             ["xvc%d" % t, "nown%d" % t], ["xvin%d" % t, "nownin%d" % t], 3000)
+            gat("S", nt(T.xvq, t), T.xA[:, 0:W], nt(T.prr, t, 16), L, ["xA", "prr%d" % t], ["xvq%d" % t])
+        ts(nt(T.ownh, t), aqw.indirect(nt(T.prm, t, 16)), -2048.0, None, A.add, None, 60 + GA * L, AQ + ["prm"], ["ownh%d" % t])
+        ts(nt(T.nown, t), T.aqs[:, t:W:16], -2048.0, T.nrm[:, 4 + t:5 + t], A.add, A.mult, L, AQ + ["nrn"], ["nown%d" % t])
     cp(T.tgu[:], T.tgs[:], L, ["tgs"], ["tgu"])
 
-    def wave_offsets(t, w, zrow, zkey):
-        h = w - 1
-        st = T.st1[:, 32 * h:32 * h + 32]
-        scan(st, T.cfz[:, 0:32], zrow, A.add, A.max, 32, ["cfz", zkey], ["st1%d" % h])
-        for c1 in range(2):
-            o = 64 * h + 32 * c1
-            ts(T.new[:, o:o + 32], zrow, kc, T.st1[:, 32 * h + 16 * c1 + 15:32 * h + 16 * c1 + 16], A.add, A.not_equal, 32,
-               [zkey, "st1%d" % h, "kc"], ["new%d" % o])
-        ts(T.zcol[:, 2 * h:2 * h + 2], T.st1[:, 32 * h + 15:32 * h + 32:16], kc, None, A.subtract, None, 2, ["st1%d" % h, "kc"], ["zcol%d" % h])
-        scan(nt(T.wsc, h, 64), T.cwave[:], nt(T.new, h, 64), A.add, A.min, 32, ["cwave", "new%d" % (64 * h), "new%d" % (64 * h + 32)], ["wsc%d" % h])
-        for c1 in range(2):
-            o = 4 * t + 2 * h + c1
-            e = 64 * h + 32 * c1 + 31
-            ts(T.woff[:, o:o + 1], T.wsc[:, e:e + 1], T.ndum[:, c1:c1 + 1], T.zcol[:, 2 * h + c1:2 * h + c1 + 1],
-               A.mult, A.max, 1, ["wsc%d" % h, "ndum", "zcol%d" % h], ["woff%d" % o])
+    REP, YK, room = {}, {}, 0
+    for t in range(1, RO):
+        for a, b, e in spans(CFG["cg"][t]):
+            if e == "F":
+                REP[t, a] = T.yy[:, room:room + 16 * (b - a)]
+                ts(T.repl[:, room // 16:room // 16 + b - a], prow[:, a:b], float(t), None, A.add, None, b - a,
+                   ["prow%d" % x for x, y, z in parts], ["repl%d" % room])
+                gat("S", REP[t, a], T.xA[:, 0:W], T.repl[:, room // 16:room // 16 + b - a], 16 * (b - a), ["xA", "repl%d" % room], ["rep%d_%d" % (t, a)])
+                YK[t, a] = ["yy%d" % x for x in range(room // 512, (room + 16 * (b - a) - 1) // 512 + 1)]
+                room += 16 * (b - a)
+
+    def gathers(tag, raw, win, wkey, lst, lkeys, who, t=0):
+        for a, b, e in who:
+            wr = ["%sraw%d" % (tag, u) for u in range(a // 16, b // 16)]
+            if e == "F":
+                tt(raw[:, 16 * a:16 * b], win.indirect(lst[:, a:b]), REP[t, a], A.subtract, 60 + GA * 16 * (b - a),
+                   [wkey, "rep%d_%d" % (t, a)] + YK[t, a] + lkeys(a, b), wr, [], True)
+            else:
+                gat(e, raw[:, 16 * a:16 * b], win, lst[:, a:b], 16 * (b - a), [wkey] + lkeys(a, b), wr)
+
+    def scores(tag, raw, non, a, b, kind, xv, xkey, blocks, key, kb, first, last, diff, skip=-1):
+        rk = ["%sraw%d" % (tag, u) for u in range(a // 16, b // 16)]
+        nk = ["%snon%d_%d" % (tag, u, k) for k in range(16) for u in range(a // 16, b // 16)]
+        m = len(nk) // 16
+        if kind in "MR":
+            mm([(o, Z(T.zm16, r), raw[:, 16 * i:16 * j], first and x == 0, False, n) for x, (r, o, i, j, st, n) in enumerate(blocks)],
+               rk + ["zm16"], [key], [kb], CFG["per"], True)
+        if kind == "R":
+            ts(non[:, a:b, :], raw[:, 16 * a:16 * b], 0.0, None, A.max, None, 8 * (b - a), rk, nk, [], True)
+        elif kind == "M":
+            for k in range(16):
+                tt(non[:, a:b, k], raw[:, 16 * a + k:16 * b:16], T.B0[:, a:b], A.max, b - a, rk + ["B0lo"], nk[m * k:m * k + m], ["B0"], True)
+                if k % CFG["mg"] == CFG["mg"] - 1:
+                    join(CFG["mg"])
+        else:
+            for kh in range(2):
+                bn = diff[kh]
+                k0 = 8 * kh + (1 if skip == 8 * kh else 0)
+                nn = 8 * kh + 8 - k0
+                w = nn * (b - a)
+                lst = []
+                for k in range(nn):
+                    o = T[bn][:, k:w:nn]
+                    lst += [(o, T.eye[:], raw[:, 16 * a + k0 + k:16 * b:16], k == 0, False, b - a), (o, T.neye[:], xv[:, a:b], False, k == nn - 1, b - a)]
+                mm(lst, rk + ["eye", "neye", xkey], [bn], [bn], CFG["per"], True)
+                ac(non[:, a:b, k0:k0 + nn], T[bn][:, 0:w], AF.Abs, w, [bn], nk[8 * m * kh:8 * m * kh + 8 * m], [bn])
+        z = T.z16 if kind == "A" else T.z32
+        mm([(o, Z(z, r), non[:, i:j:st, :], first and kind == "A" and x == 0, last and x == len(blocks) - 1, n) for x, (r, o, i, j, st, n) in enumerate(blocks)],
+           nk + ["z32", "z16"], [key], [kb], CFG["per"], True)
 
     def redirect(win, key, t, w, more=()):
         o = 4 * t + 2 * (w - 1)
-        sca(win, T.woff[:, o:o + 2], T.urow[:, 128 * t + 32 * (w - 1):128 * t + 32 * w], 32,
-            ["woff%d" % o, "woff%d" % (o + 1), "urow%d" % t] + list(more), [key])
+        sca(win, T.woff[:, o:o + 2], T.urow[:, 64 * t + 32 * (w - 1):64 * t + 32 * w], 32,
+            ["woff%d" % o, "woff%d" % (o + 1), "urow%d" % t], [key] + list(more))
 
     def night(t):
         s = str(t)
-        lst = []
-        for a, b in parts:
-            nc = (b - a) // 16
-            for c in range(a // 16, b // 16):
-                o = t * L + 128 * (c % 2) + c // 2
-                lst.append((T.B0[:, a + c - a // 16:b:nc], T.eye[:], T.xvc[:, o:o + 121:8], True, True, 16))
-        mm(lst, ["eye", "xvc" + s], ["xvP"], ["B0"])
-        for a, b, e in runs(CFG["cg"][t], 32):
-            gat(e, T.near[:, 16 * a:16 * b], T.xA[:, 0:W], T.ownu[:, t * L + a:t * L + b], 16 * (b - a), ["xA", "ownu" + s],
-                ["near%d" % u for u in range(a // 32, b // 32)])
-        for n, (a, b) in enumerate(parts):
-            nk = ["near%d" % u for u in range(a // 32, b // 32)]
-            w = b - a
-            for k in range(16):
-                tt(T.mc[:, 16 * a + k:16 * b:16], T.near[:, 16 * a + k:16 * b:16], T.B0[:, a:b], A.max, w, nk + ["xvP"], ["mc%d_%d" % (n, k)], ["B0"], True)
-            kb, kk, out = ("B4", "cnt3", T.B4[:, L:L + b]) if a == 0 else ("B2", "key", T.B2[:, a:b])
-            mm([(out, Z(T.zm16, r), T.near[:, 16 * a + w * r:16 * a + w * (r + 1)], r == 0, False, w) for r in range(16)], nk + ["zm16"], [kk], [kb])
-            mm([(out, Z(T.z32, r), T.mc[:, 16 * a + w * r:16 * a + w * (r + 1)], False, r == 15, w) for r in range(16)],
-               ["mc%d_%d" % (n, k) for k in range(16)] + ["z32"], [kk], [kb])
-            if b not in (96, L):
-                continue
-            a = 0 if b == 96 else 96
-            ca, cb, h = a // 16, b // 16, "A" if a == 0 else "B"
-            scan(T.ksc[:, a:b], T.cmax[:, a:b], out if a == 0 else T.B2[:, a:b], A.add, A.max, b - a, ["cmax", kk], ["ksc" + h], [kb])
-            cp(T.ki[:, ca:cb], T.ksc[:, a + 15:b:16], 1, ["ksc" + h], ["ki" + h])
-            ts(T.kj[:, ca:cb], T.ki[:, ca:cb], 15, None, A.bitwise_and, None, 1, ["ki" + h], ["kj" + h])
-            cp(T.ku[:, ca:cb], T.kj[:, ca:cb], 1, ["kj" + h], ["ku" + h])
-            for u in ((1, 0) if a == 0 else (1,)):
-                tt(T.sel[:, u, a:b], T.oh[:, 16 - 16 * u:32 - 16 * u].indirect(T.ku[:, ca:cb]), T.ownh[:, t * L + a:t * L + b], A.mult,
-                   60 + GA * (b - a), ["ku" + h, "oh%d" % (1 - u), "ownh" + s], ["sel%s%d" % (h, u)])
-            if a == 0:
-                mm([(T.B4[:, 0:12], Z(T.zh, r), T.sel[:, :, r:96:16], r == 0, r == 15, 12) for r in range(16)]
-                   + [(T.B4[:, 16:80], T.boh[:], T.sel[:, :, 0:32], True, True, 64), (T.B4[:, 80:112], T.boh[:], T.sel[:, 0, 0:32], True, True, 32)],
-                   ["selA0", "selA1", "zh", "boh"], ["lstP"], ["B4"], 18)
-                for c1 in range(2):
-                    for po in range(2):
-                        o = 128 * c1 + 64 * po
-                        ts(T.nev[:, o:o + 64], T.B4[:, 16:80], T.B4[:, 6 * po + c1:6 * po + c1 + 1], None, A.not_equal, None, 64,
-                           ["lstP"], ["nev%d" % o], ["B4"])
-                ts(T.lsta[:, 0:12], T.B4[:, 0:12], 2048.0, None, A.add, None, 12, ["lstP"], ["lsta"], ["B4"])
-                ts(T.rowpo[:], T.B4[:, 16:112], 2048.0, None, A.add, None, 96, ["lstP"], ["rowpo"], ["B4"])
-                ts(nt(T.ulist, t, 8), T.B4[:, 2:10], 2048.0, None, A.add, None, 8, ["lstP"], ["ulist" + s], ["B4"])
-                scan(T.nsc[:], T.cvoid[:], T.nev[:], A.add, A.min, 128, ["cvoid", "nev0", "nev64", "nev128", "nev192"], ["nsc"])
-                for po in range(2):
-                    for c1 in range(2):
-                        e = 2 * po + c1
-                        ts(T.soff[:, 4 * t + e:4 * t + e + 1], T.nsc[:, 128 * c1 + 127:128 * c1 + 128], T.ndum[:, e:e + 1],
-                           T.lsta[:, 6 * po + c1:6 * po + c1 + 1], A.mult, A.max, 1, ["nsc", "ndum", "lsta"], ["soff%d_%d" % (t, e)])
-                so = ["soff%d_%d" % (t, e) for e in range(4)]
-                sca(T.stab[:, 0:WD], nt(T.soff, t, 4), T.rowpo[:, 32:96], 64, so + ["rowpo"] + STAB0, ["stab"])
-                gat("V", nt(T.urow, t, 128), T.stab[:, 0:WD], nt(T.ulist, t, 8), 128, ["stab", "ulist" + s], ["urow" + s])
-                wave_offsets(t, 1, T.urow[:, 128 * t + 96:128 * t + 128], "urow" + s)
+        xv = nt(T.xvc, t)
+        B0, B1, B2 = T.B0, T.B1, T.B2
+        xq, qk = (xv, "xvc0") if t == 0 else (nt(T.xvq, t), "xvq" + s)
+        how = spans(CFG["cn"][t])
+        mm([(B0[:, 0:L], T.eye[:], xq, True, True, L)], ["eye", qk], ["B0lo"], ["B0"])
+        DR = 32 if CFG["split"] and t > 0 else FIRST
+        bank = lambda b: "B2" if t == 0 or b > FIRST else "B1" if b <= DR else "B3"
+        gathers("c", T.near, T.xA[:, 0:W], "xA", nt(T.ownu, t), lambda a, b: ["ownu%d_%d" % (t, p) for p in range(a * PIECES // L, (b - 1) * PIECES // L + 1)],
+                spans(CFG["cg"][t]), t)
+
+        def part(a, b, kind):
+            if t == 0:
+                blocks = [((i // 8) % 16, B2[:, i // 128 * 128:i // 128 * 128 + 128], i, i + 8, 1, 128) for i in range(a, b, 8)]
             else:
-                mm([(T.B0[:, L:L + 16], Z(T.zh, r), T.sel[:, 1, 32 * (r % 8) + r // 8:32 * (r % 8) + 32:2], r == 0, r == 15, 16) for r in range(16)],
-                   ["selA1", "selB1", "zh"], ["lstT"], ["B0"], 16)
-                ts(T.tlist[:], T.B0[:, L:L + 16], 2048.0, None, A.add, None, 16, ["lstT"], ["tlist"], ["B0"])
-                gat("V", T.tw[:, t:W:16], T.stab[:, 0:WD], T.tlist[:], L, ["stab", "tlist"], ["tw"])
-        if t < RO - 1:
-            sca(T.stab[:, 0:WD], nt(T.soff, t, 4), T.rowpo[:, 0:64], 64, ["soff%d_%d" % (t, e) for e in range(4)] + ["rowpo"], ["stab"])
+                x, y = [(x, y) for x, y, z in parts if x <= a < y][0]
+                nc = (y - x) // 16
+                blocks = [(r, T[bank(b)][:, x:y], x + r * nc, x + (r + 1) * nc, 1, y - x) for r in range((a - x) // nc, (b - x) // nc)]
+            scores("c", T.near, T.mc, a, b, kind, xq, qk, blocks, bank(b) + "lo", bank(b), a == 0 or (t > 0 and a in (DR, FIRST)),
+                   b == L or (t > 0 and b in (DR, FIRST)), ("B3", "B3"))
+
+        def best(a, b, kb, h):
+            ca, cb = a // 16, b // 16
+            scan(T.ksc[:, a:b], T.cmax[:, a:b], T[kb][:, a:b], A.add, A.max, b - a, ["cmax", kb + "lo", "ksc"], ["ksc" + x for x in h], [kb])
+            cp(T.ki[:, ca:cb], T.ksc[:, a + 15:b:16], 16, ["ksc" + x for x in h], ["ki" + x for x in h])
+            ts(T.kj[:, ca:cb], T.ki[:, ca:cb], 15, None, A.bitwise_and, None, 16, ["ki" + x for x in h], ["kj" + x for x in h])
+            if t == 0:
+                for x in range(2):
+                    cp(T.ku[:, x:16:2], T.kj[:, 8 * x:8 * x + 8], 8, ["kjA"], [["kuA", "kuD"], ["kuB"]][x])
+            else:
+                cp(T.ku[:, ca:cb], T.kj[:, ca:cb], 16, ["kj" + h], ["ku" + h])
+
+        def pick(u, a, b, h):
+            tt(T.sel[:, u, a:b], T.oh[:, 16 - 16 * u:32 - 16 * u].indirect(T.ku[:, a // 16:b // 16]), T.ownh[:, t * L + a:t * L + b], A.mult,
+               60 + GA * (b - a), (["kuA", "kuB"] if t == 0 else ["ku" + h]) + ["oh%d" % (1 - u), "ownh" + s], ["sel%s%d" % (h, u)])
+        for a, b, kind in how:
+            if t == 0 or b <= FIRST:
+                part(a, b, kind)
+        if t == 0:
+            best(0, L, "B2", "DAB")
+        else:
+            best(0, DR, "B1", "D")
+            if DR < FIRST:
+                best(DR, FIRST, "B3", "A")
+        for a, b, h in ((0, DR, "D"), (DR, FIRST, "A")):
+            if a < b:
+                pick(1, a, b, h)
+                pick(0, a, b, h)
+        o = FIRST
+        rows = [(B1[:, o + 16:o + 80], T.boh[:], T.sel[:, :, 0:32], False, False, 64), (B1[:, o + 80:o + 112], T.boh[:], T.sel[:, 0, 0:32], False, DR < FIRST, 32)]
+        mm([(B1[:, o:o + 144], T.boh[:], T.c128[:], True, False, 144)], ["boh", "c128"], ["B1md"], ["B1"])
+        if DR < FIRST:
+            B3, wb, zo = T.B3, "B3", o + 16
+            lst = lambda u, c1, role: B1[:, o + 2 * u + c1:o + 2 * u + c1 + 1] if role == 0 else B3[:, o + 4 + c1:o + 5 + c1]
+            mm([(B1[:, o:o + 4], Z(T.zh, r), T.sel[:, :, r:32:16], False, False, 4) for r in range(16)] + rows, ["selD0", "selD1", "zh", "boh"], ["B1md"], ["B1"], 18)
+            mm([(B3[:, o:o + 48], T.boh[:], T.c128[:, 0:48], True, False, 48)], ["boh", "c128"], ["B3md"], ["B3"])
+            mm([(B3[:, o:o + 8], Z(T.zh, r), T.sel[:, :, 32 + r:FIRST:16], False, False, 8) for r in range(16)]
+               + [(B3[:, o + 16:o + 48], T.boh[:], T.sel[:, 1, 32:64], False, True, 32)], ["selA0", "selA1", "zh", "boh"], ["B3md"], ["B3"], 17)
+            ul, uz = [(0, 8, o)], (0, 4, 6)
+        else:
+            B3, wb, zo = B1, "B1", o + 112
+            lst = lambda u, c1, role: B1[:, o + 6 * u + 2 * role + c1:o + 6 * u + 2 * role + c1 + 1]
+            mm([(B1[:, o:o + 12], Z(T.zh, r), T.sel[:, :, r:FIRST:16], False, False, 12) for r in range(16)] + rows
+               + [(B1[:, zo:zo + 32], T.boh[:], T.sel[:, 1, 32:64], False, True, 32)], ["selD0", "selD1", "zh", "boh"], ["B1md"], ["B1"], 19)
+            ul, uz = [(0, 10, o + 2)], (0, 6, 8)
+        for c1 in range(2):
+            for po in range(2):
+                e = 132 * c1 + 2 + 64 * po
+                ts(T.eqd[:, e:e + 64], B1[:, o + 16:o + 80], lst(po, c1, 0), T.dum[:, c1:c1 + 1], A.is_equal, A.mult, 64,
+                   ["B1md", "dum"], ["eqd%d" % (2 * c1 + po)], ["B1"])
+        join(4)
+        scan(T.nsc[:], T.cvoid[:], T.eqd[:], A.add, A.max, 132, ["cvoid", "eqd0", "eqd1", "eqd2", "eqd3"], ["nsc"])
+        cp(T.rowpo[:], B1[:, o + 16:o + 112], 96, ["B1md"], ["rowpo"], ["B1"])
+        for po in range(2):
+            for c1 in range(2):
+                e = 2 * po + c1
+                ts(T.soff[:, 4 * t + e:4 * t + e + 1], T.nsc[:, 132 * c1 + 130 + po:132 * c1 + 131 + po], lst(po, c1, 0), None, A.max, None, 1,
+                   ["nsc", "B1md"], ["soff%d_%d" % (t, e)], ["B1"])
+        join(4)
+        so = ["soff%d_%d" % (t, e) for e in range(4)]
+        cp(T.ulist[:, 10 * t:10 * t + ul[0][1]], B3[:, ul[0][2]:ul[0][2] + ul[0][1]], 10, [wb + "md"], ["ulist" + s], [wb])
+        for c1 in range(2):
+            ts(T.eqw[:, 34 * c1 + 1:34 * c1 + 33], B3[:, zo:zo + 32], lst(1, c1, 1), T.dum[:, c1:c1 + 1], A.is_equal, A.mult, 32,
+               [wb + "md", "dum"], ["eqw%d" % c1], [wb])
+        join(2)
+        scan(T.wsc[:, 0:68], T.cwave[:], T.eqw[:, 0:68], A.add, A.max, 68, ["cwave", "eqw0", "eqw1"], ["wsc0"])
+        sca(T.stab[:, 0:WD], nt(T.soff, t, 4), T.rowpo[:, 32:96], 64, so + ["rowpo"] + STAB0, ["stab"])
+        st = T.stab[:, 0:W]
+        gat("V", T.zr1[:], st, T.ulist[:, 10 * t + uz[1]:10 * t + uz[1] + 2], 32, ["stab", "ulist" + s], ["zr1"])
+        gat("V", nt(T.urow, t, 64), st, T.ulist[:, 10 * t:10 * t + 4], 64, ["stab", "ulist" + s], ["urow" + s])
+        scan(T.st1[:, 0:32], T.cfz[:, 0:32], T.zr1[:], A.add, A.max, 32, ["cfz", "zr1"], ["st10"])
+        for c1 in range(2):
+            ts(T.woff[:, 4 * t + c1:4 * t + c1 + 1], T.st1[:, 16 * c1 + 15:16 * c1 + 16], kc, T.wsc[:, 34 * c1 + 33:34 * c1 + 34], A.subtract, A.max, 1,
+               ["st10", "kc", "wsc0"], ["woff%d" % (4 * t + c1)])
+        join(2)
+        redo = CFG["redo"] and t > 0
+
+        def rest():
+            if t > 0:
+                for a, b, kind in how:
+                    if b > FIRST:
+                        part(a, b, kind)
+                best(FIRST, L, "B2", "B")
+            pick(1, FIRST, L, "B")
+            mm([(B0[:, L:L + 16], T.boh[:], T.c128[:, 0:16], True, False, 16)]
+               + [(B0[:, L:L + 16], Z(T.zh, r), T.sel[:, 1, 32 * (r % 8) + r // 8:32 * (r % 8) + 32:2], False, r == 15, 16) for r in range(16)],
+               ["selD1", "selA1", "selB1", "zh", "boh", "c128"], ["B0hi"], ["B0"], 17)
+            cp(T.tlist[:], B0[:, L:L + 16], 16, ["B0hi"], ["tlist"], ["B0"])
+            gat("V", T.tw[:, t:W:16], st, T.tlist[:], L, ["stab", "tlist"], ["tw"])
+            if t < RO - 1 and CFG["reset"] == "G":
+                for h in range(8):
+                    iota(nt(T.stab, h, 512), [[1, 512]], 512 * h, 0, 512, ["stab"])
+            elif t < RO - 1:
+                sca(T.stab[:, 0:WD], nt(T.soff, t, 4), T.rowpo[:, 0:64], 64, so + ["rowpo"], ["stab"])
+        if redo:
+            gat("V", T.tw[:, 32 + t:W:128], st, T.ulist[:, 10 * t + uz[2]:10 * t + uz[2] + 2], 32, ["stab", "ulist" + s], ["tw"])
+        else:
+            rest()
         redirect(T.tw[:, 0:WD], "tw", t, 1)
-        wave_offsets(t, 2, T.tw[:, 32 + t:W:128], "tw")
+        zrow = T.tw[:, 32 + t:W:128]
+        scan(T.st1[:, 32:64], T.cfz[:, 0:32], zrow, A.add, A.max, 32, ["cfz", "tw"], ["st11"])
+        for c1 in range(2):
+            ts(T.eqw[:, 68 + 34 * c1 + 1:68 + 34 * c1 + 33], zrow, kc, T.st1[:, 47 + 16 * c1:48 + 16 * c1], A.add, A.is_equal, 32,
+               ["tw", "st11", "kc"], ["eqw%d" % (2 + c1)])
+        join(2)
+        ts(T.zcol[:], T.st1[:, 47:64:16], kc, None, A.subtract, None, 2, ["st11", "kc"], ["zcol"])
+        scan(T.wsc[:, 68:136], T.cwave[:], T.eqw[:, 68:136], A.add, A.max, 68, ["cwave", "eqw2", "eqw3"], ["wsc1"])
+        for c1 in range(2):
+            ts(T.woff[:, 4 * t + 2 + c1:4 * t + 3 + c1], T.wsc[:, 101 + 34 * c1:102 + 34 * c1], T.dum[:, c1:c1 + 1], T.zcol[:, c1:c1 + 1],
+               A.mult, A.max, 1, ["wsc1", "dum", "zcol"], ["woff%d" % (4 * t + 2 + c1)])
+        join(2)
+        if redo:
+            rest()
+            redirect(T.tw[:, 0:WD], "tw", t, 1)
         redirect(T.tw[:, 0:WD], "tw", t, 2)
-        kt = T.kct[:, t:t + 1]
-        for o in range(2):
-            scan(T.bsc[:, 32 * o:32 * o + 32], T.cfz[:, 0:32], T.tw[:, 16 * (3 + o) + t:W:128], A.add, A.max, 32, ["cfz", "tw"], ["bsc%d" % o])
-        for c in range(4):
-            ts(T.at1[:, 64 * c:64 * c + 64], T.idrow[:], kt, T.bsc[:, 16 * c + 15:16 * c + 16], A.add, A.is_equal, 64,
-               ["idrow", "kct", "bsc%d" % (c // 2)], ["at1%d" % c])
-        for o in range(2):
-            ts(T.ub[:, 32 * o:32 * o + 32], T.tw[:, 16 * (3 + o) + t:W:128], float(-t), None, A.add, None, 32, ["tw"], ["ub%d" % o])
-        ts(T.ucol[:], T.bsc[:, 15:64:16], kt, None, A.subtract, None, 4, ["bsc0", "bsc1", "kct"], ["ucol"])
-        for c in range(4):
-            mm([(T.B4[:, 128:192], T.bo[:], T.at1[:, 64 * c:64 * c + 64], c == 0, c == 3, 64)], ["bo", "at1%d" % c], ["cnt1"], ["B4"])
         scan(T.asc[:], T.cfz[:], T.tw[:, t:W:16], A.add, A.max, L, ["cfz", "tw"], ["asc"])
         ts(nt(T.alist, t, 16), T.asc[:, 15:L:16], kc, None, A.subtract, None, 16, ["asc", "kc"], ["alist" + s])
-        send(1 + t % 3, [(nt(T.alin, t, 16), nt(T.alist, t, 16))], "ra" + s, "lsm", ["alist" + s], ["alin" + s], 2500)
-        if t == 0:
-            send(-2, [(T.rep2[:], T.xB[:])], "rr2", "lr2", ["xB", "alist0"], ["rep2"], 7000)
-        tt(T.tm[:], T.ub[:], T.B4[:, 128:192], A.add, 64, ["ub0", "ub1", "cnt1"], ["tm"], ["B4"])
+        for h in range(2):
+            ts(nt(T.ub, h, 32), T.tw[:, 16 * (3 + h) + t:W:128], float(-t), None, A.add, None, 32, ["tw"], ["ub%d" % h])
+        join(2)
+        scan(T.bsc[:], T.cfz[:, 0:64], T.ub[:], A.add, A.max, 64, ["cfz", "ub0", "ub1"], ["bsc"])
         for c in range(4):
-            ts(T.a2[:, 64 * c:64 * c + 64], T.tm[:], T.idcol[:, c:c + 1], None, A.is_equal, None, 64, ["tm", "idcol"], ["a2%d" % c])
+            ts(nt(T.at1, c, 64), T.idrow[:], kc, T.bsc[:, 16 * c + 15:16 * c + 16], A.add, A.is_equal, 64, ["idrow", "kc", "bsc"], ["at1%d" % c])
+        join(4)
+        ts(T.ucol[:], T.bsc[:, 15:64:16], kc, None, A.subtract, None, 4, ["bsc", "kc"], ["ucol"])
+        mm([(B1[:, 0:64], T.bo[:], nt(T.at1, c, 64), c == 0, c == 3, 64) for c in range(4)], ["bo", "at10"], ["B1lo"], ["B1"])
+        tt(T.tm[:], T.ub[:], B1[:, 0:64], A.add, 64, ["ub0", "ub1", "B1lo"], ["tm"], ["B1"])
+        for c in range(4):
+            ts(nt(T.a2, c, 64), T.tm[:], T.idcol[:, c:c + 1], None, A.is_equal, None, 64, ["tm", "idcol"], ["a2%d" % c])
+        join(4)
         scan(T.b2[:], T.rst[:], T.a2[:], A.mult, A.max, L, ["rst"] + ["a2%d" % c for c in range(4)], ["b2"])
+        d = 1 + t % 3
+        gat(CFG["xa"], T.xa[:], T["rep%d" % d][:, 0:W], nt(T.alist, t, 16), L, ["rep%d" % d, "alist" + s], ["xa"])
+        free, fk = nt(T.free, t), "free" + s
+        new, nk = (T.xA[:, t:W:16], "xA") if t < RO - 1 else (nt(T.nxc, t), "nxc" + s)
+        clamp = CFG["clamp"]
+        if clamp:
+            mm([(B2[:, 0:L], T.hey[:], xv, True, False, L), (B2[:, 0:L], T.nhey[:], T.half[:], False, False, L)], ["hey", "nhey", "half", "xvc" + s], ["B2lo"], ["B2"])
+            mm([(B2[:, 0:L], T.hey[:], T.xa[:], False, True, L)], ["hey", "xa"], ["B2lo"], ["B2"])
+            ts(T.mh[:], B2[:, 0:L], MAGIC, -MAGIC, A.add, A.add, L, ["B2lo"], ["mh"], ["B2"])
+            mm([(B1[:, L:2 * L], T.eye[:], T.mh[:], True, False, L)], ["eye", "mh"], ["B1hi"], ["B1"])
+            mm([(B0[:, 0:L], T.eye[:], T.mh[:], True, False, L)], ["eye", "mh"], ["B0lo"], ["B0"])
+        else:
+            mm([(B0[:, 0:L], T.eye[:], xv, True, False, L), (B0[:, 0:L], T.nhey[:], T.half[:], False, False, L)], ["eye", "nhey", "half", "xvc" + s], ["B0lo"], ["B0"])
+            mm([(B2[:, 0:L], T.nhey[:], xv, True, False, L)], ["nhey", "xvc" + s], ["B2lo"], ["B2"])
+            mm([(B2[:, 0:L], T.hey[:], T.xa[:], False, True, L)], ["hey", "xa"], ["B2lo"], ["B2"])
         for c in range(4):
             ts(nt(T.at3, c), T.lanerow[:], T.ucol[:, c:c + 1], T.b2[:, 64 * c + 63:64 * c + 64], A.is_equal, A.is_gt, 128,
                ["lanerow", "ucol", "b2"], ["at3%d" % c])
-            mm([(T.B4[:, L:2 * L], T.bo[:], nt(T.at3, c), c == 0, c == 3, L)], ["bo", "at3%d" % c], ["cnt3"], ["B4"])
-        free = nt(T.B5, t % 2)
-        fk = "free%d" % (t % 2)
-        ts(free, T.B4[:, L:2 * L], 0.0, None, A.is_equal, None, L, ["cnt3"], [fk], ["B4", "B5"])
-        d = 1 + t % 3
-        gat("S", T.xa[:], T["rep%d" % d][:, 0:W], nt(T.alist, t, 16), L, ["rep%d" % d, "alist" + s], ["xa"])
-        o = T.B2[:, L:2 * L]
-        mm([(o, T.nhey[:], nt(T.xvc, t), True, False, L), (o, T.nhey[:], T.half[:], False, False, L)], ["nhey", "half", "xvc" + s], ["dx"], ["B2"])
-        mm([(o, T.hey[:], T.xa[:], False, True, L)], ["hey", "xa"], ["dx"], ["B2"])
-        cp(T.hx[:], o, L, ["dx"], ["hx"], ["B2"])
-        tt(T.B4[:, L:2 * L], T.hx[:], free, A.mult, L, ["hx", fk], ["cnt3"], ["B4", "B5"])
-        if t < RO - 1:
-            tt(T.xA[:, t:W:16], nt(T.xvc, t), T.B4[:, L:2 * L], A.add, L, ["xvc" + s, "cnt3"], ["xA"], ["B4"])
-            gcp(nt(T.nxc, t), T.xA[:, t:W:16], L, ["xA"], ["nxc" + s])
+            mm([(B1[:, L:2 * L], T.bo[:], nt(T.at3, c), c == 0 and not clamp, c == 3, L)], ["bo", "at3%d" % c], ["B1hi"], ["B1"])
+            if clamp:
+                mm([(B0[:, 0:L], T.nbo[:], nt(T.at3, c), False, c == 3, L)], ["nbo", "at3%d" % c], ["B0lo"], ["B0"])
+        if clamp:
+            tt(T.xa[:], xv, B1[:, L:2 * L], A.min, L, ["B1hi", "xvc" + s], ["xa"], ["B1"])
+            tt(new, T.xa[:], B0[:, 0:L], A.max, L, ["B0lo", "xa"], [nk], ["B0"])
+            ts(free, B1[:, L:2 * L], KF / 2, None, A.is_lt, None, L, ["B1hi"], [fk], ["B1"])
         else:
-            tt(nt(T.nxc, t), nt(T.xvc, t), T.B4[:, L:2 * L], A.add, L, ["xvc" + s, "cnt3"], ["nxc" + s], ["B4"])
-        dma("Y", T.yx[:, t * L:(t + 1) * L], nt(T.nxc, t), "outs", ["nxc" + s], [], 2500)
-        for k, (tu, du) in enumerate(UPD):
-            if tu == t:
-                send(-du, [(nt(T.updin, k), nt(T.nxc, t))], "ru%d" % k, "lsm", ["nxc" + s], ["updin%d" % k], 2500)
-                gcp(T["rep%d" % du][:, t:W:16], nt(T.updin, k), L, ["updin%d" % k], ["rep%d" % du])
+            if CFG["free"] == "S":
+                op("S", [lambda: S.activation(free, B1[:, L:2 * L], AF.Relu, bias=1.0, scale=-1.0)], L, ["B1hi"], [fk], ["B1"])
+            else:
+                ts(free, B1[:, L:2 * L], 0.0, None, A.is_equal, None, L, ["B1hi"], [fk], ["B1"])
+            tt(T.mh[:], B2[:, 0:L], free, A.mult, L, ["B2lo", fk], ["mh"], ["B2"])
+            mm([(B0[:, 0:L], T.eye[:], T.mh[:], False, True, L)], ["eye", "mh"], ["B0lo"], ["B0"])
+            ts(new, B0[:, 0:L], MAGIC, -MAGIC, A.add, A.add, L, ["B0lo"], [nk], ["B0"])
+        if t < RO - 1:
+            gcp(nt(T.nxc, t), T.xA[:, t:W:16], L, ["xA"], ["nxc" + s])
+            ks = [k for k, (tu, du) in enumerate(UPD) if tu == t]
+            send([(UPD[k][1], nt(T.updin, k), nt(T.nxc, t), "ux%d" % k) for k in ks], "lsm", ["nxc" + s, "rs"], ["updin%d" % k for k in ks] + ["rs"], 0.3)
+        if t == 0:
+            own = (mate + 3) % N == rank
+            send([(rank - mate, T.rep3[:], (T.xA if own else T.rep2)[:], "rx3")], "lx3", ["xA", "rep2", "rs"], ["rep3", "rs"], 1.0)
+            send([(rank - mate, T.aqr3[:], (T.aqs if own else T.aqr2)[:], "rq3")], "lq3", AQ + ["aqr2", "rs"], ["aqr3", "rs"], 2.0, 3000)
+        dma(T.yx[:, t * L:(t + 1) * L], nt(T.nxc, t), "outs", ["nxc" + s], [], 0.1)
 
     def visit(t):
         s = str(t)
-        gat("V", T.alu[:], aqw, nt(T.alin, t, 16), L, ["aq", "alin" + s], ["alu"])
-        if t == 0:
+        d = 1 + t % 3
+        rep, rk, aqw, ak = T["rep%d" % d][:, 0:W], "rep%d" % d, T["aqr%d" % d][:, 0:W], "aqr%d" % d
+        xv, al = nt(T.xvc, t), nt(T.alist, t, 16)
+        if t > 0 and t not in CFG["patch"]:
+            renew(t - 1, [d])
+        gat("V", T.alu[:], aqw, al, L, [ak, "aqr1b", "alist" + s], ["alu"], False)
+        gathers("v", T.far, rep, rk, T.alu, lambda a, b: ["alu"], spans(CFG["vg"][t]))
+        for a in range(0, L, 64):
+            scores("v", T.far, T.mv, a, a + 64, "A", xv, "xvc" + s, [(r, T.B6[:, a:a + 64], a + r, a + 64, 16, 64) for r in range(16)],
+                   "B6lo", "B6", a == 0, a + 64 == L, ("B4", "B5"), 0 if t == 1 and t in CFG["patch"] else -1)
+        if t not in CFG["patch"]:
             ts(T.alh[:], T.alu[:], -2048.0, None, A.add, None, 128, ["alu"], ["alh"])
         else:
-            back(t - 1)
-            ts(T.alh[:], aqw.indirect(nt(T.alin, t, 16)), -2048.0, None, A.add, None, 60 + GA * L, ["aq", "alin" + s], ["alh"])
-        for a, b, e in runs(CFG["vg"][t], 64):
-            gat(e, T.far[:, 16 * a:16 * b], T.xB[:, 0:W], T.alu[:, a:b], 16 * (b - a), ["xB", "alu"], ["far%d" % (a // 64)])
-        for hf in range(2):
-            a, b = 128 * hf, 128 * hf + 128
-            fk = ["far%d" % (2 * hf), "far%d" % (2 * hf + 1)]
-            mk = ["mv%d_%d" % (hf, k) for k in range(16)]
-            xv = T.xvin[:, t * L + a:t * L + b]
-            for kq in range(4):
-                bn = "B%d" % (6 + kq % 2)
-                lst = []
-                ks = [kk for kk in range(4) if 4 * kq + kk != t - 1]
-                for kk in ks:
-                    o = nt(T[bn], kk, 128)
-                    lst += [(o, T.eye[:], T.far[:, 16 * a + 4 * kq + kk:16 * b:16], True, False, 128), (o, T.neye[:], xv, False, True, 128)]
-                mm(lst, fk + ["eye", "neye", "xvin" + s], [bn], [bn], 4, True)
-                for kk in ks:
-                    ac(T.mv[:, a:b, 4 * kq + kk], nt(T[bn], kk, 128), AF.Abs, 128, [bn], [mk[4 * kq + kk]], [bn])
-            mm([(T.B3[:, a:b], Z(T.z16, r), T.mv[:, a + r:b:16, :], r == 0, r == 15, 128) for r in range(16)], ["z16"] + mk, ["keyV"], ["B3"], 4, True)
-        if t > 0:
+            renew(t - 1, [d])
+            ts(T.alh[:], aqw.indirect(al), -2048.0, None, A.add, None, 60 + GA * L, [ak, "alist" + s], ["alh"])
             o = 144 * (t - 1) + 15
-            mm([(T.B1[:, L:L + 16], T.bok[:, o - r:o + 128 - r], T.alh[:, r:L:16], r == 0, r == 15, 16) for r in range(16)],
-               ["bok%d" % (t - 1), "alh"], ["eP"], ["B1"])
-            ts(T.plist[:], T.B1[:, L:L + 16], 2048.0, None, A.add, None, 16, ["eP"], ["plist"], ["B1"])
-            gat("S", T.farp[:], T.xB[:, 0:W], T.plist[:], L, ["xB", "plist"], ["farp"])
-            mm([(T.B6[:, 0:L], T.eye[:], T.farp[:], True, False, L), (T.B6[:, 0:L], T.neye[:], nt(T.xvin, t), False, True, L)],
-               ["farp", "eye", "neye", "xvin" + s], ["B6"], ["B6"])
-            ac(T.mvp[:], T.B6[:, 0:L], AF.Abs, L, ["B6"], ["mvp"], ["B6"])
-            mm([(T.B3[:, t - 1:L:16], Z(T.z16, r), T.mvp[:, r:L:16], r == 0, r == 15, 16) for r in range(16)], ["z16", "mvp"], ["keyV"], ["B3"])
-        if t < RO - 1:
-            gcp(T.xB[:, t:W:16], nt(T.nxc, t), L, ["nxc" + s], ["xB"])
-        if t == 0:
-            send(-3, [(T.rep3[:], T.xB[:])], "rr3", "lr3", ["xB"], ["rep3"], 7000)
-        scan(T.vsc[:], T.cmin[:], T.B3[:, 0:L], A.add, A.min, L, ["cmin", "keyV"], ["vsc"], ["B3"])
+            mm([(T.B7[:, L:L + 16], T.boh[:], T.c128[:, 0:16], True, False, 16)]
+               + [(T.B7[:, L:L + 16], T.bok[:, o - r:o + 128 - r], T.alh[:, r:L:16], False, r == 15, 16) for r in range(16)],
+               ["bok%d" % (t - 1), "alh", "boh", "c128"], ["B7hi"], ["B7"], 17)
+            cp(T.plist[:], T.B7[:, L:L + 16], 16, ["B7hi"], ["plist"], ["B7"])
+            gat("S", T.farp[:], rep, T.plist[:], L, [rk, "plist"], ["farp"])
+            mm([(T.B4[:, 0:L], T.eye[:], T.farp[:], True, False, L), (T.B4[:, 0:L], T.neye[:], xv, False, True, L)],
+               ["farp", "eye", "neye", "xvc" + s], ["B4"], ["B4"])
+            ac(T.mvp[:], T.B4[:, 0:L], AF.Abs, L, ["B4"], ["mvp"], ["B4"], False)
+            mm([(T.B6[:, t - 1:L:16], Z(T.z16, r), T.mvp[:, r:L:16], r == 0, r == 15, 16) for r in range(16)], ["z16", "mvp"], ["B6lo"], ["B6"], 16)
+        scan(T.vsc[:], T.cmin[:], T.B6[:, 0:L], A.add, A.min, L, ["cmin", "B6lo"], ["vsc"], ["B6"])
         cp(T.vi[:], T.vsc[:, 15:L:16], 16, ["vsc"], ["vi"])
         ts(T.vj[:], T.vi[:], 15, None, A.bitwise_and, None, 16, ["vi"], ["vj"])
         cp(T.vu[:], T.vj[:], 16, ["vj"], ["vu"])
+        mm([(T.B6[:, L:2 * L], Z(T.zh, t), nt(T.nown, t), True, False, L)], ["zh", "nown" + s], ["B6hi"], ["B6"])
         tt(T.selv[:], T.oh[:, 32:48].indirect(T.vu[:]), T.alh[:], A.mult, 60 + GA * L, ["vu", "oh2", "alh"], ["selv"])
-        mm([(T.B1[:, 0:L], Z(T.zh, t), nt(T.nownin, t), True, False, L)], ["zh", "nownin" + s], ["dP"], ["B1"])
-        mm([(T.B1[:, 0:L], Z(T.zh, t), T.selv[:], False, True, L)], ["zh", "selv"], ["dP"], ["B1"])
-        ac(nt(T.dout, t), T.B1[:, 0:L], AF.Copy, L, ["dP"], ["dout" + s], ["B1"])
-        send(-1 - t % 3, [(nt(T.din, t), nt(T.dout, t))], "rd" + s, "lsm", ["dout" + s], ["din" + s], 2800)
+        mm([(T.B6[:, L:2 * L], Z(T.zh, t), T.selv[:], False, True, L)], ["zh", "selv"], ["B6hi"], ["B6"])
+        tt(T.B7[:, L:2 * L], T.B6[:, L:2 * L], nt(T.free, t), A.mult, L, ["B6hi", "free" + s], ["B7hi"], ["B6", "B7"])
+        tt(nt(T.ymc, t), T.aqs[:, t:W:16], T.B7[:, L:2 * L], A.add, L, AQ + ["B7hi"], ["ymc" + s] + TMP, ["B7"])
+        ks = [k for k, (tu, du) in enumerate(UPD) if tu == t]
+        if ks:
+            send([(UPD[k][1], nt(T.ymin, k), nt(T.ymc, t), "uq%d" % k) for k in ks], "lsm", ["ymc" + s, "rs"], ["ymin%d" % k for k in ks] + ["rs"], 0.5)
+        dma(T.ym[:, t * L:(t + 1) * L], T.ymc[t:128:16, t * L:(t + 1) * L], "outs", ["ymc" + s], [], 0.05)
+        for k in ks:
+            gcp(T["rep%d" % UPD[k][1]][:, t:W:16], nt(T.updin, k), L, ["updin%d" % k], ["rep%d" % UPD[k][1]])
+        if t > 0:
+            renew(t - 1, [x for x in (1, 2, 3) if x != d])
 
-    def back(t):
-        s = str(t)
-        tt(T.B1[:, L:2 * L], nt(T.din, t), nt(T.B5, t % 2), A.mult, L, ["din" + s, "free%d" % (t % 2)], ["eP"], ["B1", "B5"])
-        if t < RO - 1:
-            tt(T.aqs[:, t:W:16], T.aqs[:, t:W:16], T.B1[:, L:2 * L], A.add, L, ["aq", "eP"], ["aq"], ["B1"])
-            cp(nt(T.ymc, t), T.aqs[:, t:W:16], L, ["aq"], ["ymc" + s])
-        else:
-            tt(nt(T.ymc, t), T.aqs[:, t:W:16], T.B1[:, L:2 * L], A.add, L, ["aq", "eP"], ["ymc" + s], ["B1"])
-        dma("Y", T.ym[:, t * L:(t + 1) * L], T.ymc[t:128:16, t * L:(t + 1) * L], "outs", ["ymc" + s], [], 2500)
+    def renew(t, dists):
+        for k, (tu, du) in enumerate(UPD):
+            if tu == t and du in dists:
+                (gcp if CFG["renew"] == "G" else cp)(T["aqr%d" % du][:, t:W:16], nt(T.ymin, k), L, ["ymin%d" % k], ["aqr%d" % du])
 
     def targets():
         st = T.stab[:, 0:WD]
         for t in (2, 1, 0):
             so = ["soff%d_%d" % (t, e) for e in range(4)]
-            gat("S", nt(T.vall, t), st, nt(T.alist, t, 16), L, ["stab", "alist%d" % t], ["vall%d" % t])
+            gat("S", nt(T.vall, t), st, nt(T.alist, t, 16), L, ["stab", "alist%d" % t, "ymc0"], ["vall%d" % t])
             gat("V", T.swp[:, 0:32], st, T.soff[:, 4 * t + 2:4 * t + 4], 32, ["stab"] + so, ["swp0"])
             gat("V", T.swp[:, 32:64], st, T.soff[:, 4 * t:4 * t + 2], 32, ["stab"] + so, ["swp1"])
             sca(st, nt(T.soff, t, 4), T.swp[:], 64, so + ["swp0", "swp1"], ["stab"])
-            gat("S", T.urow[:, 128 * t:128 * t + 64], st, T.ulist[:, 8 * t:8 * t + 4], 64, ["stab", "ulist%d" % t], ["urow%d" % t])
-        q = 32
-        for n in range(L // q):
-            gat(CFG["yg"][n], T.yy[:, 16 * q * n:16 * q * (n + 1)], st, T.tgu[:, q * n:q * (n + 1)], 16 * q, ["stab", "tgu"], ["yy%d" % n])
+            gat("S", nt(T.urow, t, 64), st, T.ulist[:, 10 * t:10 * t + 4], 64, ["stab", "ulist%d" % t], ["urow%d" % t])
+        n8 = len(CFG["yg"])
+        w = L // n8
+        for n in range(n8):
+            gat(CFG["yg"][n], T.yy[:, 16 * w * n:16 * w * (n + 1)], st, T.tgu[:, w * n:w * (n + 1)], 16 * w, ["stab", "tgu"], ["yy%d" % x for x in range(n * 8 // n8, (n + 1) * 8 // n8)])
         for t in range(RO):
-            redirect(T.yy[:, 0:WD], "yy", t, 1, ["yy%d" % n for n in range(L // q)] if t == 0 else [])
+            redirect(T.yy[:, 0:WD], "yy", t, 1, ["yy%d" % n for n in range(9)] if t == 0 else [])
             redirect(T.yy[:, 0:WD], "yy", t, 2)
-            if t < RO - 1:
-                cp(T.yy[:, t:W:16], nt(T.vall, t), L, ["vall%d" % t], ["yy"])
-            else:
-                cp(T.yy[:, t:W:16], T.tw[:, t:W:16], L, ["tw"], ["yy"])
-        dma("Y", T.yt[:, :], T.yy[0:128:16, 0:W], "outs", ["yy"], [], 3000)
+            o, a, key = (T.yy[:, t:W:16], nt(T.vall, t), "vall%d" % t) if t < RO - 1 else (T.yy[:, t:W:16], T.tw[:, t:W:16], "tw")
+            cp(o, a, L, [key], ["yy"])
+            ops[-1]["alt"] = {"V": (ops[-1]["f"], L), "S": ([lambda o=o, a=a: S.activation(o, a, AF.Copy)], L)}
+        dma(T.yt[:, :], T.yy[0:128:16, 0:W], "outs", ["yy"], [], 0.2)
 
     for t in range(RO):
+        phase[0] = "n"
         night(t)
         if t == RO - 1:
+            phase[0] = "t"
             targets()
+        phase[0] = "v"
         visit(t)
-    back(RO - 1)
     return ops
 
 
@@ -437,17 +599,22 @@ def depend(ops):
     for i, o in enumerate(ops):
         dep = {}
 
-        def add(j, how):
-            dep[(j, how)] = not (o["e"] == "P" and ops[j]["e"] == "P")
+        def add(j, how, key=None):
+            if key in ("ld", "rs", "hs"):
+                dep.setdefault((j, "o", None), False)
+            elif how == "w" and ops[j]["k"] == "r":
+                dep[(j, how, ops[j]["W"].index(key))] = True
+            else:
+                dep[(j, how, 0)] = not (o["e"] == "P" and ops[j]["e"] == "P")
         for k in o["R"]:
             if k in last:
-                add(last[k], "w")
+                add(last[k], "w", k)
         for k in o["W"]:
             if k in last:
-                add(last[k], "w")
+                add(last[k], "w", k)
             for j in readers.get(k, []):
                 if j != i:
-                    add(j, "r")
+                    add(j, "r", k)
         for b in o["b"]:
             eng, cur, prev = epoch.get(b, (None, [], []))
             if eng == o["e"]:
@@ -462,23 +629,23 @@ def depend(ops):
         for k in o["W"]:
             last[k] = i
             readers[k] = []
-        o["dep"] = [(j, how, wt) for (j, how), wt in dep.items()]
+        o["dep"] = [(j, how, n, wt) for (j, how, n), wt in dep.items()]
 
 
-def place(eng, dur, pred, prio):
+def place(eng, dur, pred, prio, first=None):
     n = len(eng)
     p = list(prio)
-    for i in range(n):
-        for j, lt in pred[i]:
+    for i in (range(n) if first is None else range(n - 1, -1, -1)):
+        for j, lt, dm in pred[i]:
             if p[j] >= p[i]:
                 p[i] = p[j] + 0.001
-    lo = {e: [] for e in "VSPGY"}
-    hi = {e: [] for e in "VSPGY"}
+    lo = {e: [] for e in "VSPGYH"}
+    hi = {e: [] for e in "VSPGYH"}
     start = [0.0] * n
     for i in sorted(range(n), key=lambda k: p[k]):
-        t = 0.0
-        for j, lt in pred[i]:
-            x = start[j] + dur[j] + lt
+        t = 0.0 if first is None else first[i]
+        for j, lt, dm in pred[i]:
+            x = start[j] + dur[j] + lt + dm
             if x > t:
                 t = x
         a, b, d = lo[eng[i]], hi[eng[i]], dur[i]
@@ -494,36 +661,46 @@ def place(eng, dur, pred, prio):
     return start
 
 
-def replay(eng, dur, pred, tail, order):
-    fin, why, free, last = [0.0] * len(eng), [None] * len(eng), {e: 0.0 for e in "VSPGY"}, {e: None for e in "VSPGY"}
+def replay(eng, dur, pred, move, lat, order):
+    n = len(eng)
+    fin, done, why, free, last = [0.0] * n, [0.0] * n, [None] * n, {e: 0.0 for e in "VSPGYH"}, {e: None for e in "VSPGYH"}
+    busy = {True: 0.0, False: 0.0}
     for i in order:
         t, w = free[eng[i]], (last[eng[i]], True)
-        for j, lt in pred[i]:
-            if fin[j] + lt >= t:
-                t, w = fin[j] + lt, (j, False)
-        fin[i] = free[eng[i]] = t + dur[i]
+        for j, lt, dm in pred[i]:
+            x = (done[j] if dm else fin[j]) + lt
+            if x >= t:
+                t, w = x, (j, False)
+        fin[i] = done[i] = free[eng[i]] = t + dur[i]
+        if move[i]:
+            busy[eng[i] == "H"] = done[i] = max(fin[i] + lat, busy[eng[i] == "H"]) + move[i]
         why[i], last[eng[i]] = w, i
-    i = max(range(len(eng)), key=lambda k: fin[k] + tail[k])
-    end, pairs = fin[i] + tail[i], []
+    i = max(range(n), key=lambda k: done[k])
+    return done[i], why, fin, i
+
+
+def neighbours(why, i):
+    pairs = []
     while i is not None:
         if why[i][1] and why[i][0] is not None:
             pairs.append((why[i][0], i))
         i = why[i][0]
-    return end, pairs
+    return pairs
 
 
 def schedule(sets):
     ops = sets[0]
     n = len(ops)
     eng = [o["e"] for o in ops]
-    tail = [o["lat"] for o in ops]
     durs = [[o["d"] for o in s] for s in sets]
-    preds = [[[(j, ops[j]["lat"] + (c[3] if wt else 0.0)) for j, how, wt in o["dep"]] for o in ops] for c in COSTS]
+    moves = [[o["mib"] * c[4] for o in ops] for c in COSTS]
+    tail = [(COSTS[0][5] + moves[0][i] + o["hint"]) if o["mib"] else 0.0 for i, o in enumerate(ops)]
+    preds = [[[(j, c[3] if wt else 0.0, 0.0 if how == "o" else tail[j]) for j, how, k, wt in o["dep"]] for o in ops] for c in COSTS]
     level = [durs[0][i] + tail[i] for i in range(n)]
     last = list(level)
     for i in range(n - 1, -1, -1):
-        for j, lt in preds[0][i]:
-            level[j] = max(level[j], durs[0][j] + lt + level[i])
+        for j, lt, dm in preds[0][i]:
+            level[j] = max(level[j], durs[0][j] + lt + dm + level[i])
     group, names, count = [], {}, 0
     for i, o in enumerate(ops):
         key = (o["e"], (o["W"] + ["-"])[0].split("_")[0])
@@ -535,18 +712,41 @@ def schedule(sets):
     group = np.array(group)
     rs = np.random.RandomState(CFG["seed"])
 
-    def score(prio, bound=1e18):
+    loose = [i for i, o in enumerate(ops) if "alt" in o]
+    marks = [i for i, o in enumerate(ops) if o["e"] == "V" and o["W"][0][:-1] in ("x", "alist", "ymc")]
+
+    def critical(res):
+        x = res[rs.randint(len(res))]
+        return neighbours(x[1], x[3] if rs.randint(2) else marks[rs.randint(len(marks))])
+
+    def score(prio, eng, bound=1e18):
         st = place(eng, durs[0], preds[0], prio)
-        if max(st[k] + last[k] for k in range(n)) > bound:
-            return None
         order = sorted(range(n), key=lambda k: (st[k], k))
-        res = [replay(eng, durs[m], preds[m], tail, order) for m in range(len(sets))]
-        return sum(x[0] for x in res) / len(res), np.array(st), order, res
-    top = best = score([-(level[i] + (0.0 if ops[i]["bulk"] else CFG["bonus"])) for i in range(n)])
+        res = [replay(eng, durs[0], preds[0], moves[0], COSTS[0][5], order)]
+        if res[0][0] > bound:
+            return None
+        res += [replay(eng, durs[m], preds[m], moves[m], COSTS[m][5], order) for m in range(1, len(sets))]
+        return sum(x[0] + CFG["pull"] * sum(x[2][k] for k in marks) for x in res) / len(res), np.array(st), order, res, eng
+    top = best = min((score([-(level[i] + (0.0 if ops[i]["bulk"] else x) + (y if ops[i]["ph"] == "n" else 0.0)) for i in range(n)], eng)
+                      for x in CFG["bonus"] for y in CFG["lead"]), key=lambda z: z[0])
+    succ = [[] for i in range(n)]
+    for i in range(n):
+        for j, lt, dm in preds[0][i]:
+            succ[j].append((i, lt, dm))
+    d0 = np.array(durs[0])
     for it in range(CFG["tries"]):
-        p = best[1].copy()
-        if it % 4:
-            pairs = best[3][rs.randint(len(sets))][1]
+        p, eng = best[1].copy(), best[4]
+        if it < 12 or it % CFG["turn"] == 0:
+            p = -np.array(place(eng, durs[0], succ, (-p - d0 + rs.normal(size=n) * rs.choice([0.0, 30.0, 100.0])).tolist(), tail)) - d0
+        elif it % 8 == 3:
+            eng = list(eng)
+            pairs = [x for ab in critical(best[3]) for x in ab if "alt" in ops[x]]
+            a = pairs[rs.randint(len(pairs))] if pairs and rs.randint(2) else loose[rs.randint(len(loose))]
+            near = [x for x in loose if eng[x] != eng[a] and abs(p[x] - p[a]) < 2500]
+            for x in [a] + ([near[rs.randint(len(near))]] if near and rs.randint(2) else []):
+                eng[x] = "S" if eng[x] == "V" else "V"
+        elif it % 4:
+            pairs = critical(best[3])
             a, b = pairs[rs.randint(len(pairs))]
             kind = rs.randint(4)
             if kind == 0:
@@ -558,56 +758,64 @@ def schedule(sets):
             else:
                 p[group == group[a]] += p[group == group[b]].max() - p[a] + 1.0
         else:
-            near = np.unique(group[np.abs(p - rs.uniform(8000, p.max())) < 3000])
+            near = np.unique(group[np.abs(p - rs.uniform(6000, p.max())) < 3000])
             if len(near) == 0:
                 continue
             for x in rs.choice(near, rs.randint(1, 4)):
                 p[group == x] += rs.normal() * rs.choice([300.0, 1200.0, 4000.0])
-        cand = score(p.tolist(), best[3][0][0] + 300.0)
+        cand = score(p.tolist(), eng, best[3][0][0] + 300.0)
         if cand is not None and cand[0] <= best[0] + CFG["temp"] * (1.0 - it / CFG["tries"]) * rs.exponential():
             best = cand
         if best[0] < top[0]:
             top = best
     for i in range(n):
-        ops[i]["t"] = float(top[1][i])
-    return top[2], [x[0] for x in top[3]]
+        ops[i]["t"] = top[3][0][2][i] - durs[0][i]
+    return top[2], [x[0] for x in top[3]], top[4]
 
 
 MEMO = {}
 
 
 def rank_program(g, core, T, topo):
-    rank = T.rank_of(core)
+    rank, helping = T.rank_of(core), core in helpers(T, topo)
+    if helping:
+        rank = helpers(T, topo).index(core)
     if rank is None:
         return
     sets = [build(g, T, topo, rank, c) for c in (COSTS if "order" not in MEMO else COSTS[:1])]
     ops = sets[0]
     depend(ops)
     if "order" not in MEMO:
-        MEMO["order"] = schedule(sets)[0]
-    order = MEMO["order"]
-    queue = {"V": g.vector, "S": g.scalar, "P": g.tensor, "G": g, "Y": g.sync}
+        MEMO["order"] = schedule(sets)
+    order, ends, eng = MEMO["order"]
+    for o, e in zip(ops, eng):
+        if e != o["e"]:
+            o["e"], o["f"] = e, o["alt"][e][0]
+    queue = {"H": g} if helping else {"V": g.vector, "S": g.scalar, "P": g.tensor, "G": g, "Y": g.sync}
     total = {}
     for i in order:
         o = ops[i]
         if o["k"] == "c":
             sm = "e" + o["e"]
             total[sm] = total.get(sm, 0) + len(o["f"])
-            o["tw"] = o["tr"] = (sm, total[sm])
+            o["tw"] = o["tr"] = [(sm, total[sm])]
         else:
-            total[o["sem"]] = total.get(o["sem"], 0) + o["cnt"]
-            o["tw"] = o["tr"] = (o["sem"], total[o["sem"]])
+            for sm in o["sem"]:
+                total[sm] = total.get(sm, 0) + o["cnt"]
+            o["tw"] = o["tr"] = [(sm, total[sm]) for sm in o["sem"]]
             if o["k"] == "r":
-                total[o["lsem"]] = total.get(o["lsem"], 0) + o["cnt"]
-                o["tr"] = (o["lsem"], total[o["lsem"]])
+                total[o["lsem"]] = total.get(o["lsem"], 0) + o["cnt"] * len(o["sem"])
+                o["tr"] = [(o["lsem"], total[o["lsem"]])]
     seen = {e: {} for e in queue}
     for i in order:
         o = ops[i]
+        if o["e"] not in queue:
+            continue
         q = queue[o["e"]]
         need = {}
-        for j, how, wt in o["dep"]:
+        for j, how, k, wt in o["dep"]:
             if wt:
-                sm, c = ops[j]["t" + how]
+                sm, c = ops[j]["t" + how][k]
                 need[sm] = max(need.get(sm, 0), c)
         for sm, c in need.items():
             if seen[o["e"]].get(sm, 0) < c:
@@ -618,7 +826,7 @@ def rank_program(g, core, T, topo):
             if o["k"] == "c":
                 ins.then_inc(T.sem["e" + o["e"]], 1)
             elif o["k"] == "d":
-                ins.then_inc(T.sem[o["sem"]], 16)
+                ins.then_inc(T.sem[o["sem"][0]], 16)
     for sm, c in total.items():
-        if max(seen[e].get(sm, 0) for e in seen) < c:
+        if (sm[0] == "h") == helping and max(seen[e].get(sm, 0) for e in seen) < c:
             g.wait_ge(T.sem[sm], c)

@@ -9,13 +9,13 @@ MAGIC = 12582912.0
 
 F32, BF, F16, I32, U16 = "float32", "bfloat16", "float16", "int32", "uint16"
 SB = {
-    BF: {"xA": W, "rep1": W, "rep2": W, "rep3": W, "near": W, "far": W, "xvc": RO * L, "xvq": RO * L, "nxc": RO * L, "updin": 6 * L, "at1": L,
-         "a2": L, "at3": 4 * L, "idrow": 64, "lanerow": L, "farp": L, "mvp": L, "xa": L, "mh": L, "free": RO * L, "nbo": 128, "hey": 128, "nhey": 128,
+    BF: {"xA": W, "rep1": W, "rep2": W, "rep3": W, "near": W, "far": W, "xvc": RO * L, "xvq": 3 * L, "nxc": RO * L, "updin": 6 * L, "at1": L,
+         "a2": L, "at3": 4 * L, "idrow": 64, "lanerow": L, "farp": L, "mvp": L, "xa": L, "mh": L, "free": RO * L, "hey": 128, "nhey": 128,
          "half": L, "z32": 144, "zm16": 144, "z16": 144, "eye": 128, "neye": 128, "bo": 128, "oh": 48, "rst": L},
     F16: {"ownh": RO * L, "nown": RO * L, "alh": L, "selv": L, "zh": 144, "boh": 128, "bok": 432, "c128": 144, "eqd": 264,
           "cvoid": 264, "nsc": 264},
     I32: {"aqs": W, "aqr1": W, "aqr2": W, "aqr3": W, "tgs": L, "ki": 16, "kj": 16, "vi": 16, "vj": 16, "pi": 2, "ri": 2},
-    U16: {"tgu": L, "ownu": RO * L, "alist": RO * 16, "alu": L, "plist": 16, "ku": 16, "vu": 16, "ulist": RO * 10, "tlist": 16, "soff": RO * 4,
+    U16: {"tgu": L, "ownj": L, "ownu": RO * L, "alist": RO * 16, "alu": L, "plist": 16, "ku": 16, "vu": 16, "ulist": RO * 10, "tlist": 16, "soff": RO * 4,
           "woff": RO * 4, "repl": WD // 16, "prm": RO * 16, "prr": RO * 16},
     F32: {"stab": WD, "tw": WD, "yy": WD, "ymc": RO * L, "ymin": 6 * L, "ksc": L, "vsc": L, "rowpo": 96, "st1": 64, "zcol": 2, "asc": L,
           "ub": 64, "bsc": 64, "ucol": 4, "tm": 64, "swp": 64, "vall": 3 * L, "nrow": L, "urow": RO * 64, "zr1": 32, "b2": L, "kcm": 4,
@@ -23,20 +23,21 @@ SB = {
 }
 SCRATCH = {k: ("sbuf", [128, n], d) for d in SB for k, n in SB[d].items()}
 SCRATCH.update({k: ("sbuf", [128, L, 16], BF) for k in ("mc", "mv")})
+SCRATCH["nbo"] = ("sbuf", [128, 128], BF)
 SCRATCH["sel"] = ("sbuf", [128, 2, L], F16)
 SCRATCH.update({"B%d" % b: ("psum", [128, 512], F32) for b in range(8)})
 UPD = [(0, 2), (0, 3), (0, 1), (1, 3), (1, 1), (2, 1)]
-PIECES = 4
+PIECES = 8
 SEMAPHORES = (["eV", "eS", "eP", "eG", "ldx", "ldt", "outs", "lsm"] + ["ldq%d" % p for p in range(PIECES)]
-              + ["lx1", "lx2", "lx3", "lq1", "lq3", "rx1", "rx2", "rx3", "rq0", "rq1", "rq2", "rq3", "hq0", "hq1", "hl"] + ["u%s%d" % (a, k) for a in "xq" for k in range(len(UPD))])
-COSTS = [(1.56, 3.8, 0.5, 150.0, 3000.0, 2200.0), (1.15, 2.2, 0.45, 110.0, 4500.0, 2800.0), (1.95, 5.4, 0.65, 210.0, 3600.0, 2500.0)]
+              + ["lx1", "lx2", "lq1", "rx1", "rx2", "rx3", "rq0", "rq1", "rq2", "rq3", "hq0", "hq1", "hl"] + ["u%s%d" % (a, k) for a in "xq" for k in range(len(UPD))])
+COSTS = [(1.56, 3.8, 0.5, 250.0, 3000.0, 2200.0, 1.0), (1.25, 2.5, 0.5, 220.0, 4200.0, 2800.0, 1.1), (1.8, 5.0, 0.5, 280.0, 3300.0, 2500.0, 1.3)]
 CFG = {
-    "cg": ["S64 V64 S64 V64"] + ["F32 S64 S64 S48 F48"] * 3,
-    "cn": ["A64 M64 A64 M64"] + ["R32 M64 M64 M48 R48"] * 3,
-    "parts": "P32 P64 P64 P96", "clamp": 1, "split": 1, "per": 8,
+    "cg": ["S32 S32 V32 S32 V32 S32 V32 S16 V16", "F96 S64 S64 S32", "F96 S64 S64 S32", "F48 S48 S64 S64 S32"],
+    "cn": ["M64 A64 M64 M64", "R96 M64 M96", "R96 M64 M96", "R48 M48 M64 M96"],
+    "parts": "P96 P64 P96", "clamp": 1, "split": 0, "per": 8, "late": [1, 2],
     "vg": ["S64 S64 S64 S64"] * 3 + ["V64 S64 V64 V64"],
-    "yg": "SVSVSVSV", "xa": "S", "free": "V", "redo": 1, "patch": [1, 2, 3], "reset": "G", "renew": "G",
-    "bonus": [0.0, 700.0, 1500.0, 3000.0], "lead": [0.0, 1000.0, 2000.0, 4000.0, 8000.0, 16000.0], "tries": 10000, "seed": 2, "temp": 50.0, "pull": 0.05, "turn": 100, "mg": 2,
+    "yg": "SVSVSVSV", "xa": "S", "free": "V", "redo": 1, "reset": "V", "lists": "G", "renew": "GGGGGG",
+    "bonus": [0.0, 700.0, 1500.0, 3000.0], "lead": [0.0, 1000.0, 2000.0, 4000.0, 8000.0, 16000.0], "tries": 15000, "seed": 5, "temp": 50.0, "pull": 0.1, "turn": 100, "mg": 2, "near": 0.15,
 }
 FIRST = 96
 
@@ -64,7 +65,6 @@ def build(g, T, topo, rank, cost):
     ops, phase = [], ["s"]
     V, S, P = g.vector, g.scalar, g.tensor
     core, helper = T.cores[rank], helpers(T, topo)[rank]
-    mate = [r for r in range(N) if r != rank and topo.die(T.cores[r]) == topo.die(core)][0]
     GA, SCA, PE = cost[:3]
 
     def op(eng, fns, dur, R, Wr, banks=(), kind="c", sem=None, lsem=None, cnt=0, mib=0.0, hint=0.0, bulk=False):
@@ -85,6 +85,9 @@ def build(g, T, topo, rank, cost):
 
     def fill(out, n, c, R, Wr):
         ts(out, T.nrow[:, 0:n], 0.0, c, A.mult, A.add, n, ["nrow"] + R, Wr)
+
+    def put(out, n, c, key):
+        op("V", [lambda: V.memset(out, c)], max(64, n), [], [key])
 
     def tt(out, a, b, o, n, R, Wr, banks=(), bulk=False):
         op("V", [lambda: V.tensor_tensor(out, a, b, o)], max(64, n), R, Wr, banks, bulk=bulk)
@@ -151,32 +154,31 @@ def build(g, T, topo, rank, cost):
     q = W // PIECES
     AQ = ["aq%d" % p for p in range(PIECES)]
     aqw = T.aqs[:, 0:W]
+    dma(T.xA[:], T.x[:], "ldx", ["ld"], ["xA", "ld"], 1.0)
     for p in range(PIECES):
-        dma(T.aqs[:, p * q:(p + 1) * q], T.aq[:, p * q:(p + 1) * q], "ldq%d" % p, ["ld"], [AQ[p], "ld"], 2.0 / PIECES, 0 if p == 0 else 3000 + 6000 * p / PIECES)
-        if p == 0:
-            dma(T.xA[:], T.x[:], "ldx", ["ld"], ["xA", "ld"], 1.0, 6000 / PIECES)
+        dma(T.aqs[:, p * q:(p + 1) * q], T.aq[:, p * q:(p + 1) * q], "ldq%d" % p, ["ld"], [AQ[p], "ld"], 2.0 / PIECES, 2900 + 5900 * p / PIECES)
     dma(T.tgs[:], T.tg[:], "ldt", ["ld"], ["tgs", "ld"], 0.125, 9000)
 
     col = T.col
     rc, pc, gc15, gc0, r128, kc, r1, c15, cu, cv, t0, r4 = [col[:, i:i + 1] for i in range(12)]
     iota(T.pi[:], [[0, 2]], 0, 1, 2, ["pi"], False)
     iota(T.nrow[:], [[1, L]], 0, 0, L, ["nrow"])
-    iota(T.ksc[:], [[0, 16], [1, 16]], 0, 0, L, ["ksc"])
     ina, g16, vw, inw = T.ymc[:, 0:264], T.ymc[:, 272:400], T.ymc[:, 400:464], T.ymc[:, 464:532]
     prow, psc, pf = T.vall[:, 0:L], T.vall[:, L:2 * L], T.vall[:, 2 * L:2 * L + 64]
     iota(g16, [[16, 8], [0, 16]], 0, 0, 128, ["g16"])
     iota(T.asc[:], [[-16, 2], [0, 4], [1, 32]], 0, 0, L, ["asc"])
     iota(vw, [[-16, 2], [1, 32]], 0, 0, 64, ["vw"])
-    iota(T.vsc[:], [[0, 4], [1, 64]], 0, 0, L, ["vsc"])
+    iota(T.lanerow[:], [[16, L]], 0, 0, L, ["lanerow"])
     parts = spans(CFG["parts"])
     for a, b, kind in parts:
         iota(prow[:, a:b], [[128, 16], [16, (b - a) // 32], [2048, 2]], a // 2, 0, b - a, ["prow%d" % a])
     iota(pf, [[1, 4], [16, 8], [2048, 2]], 0, 0, 64, ["pf"])
     iota(T.idrow[:], [[16, 2], [128, 32]], 48, 0, 64, ["idrow"])
     iota(T.idf[:], [[16, 2], [2048, 2]], 48, 0, 4, ["idf"])
-    for h in range(8):
-        iota(nt(T.stab, h, WD // 8), [[1, WD // 8]], h * WD // 8, 0, WD // 8, ["stab%d" % h])
-    STAB0 = ["stab%d" % h for h in range(8)]
+    for h in range(WD // L):
+        op("S", [lambda h=h: S.activation(nt(T.stab, h), T.nrow[:], AF.Identity, bias=float(L * h))], L, ["nrow"], ["stab%d" % h])
+    join(5)
+    STAB0 = ["stab%d" % h for h in range(WD // L)]
     ts(T.ri[:], T.pi[:], 15, None, A.bitwise_and, None, 2, ["pi"], ["ri"])
     cp(rc, T.ri[:, 0:1], 1, ["ri"], ["rc"])
     cp(pc, T.pi[:, 0:1], 1, ["pi"], ["pc"])
@@ -196,38 +198,43 @@ def build(g, T, topo, rank, cost):
     ts(T.dum[:], T.nrow[:, 0:128:64], r4, None, A.add, None, 2, ["nrow", "r4"], ["dum"])
     for i, (c, key) in enumerate(((c15, "c15"), (cu, "cu"), (cv, "cv"))):
         ts(T.oh[:, 16 * i:16 * i + 16], T.nrow[:, 0:16], c, None, A.is_equal, None, 16, ["nrow", key], ["oh%d" % i])
-    for buf, sc, key in ((T.z32, 32.0, "z32"), (T.zm16, -16.0, "zm16"), (T.z16, 16.0, "z16"), (T.zh, 1.0, "zh")):
-        ts(buf[:], T.nrow[:, 0:144], gc15, sc, A.is_equal, A.mult, 144, ["nrow", "gc15"], [key])
-    for buf, sc, key in ((T.eye, 1.0, "eye"), (T.neye, -1.0, "neye"), (T.hey, 0.5, "hey"), (T.nhey, -0.5, "nhey")):
-        ts(buf[:], T.nrow[:, 0:128], pc, sc, A.is_equal, A.mult, 128, ["nrow", "pc"], [key])
-    fill(T.half[:], L, 0.5, [], ["half"])
+    ts(T.zh[:], T.nrow[:, 0:144], gc15, None, A.is_equal, None, 144, ["nrow", "gc15"], ["zh"])
+    ts(T.eye[:], T.nrow[:, 0:128], pc, None, A.is_equal, None, 128, ["nrow", "pc"], ["eye"])
+    for buf, sc, key in ((T.z32, 32.0, "z32"), (T.zm16, -16.0, "zm16"), (T.z16, 16.0, "z16")):
+        ts(buf[:], T.zh[:], sc, None, A.mult, None, 72, ["zh"], [key])
+    for buf, sc, key in ((T.neye, -1.0, "neye"), (T.hey, 0.5, "hey"), (T.nhey, -0.5, "nhey")):
+        ts(buf[:], T.eye[:], sc, None, A.mult, None, 64, ["eye"], [key])
+    put(T.half[:], 128, 0.5, "half")
     fill(T.c128[:], 144, 128.0, [], ["c128"])
     ts(T.bo[:], g16, gc0, KF, A.is_equal, A.mult, 128, ["g16", "gc0"], ["bo"])
     ts(T.boh[:], g16, gc0, None, A.is_equal, None, 128, ["g16", "gc0"], ["boh"])
     ts(T.prm[:], pf, r128, None, A.add, None, 64, ["pf", "r128"], ["prm"])
     ts(T.kcm[:], T.nrow[:, 0:4], kc, None, A.subtract, None, 4, ["nrow", "kc"], ["kcm"])
-    ts(T.nbo[:], g16, gc0, -KF, A.is_equal, A.mult, 128, ["g16", "gc0"], ["nbo"])
+    if CFG["clamp"]:
+        ts(T.nbo[:], g16, gc0, -KF, A.is_equal, A.mult, 128, ["g16", "gc0"], ["nbo"])
     for t in range(RO - 1):
         ts(nt(T.bok, t, 144), T.zh[:], T.nrm[:, t:t + 1], None, A.mult, None, 72, ["zh", "nrm"], ["bok%d" % t])
-    ts(T.cmax[:], T.ksc[:], 0.0, -1000000.0, A.is_equal, A.mult, L, ["ksc"], ["cmax"])
-    ts(T.cmax[:], T.cmax[:], 1.0, None, A.add, None, L, ["cmax"], ["cmax"])
-    ts(T.cfz[:], T.ksc[:], rc, -20000.0, A.is_equal, A.mult, L, ["ksc", "rc"], ["cfz"])
-    ts(T.cmin[:], T.ksc[:], r1, KF, A.is_equal, A.mult, L, ["ksc", "r1"], ["cmin"])
-    tt(T.cfz[:], T.cfz[:], T.cmin[:], A.add, 2 * L, ["cfz", "cmin"], ["cfz"])
-    ts(T.cmin[:], T.cmax[:], -1.0, None, A.mult, None, L, ["cmax"], ["cmin"])
-    ts(T.rst[:], T.vsc[:], 0.0, None, A.is_gt, None, L, ["vsc"], ["rst"])
-    ts(T.lanerow[:], T.nrow[:], 16.0, None, A.mult, None, L, ["nrow"], ["lanerow"])
+    for buf, sc, key in ((T.cmax, 1.0, "cmax"), (T.cmin, -1.0, "cmin")):
+        put(buf[:], L, sc, key)
+        put(buf[:, 0:L:16], 16, -1000000.0 * sc, key)
+    ts(T.cfz[:, 0:16], T.nrow[:, 0:16], rc, -20000.0, A.is_equal, A.mult, 16, ["nrow", "rc"], ["cfz"])
+    ts(T.cfz[:, 16:32], T.nrow[:, 0:16], r1, KF, A.is_equal, A.mult, 16, ["nrow", "r1"], ["cf2"])
+    tt(T.cfz[:, 0:16], T.cfz[:, 0:16], T.cfz[:, 16:32], A.add, 32, ["cfz", "cf2"], ["cfz"])
+    for w in (16, 32, 64, 128):
+        cp(T.cfz[:, w:2 * w], T.cfz[:, 0:w], w, ["cfz"], ["cfz"])
+    put(T.rst[:], 128, 1.0, "rst")
+    put(T.rst[:, 0:L:64], 4, 0.0, "rst")
     for c1 in range(2):
         a = 128 * c1 + 32
         ts(T.asc[:, a:a + 32], T.asc[:, a:a + 32], -1.0, None, A.add, None, 32, ["asc"], ["asc"])
+    put(ina, 264, 0.0, "ina")
     for h in range(2):
-        fill(nt(ina, h, 132), 132, 0.0, [], ["ina"])
         fill(nt(T.eqd, h, 132), 132, 0.0, [], ["eqd0", "eqd1", "eqd2", "eqd3"])
         ts(ina[:, 132 * h + 2:132 * h + 130], nt(T.asc, h, 128), rc, KF, A.is_ge, A.mult, 128, ["asc", "rc"], ["ina"])
     tt(T.cvoid[:, 1:264], ina[:, 1:264], ina[:, 0:263], A.subtract, 528, ["ina"], ["cvoid"])
     fill(T.cvoid[:, 0:264:132], 2, -30000.0, ["cvoid"], ["cvoid"])
     fill(T.cvoid[:, 131:264:132], 2, -128.0, ["cvoid"], ["cvoid"])
-    fill(inw, 68, 0.0, [], ["inw"])
+    put(inw, 68, 0.0, "inw")
     fill(T.eqw[:], 136, 0.0, [], ["eqw0", "eqw1", "eqw2", "eqw3"])
     for h in range(2):
         ts(inw[:, 34 * h + 1:34 * h + 33], nt(vw, h, 32), rc, KF, A.is_ge, A.mult, 32, ["vw", "rc"], ["inw"])
@@ -242,25 +249,41 @@ def build(g, T, topo, rank, cost):
         return buf[:, 15 - r:143 - r]
 
     lo, hi = nt(T.aqs, 0, W // 2), nt(T.aqs, 1, W // 2)
-    send([(None, lo, lo, "hq0")], "lq1", AQ[:-1] + ["rs"], ["hq0", "rs"], 1.0)
+    send([(None, lo, lo, "hq0")], "lq1", AQ[:PIECES * 3 // 4] + ["rs"], ["hq0", "rs"], 1.0)
     send([(1, T.rep1[:], T.xA[:], "rx1")], "lx1", ["xA", "rs"], ["rep1", "rs"], 1.0, 2400)
     send([(1, nt(T.aqr1, 1, W // 2), hi, "rq1")], "lq1", AQ + ["rs"], ["aqr1b", "rs"], 1.0, 4800)
     send([(None, hi, hi, "hq1")], "lq1", AQ + ["rs"], ["hq1", "rs"], 1.0, 7200)
+    send([(1, T.rep2[:], T.rep1[:], "rx2")], "lx2", ["rep1", "rs"], ["rep2", "rs"], 1.0, 5400)
     send([(1, nt(T.aqr1, 0, W // 2), lo, "rq0")], "hl", ["hq0", "hs"], ["aqr1", "hs"], 1.0, by="H")
-    send([(2, T.aqr2[:], T.aqs[:], "rq2")], "hl", ["hq0", "hq1", "hs"], ["aqr2", "hs"], 2.0, 3000, by="H")
-    send([(1, T.rep2[:], T.rep1[:], "rx2")], "lx2", ["rep1", "rs"], ["rep2", "rs"], 1.0, 3000)
+    send([(2, T.aqr2[:], T.aqs[:], "rq2")], "hl", ["hq0", "hq1", "hs"], ["aqr2", "hs"], 2.0, by="H")
+    send([(3, T.aqr3[:], T.aqs[:], "rq3")], "hl", ["hq0", "hq1", "hs"], ["aqr3", "hs"], 2.0, 5400, by="H")
     for t in range(RO):
         if t == 0:
             for p in range(PIECES):
                 cp(T.ownu[:, p * q // 16:(p + 1) * q // 16], T.aqs[:, p * q:(p + 1) * q:16], q // 16, [AQ[p]], ["ownu0_%d" % p])
             cp(nt(T.xvc, t), T.xA[:, t:W:16], 128, ["xA"], ["xvc%d" % t])
         else:
-            gat("V", nt(T.ownu, t), aqw, nt(T.prr, t, 16), L, AQ + ["prr%d" % t], ["ownu%d_%d" % (t, p) for p in range(PIECES)], False)
             gcp(nt(T.xvc, t), T.xA[:, t:W:16], L, ["xA"], ["xvc%d" % t])
-            gat("S", nt(T.xvq, t), T.xA[:, 0:W], nt(T.prr, t, 16), L, ["xA", "prr%d" % t], ["xvq%d" % t])
-        ts(nt(T.ownh, t), aqw.indirect(nt(T.prm, t, 16)), -2048.0, None, A.add, None, 60 + GA * L, AQ + ["prm"], ["ownh%d" % t])
+            gat("S", nt(T.xvq, t - 1), T.xA[:, 0:W], nt(T.prr, t, 16), L, ["xA", "prr%d" % t], ["xvq%d" % t])
+        if t > 0 and CFG["lists"] == "G":
+            for a, b, kind in parts:
+                nc = (b - a) // 16
+                for c in range(nc):
+                    o = 2048 * (c % 2) + a // 2 + 16 * (c // 2) + t
+                    gcp(T.ownu[:, t * L + a + c:t * L + b:nc], T.aqs[:, o:o + 1921:128], 16, AQ, ["ownu%d_%d" % (t, c)])
+                join(nc)
+                ops[-1]["W"] = ["ownu%d_%d" % (t, p) for p in range(PIECES)]
+            for role in range(8):
+                gcp(T.ownj[:, 32 * role:32 * role + 32], T.aqs[:, 16 * role + t:W:128], 32, AQ, ["ownj"])
+                if role % 4 == 3:
+                    join(4)
+            ts(nt(T.ownh, t), T.ownj[:], -2048.0, None, A.add, None, 128, ["ownj"], ["ownh%d" % t])
+        else:
+            if t > 0:
+                gat("V", nt(T.ownu, t), aqw, nt(T.prr, t, 16), L, AQ + ["prr%d" % t], ["ownu%d_%d" % (t, p) for p in range(PIECES)], False)
+            ts(nt(T.ownh, t), aqw.indirect(nt(T.prm, t, 16)), -2048.0, None, A.add, None, 60 + GA * L, AQ + ["prm"], ["ownh%d" % t])
         ts(nt(T.nown, t), T.aqs[:, t:W:16], -2048.0, T.nrm[:, 4 + t:5 + t], A.add, A.mult, L, AQ + ["nrn"], ["nown%d" % t])
-    cp(T.tgu[:], T.tgs[:], L, ["tgs"], ["tgu"])
+    (gcp if CFG["lists"] == "G" else cp)(T.tgu[:], T.tgs[:], L, ["tgs"], ["tgu"])
 
     REP, YK, room = {}, {}, 0
     for t in range(1, RO):
@@ -282,7 +305,7 @@ def build(g, T, topo, rank, cost):
             else:
                 gat(e, raw[:, 16 * a:16 * b], win, lst[:, a:b], 16 * (b - a), [wkey] + lkeys(a, b), wr)
 
-    def scores(tag, raw, non, a, b, kind, xv, xkey, blocks, key, kb, first, last, diff, skip=-1):
+    def scores(tag, raw, non, a, b, kind, xv, xkey, blocks, key, kb, first, last, diff, skip=-1, later=None):
         rk = ["%sraw%d" % (tag, u) for u in range(a // 16, b // 16)]
         nk = ["%snon%d_%d" % (tag, u, k) for k in range(16) for u in range(a // 16, b // 16)]
         m = len(nk) // 16
@@ -299,18 +322,24 @@ def build(g, T, topo, rank, cost):
         else:
             for kh in range(2):
                 bn = diff[kh]
-                k0 = 8 * kh + (1 if skip == 8 * kh else 0)
-                nn = 8 * kh + 8 - k0
-                w = nn * (b - a)
-                lst = []
-                for k in range(nn):
-                    o = T[bn][:, k:w:nn]
-                    lst += [(o, T.eye[:], raw[:, 16 * a + k0 + k:16 * b:16], k == 0, False, b - a), (o, T.neye[:], xv[:, a:b], False, k == nn - 1, b - a)]
+                lo, hi = 8 * kh, 8 * kh + 8
+                runs = [(x, y) for x, y in (((lo, skip), (skip + 1, hi)) if lo <= skip < hi else ((lo, hi),)) if x < y]
+                lst, w = [], b - a
+                for x, y in runs:
+                    for k in range(x, y):
+                        o = T[bn][:, w * (x - lo) + k - x:w * (y - lo):y - x]
+                        lst += [(o, T.eye[:], raw[:, 16 * a + k:16 * b:16], not lst, False, w), (o, T.neye[:], xv[:, a:b], False, k == hi - 1, w)]
                 mm(lst, rk + ["eye", "neye", xkey], [bn], [bn], CFG["per"], True)
-                ac(non[:, a:b, k0:k0 + nn], T[bn][:, 0:w], AF.Abs, w, [bn], nk[8 * m * kh:8 * m * kh + 8 * m], [bn])
+                for x, y in runs:
+                    ac(non[:, a:b, x:y], T[bn][:, w * (x - lo):w * (y - lo)], AF.Abs, w * (y - x), [bn], nk[m * x:m * y], [bn])
+                join(len(runs))
         z = T.z16 if kind == "A" else T.z32
-        mm([(o, Z(z, r), non[:, i:j:st, :], first and kind == "A" and x == 0, last and x == len(blocks) - 1, n) for x, (r, o, i, j, st, n) in enumerate(blocks)],
-           nk + ["z32", "z16"], [key], [kb], CFG["per"], True)
+        total = lambda: mm([(o, Z(z, r), non[:, i:j:st, :], first and kind == "A" and x == 0, last and x == len(blocks) - 1, n)
+                            for x, (r, o, i, j, st, n) in enumerate(blocks)], nk + ["z32", "z16"], [key], [kb], CFG["per"], True)
+        if later is None:
+            total()
+        else:
+            later.append(total)
 
     def redirect(win, key, t, w, more=()):
         o = 4 * t + 2 * (w - 1)
@@ -321,7 +350,7 @@ def build(g, T, topo, rank, cost):
         s = str(t)
         xv = nt(T.xvc, t)
         B0, B1, B2 = T.B0, T.B1, T.B2
-        xq, qk = (xv, "xvc0") if t == 0 else (nt(T.xvq, t), "xvq" + s)
+        xq, qk = (xv, "xvc0") if t == 0 else (nt(T.xvq, t - 1), "xvq" + s)
         how = spans(CFG["cn"][t])
         mm([(B0[:, 0:L], T.eye[:], xq, True, True, L)], ["eye", qk], ["B0lo"], ["B0"])
         DR = 32 if CFG["split"] and t > 0 else FIRST
@@ -337,11 +366,11 @@ def build(g, T, topo, rank, cost):
                 nc = (y - x) // 16
                 blocks = [(r, T[bank(b)][:, x:y], x + r * nc, x + (r + 1) * nc, 1, y - x) for r in range((a - x) // nc, (b - x) // nc)]
             scores("c", T.near, T.mc, a, b, kind, xq, qk, blocks, bank(b) + "lo", bank(b), a == 0 or (t > 0 and a in (DR, FIRST)),
-                   b == L or (t > 0 and b in (DR, FIRST)), ("B3", "B3"))
+                   b == L or (t > 0 and b in (DR, FIRST)), ("B3", "B1" if t == 0 else "B3"))
 
         def best(a, b, kb, h):
             ca, cb = a // 16, b // 16
-            scan(T.ksc[:, a:b], T.cmax[:, a:b], T[kb][:, a:b], A.add, A.max, b - a, ["cmax", kb + "lo", "ksc"], ["ksc" + x for x in h], [kb])
+            scan(T.ksc[:, a:b], T.cmax[:, a:b], T[kb][:, a:b], A.add, A.max, b - a, ["cmax", kb + "lo"], ["ksc" + x for x in h], [kb])
             cp(T.ki[:, ca:cb], T.ksc[:, a + 15:b:16], 16, ["ksc" + x for x in h], ["ki" + x for x in h])
             ts(T.kj[:, ca:cb], T.ki[:, ca:cb], 15, None, A.bitwise_and, None, 16, ["ki" + x for x in h], ["kj" + x for x in h])
             if t == 0:
@@ -505,11 +534,9 @@ def build(g, T, topo, rank, cost):
         if t < RO - 1:
             gcp(nt(T.nxc, t), T.xA[:, t:W:16], L, ["xA"], ["nxc" + s])
             ks = [k for k, (tu, du) in enumerate(UPD) if tu == t]
-            send([(UPD[k][1], nt(T.updin, k), nt(T.nxc, t), "ux%d" % k) for k in ks], "lsm", ["nxc" + s, "rs"], ["updin%d" % k for k in ks] + ["rs"], 0.3)
+            send([(UPD[k][1], nt(T.updin, k), nt(T.nxc, t), "ux%d" % k) for k in ks], "lsm", ["nxc" + s, "rs"], ["updin%d" % k for k in ks] + ["rs"], 0.1 * len(ks))
         if t == 0:
-            own = (mate + 3) % N == rank
-            send([(rank - mate, T.rep3[:], (T.xA if own else T.rep2)[:], "rx3")], "lx3", ["xA", "rep2", "rs"], ["rep3", "rs"], 1.0)
-            send([(rank - mate, T.aqr3[:], (T.aqs if own else T.aqr2)[:], "rq3")], "lq3", AQ + ["aqr2", "rs"], ["aqr3", "rs"], 2.0, 3000)
+            send([(2, T.rep3[:], T.rep1[:], "rx3")], "lx2", ["rep1", "rs"], ["rep3", "rs"], 1.0)
         dma(T.yx[:, t * L:(t + 1) * L], nt(T.nxc, t), "outs", ["nxc" + s], [], 0.1)
 
     def visit(t):
@@ -517,14 +544,13 @@ def build(g, T, topo, rank, cost):
         d = 1 + t % 3
         rep, rk, aqw, ak = T["rep%d" % d][:, 0:W], "rep%d" % d, T["aqr%d" % d][:, 0:W], "aqr%d" % d
         xv, al = nt(T.xvc, t), nt(T.alist, t, 16)
-        if t > 0 and t not in CFG["patch"]:
-            renew(t - 1, [d])
         gat("V", T.alu[:], aqw, al, L, [ak, "aqr1b", "alist" + s], ["alu"], False)
         gathers("v", T.far, rep, rk, T.alu, lambda a, b: ["alu"], spans(CFG["vg"][t]))
+        later = []
         for a in range(0, L, 64):
             scores("v", T.far, T.mv, a, a + 64, "A", xv, "xvc" + s, [(r, T.B6[:, a:a + 64], a + r, a + 64, 16, 64) for r in range(16)],
-                   "B6lo", "B6", a == 0, a + 64 == L, ("B4", "B5"), 0 if t == 1 and t in CFG["patch"] else -1)
-        if t not in CFG["patch"]:
+                   "B6lo", "B6", a == 0, a + 64 == L, ("B4", "B5"), t - 1, later if t in CFG["late"] else None)
+        if t == 0:
             ts(T.alh[:], T.alu[:], -2048.0, None, A.add, None, 128, ["alu"], ["alh"])
         else:
             renew(t - 1, [d])
@@ -535,10 +561,15 @@ def build(g, T, topo, rank, cost):
                ["bok%d" % (t - 1), "alh", "boh", "c128"], ["B7hi"], ["B7"], 17)
             cp(T.plist[:], T.B7[:, L:L + 16], 16, ["B7hi"], ["plist"], ["B7"])
             gat("S", T.farp[:], rep, T.plist[:], L, [rk, "plist"], ["farp"])
-            mm([(T.B4[:, 0:L], T.eye[:], T.farp[:], True, False, L), (T.B4[:, 0:L], T.neye[:], xv, False, True, L)],
-               ["farp", "eye", "neye", "xvc" + s], ["B4"], ["B4"])
-            ac(T.mvp[:], T.B4[:, 0:L], AF.Abs, L, ["B4"], ["mvp"], ["B4"], False)
-            mm([(T.B6[:, t - 1:L:16], Z(T.z16, r), T.mvp[:, r:L:16], r == 0, r == 15, 16) for r in range(16)], ["z16", "mvp"], ["B6lo"], ["B6"], 16)
+            mm([(T.B7[:, 0:L], T.eye[:], T.farp[:], True, False, L), (T.B7[:, 0:L], T.neye[:], xv, False, True, L)],
+               ["farp", "eye", "neye", "xvc" + s], ["B7lo"], ["B7"])
+            if later:
+                ac(T.mv[:, :, t - 1], T.B7[:, 0:L], AF.Abs, L, ["B7lo"], ["vnon%d_%d" % (u, t - 1) for u in range(16)], ["B7"], False)
+                for total in later:
+                    total()
+            else:
+                ac(T.mvp[:], T.B7[:, 0:L], AF.Abs, L, ["B7lo"], ["mvp"], ["B7"], False)
+                mm([(T.B6[:, t - 1:L:16], Z(T.z16, r), T.mvp[:, r:L:16], r == 0, r == 15, 16) for r in range(16)], ["z16", "mvp"], ["B6lo"], ["B6"], 16)
         scan(T.vsc[:], T.cmin[:], T.B6[:, 0:L], A.add, A.min, L, ["cmin", "B6lo"], ["vsc"], ["B6"])
         cp(T.vi[:], T.vsc[:, 15:L:16], 16, ["vsc"], ["vi"])
         ts(T.vj[:], T.vi[:], 15, None, A.bitwise_and, None, 16, ["vi"], ["vj"])
@@ -550,7 +581,7 @@ def build(g, T, topo, rank, cost):
         tt(nt(T.ymc, t), T.aqs[:, t:W:16], T.B7[:, L:2 * L], A.add, L, AQ + ["B7hi"], ["ymc" + s] + TMP, ["B7"])
         ks = [k for k, (tu, du) in enumerate(UPD) if tu == t]
         if ks:
-            send([(UPD[k][1], nt(T.ymin, k), nt(T.ymc, t), "uq%d" % k) for k in ks], "lsm", ["ymc" + s, "rs"], ["ymin%d" % k for k in ks] + ["rs"], 0.5)
+            send([(UPD[k][1], nt(T.ymin, k), nt(T.ymc, t), "uq%d" % k) for k in ks], "lsm", ["ymc" + s, "rs"], ["ymin%d" % k for k in ks] + ["rs"], 0.16 * len(ks))
         dma(T.ym[:, t * L:(t + 1) * L], T.ymc[t:128:16, t * L:(t + 1) * L], "outs", ["ymc" + s], [], 0.05)
         for k in ks:
             gcp(T["rep%d" % UPD[k][1]][:, t:W:16], nt(T.updin, k), L, ["updin%d" % k], ["rep%d" % UPD[k][1]])
@@ -560,7 +591,7 @@ def build(g, T, topo, rank, cost):
     def renew(t, dists):
         for k, (tu, du) in enumerate(UPD):
             if tu == t and du in dists:
-                (gcp if CFG["renew"] == "G" else cp)(T["aqr%d" % du][:, t:W:16], nt(T.ymin, k), L, ["ymin%d" % k], ["aqr%d" % du])
+                (gcp if CFG["renew"][k] == "G" else cp)(T["aqr%d" % du][:, t:W:16], nt(T.ymin, k), L, ["ymin%d" % k], ["aqr%d" % du])
 
     def targets():
         st = T.stab[:, 0:WD]
@@ -692,12 +723,25 @@ def schedule(sets):
     ops = sets[0]
     n = len(ops)
     eng = [o["e"] for o in ops]
-    durs = [[o["d"] for o in s] for s in sets]
+    durs = [[o["d"] * (c[6] if o["k"] == "c" else 1.0) for o in s] for s, c in zip(sets, COSTS)]
     moves = [[o["mib"] * c[4] for o in ops] for c in COSTS]
     tail = [(COSTS[0][5] + moves[0][i] + o["hint"]) if o["mib"] else 0.0 for i, o in enumerate(ops)]
     preds = [[[(j, c[3] if wt else 0.0, 0.0 if how == "o" else tail[j]) for j, how, k, wt in o["dep"]] for o in ops] for c in COSTS]
+    anc, des = [0] * n, [0] * n
+    for i in range(n):
+        for j, lt, dm in preds[0][i]:
+            anc[i] |= anc[j] | 1 << j
+    for i in range(n - 1, -1, -1):
+        for j, lt, dm in preds[0][i]:
+            des[j] |= des[i] | 1 << i
+    for pred in preds:
+        for i in range(n):
+            far = 0
+            for j, lt, dm in pred[i]:
+                if lt:
+                    far |= anc[j]
+            pred[i] = [x for x in pred[i] if ops[x[0]]["k"] != "c" or ops[x[0]]["e"] == "P" or not far >> x[0] & 1]
     level = [durs[0][i] + tail[i] for i in range(n)]
-    last = list(level)
     for i in range(n - 1, -1, -1):
         for j, lt, dm in preds[0][i]:
             level[j] = max(level[j], durs[0][j] + lt + dm + level[i])
@@ -717,26 +761,46 @@ def schedule(sets):
 
     def critical(res):
         x = res[rs.randint(len(res))]
-        return neighbours(x[1], x[3] if rs.randint(2) else marks[rs.randint(len(marks))])
+        return neighbours(x[1], x[3] if rs.randint(2) else marks[rs.randint(len(marks))]) or neighbours(res[0][1], res[0][3])
 
-    def score(prio, eng, bound=1e18):
-        st = place(eng, durs[0], preds[0], prio)
-        order = sorted(range(n), key=lambda k: (st[k], k))
+    def score(prio, eng, bound=1e18, order=None):
+        if order is None:
+            st = place(eng, durs[0], preds[0], prio)
+            order = sorted(range(n), key=lambda k: (st[k], k))
         res = [replay(eng, durs[0], preds[0], moves[0], COSTS[0][5], order)]
         if res[0][0] > bound:
             return None
         res += [replay(eng, durs[m], preds[m], moves[m], COSTS[m][5], order) for m in range(1, len(sets))]
-        return sum(x[0] + CFG["pull"] * sum(x[2][k] for k in marks) for x in res) / len(res), np.array(st), order, res, eng
+        return sum(x[0] + CFG["pull"] * sum(x[2][k] for k in marks) for x in res) / len(res), np.array(res[0][2]) - d0, order, res, eng
+
+    def shift(order, a, b, ahead):
+        i, j = order.index(a), order.index(b)
+        mid = order[i:j + 1]
+        x = b if ahead else a
+        mask = (anc[x] if ahead else des[x]) | 1 << x
+        took, left = [k for k in mid if mask >> k & 1], [k for k in mid if not mask >> k & 1]
+        return order[:i] + (took + left if ahead else left + took) + order[j + 1:]
+    d0 = np.array(durs[0])
     top = best = min((score([-(level[i] + (0.0 if ops[i]["bulk"] else x) + (y if ops[i]["ph"] == "n" else 0.0)) for i in range(n)], eng)
                       for x in CFG["bonus"] for y in CFG["lead"]), key=lambda z: z[0])
     succ = [[] for i in range(n)]
     for i in range(n):
         for j, lt, dm in preds[0][i]:
             succ[j].append((i, lt, dm))
-    d0 = np.array(durs[0])
     for it in range(CFG["tries"]):
-        p, eng = best[1].copy(), best[4]
-        if it < 12 or it % CFG["turn"] == 0:
+        p, eng, order = best[1].copy(), best[4], None
+        if rs.uniform() < CFG["near"]:
+            pairs = critical(best[3])
+            a, b = pairs[rs.randint(len(pairs))]
+            if rs.randint(3) == 0:
+                same = [k for k in best[2] if eng[k] == eng[a]]
+                x = same.index(a)
+                if rs.randint(2):
+                    a = same[max(0, x - rs.randint(1, 5))]
+                else:
+                    b = same[min(len(same) - 1, x + 1 + rs.randint(1, 5))]
+            order = shift(best[2], a, b, rs.randint(2))
+        elif it < 12 or it % CFG["turn"] == 0:
             p = -np.array(place(eng, durs[0], succ, (-p - d0 + rs.normal(size=n) * rs.choice([0.0, 30.0, 100.0])).tolist(), tail)) - d0
         elif it % 8 == 3:
             eng = list(eng)
@@ -745,6 +809,8 @@ def schedule(sets):
             near = [x for x in loose if eng[x] != eng[a] and abs(p[x] - p[a]) < 2500]
             for x in [a] + ([near[rs.randint(len(near))]] if near and rs.randint(2) else []):
                 eng[x] = "S" if eng[x] == "V" else "V"
+            if rs.randint(2):
+                order = sorted(best[2], key=lambda k: p[k])
         elif it % 4:
             pairs = critical(best[3])
             a, b = pairs[rs.randint(len(pairs))]
@@ -763,7 +829,7 @@ def schedule(sets):
                 continue
             for x in rs.choice(near, rs.randint(1, 4)):
                 p[group == x] += rs.normal() * rs.choice([300.0, 1200.0, 4000.0])
-        cand = score(p.tolist(), eng, best[3][0][0] + 300.0)
+        cand = score(p.tolist(), eng, best[3][0][0] + 300.0, order)
         if cand is not None and cand[0] <= best[0] + CFG["temp"] * (1.0 - it / CFG["tries"]) * rs.exponential():
             best = cand
         if best[0] < top[0]:
@@ -793,8 +859,9 @@ def rank_program(g, core, T, topo):
             o["e"], o["f"] = e, o["alt"][e][0]
     queue = {"H": g} if helping else {"V": g.vector, "S": g.scalar, "P": g.tensor, "G": g, "Y": g.sync}
     total = {}
-    for i in order:
+    for at, i in enumerate(order):
         o = ops[i]
+        o["at"] = at
         if o["k"] == "c":
             sm = "e" + o["e"]
             total[sm] = total.get(sm, 0) + len(o["f"])
@@ -807,20 +874,26 @@ def rank_program(g, core, T, topo):
                 total[o["lsem"]] = total.get(o["lsem"], 0) + o["cnt"] * len(o["sem"])
                 o["tr"] = [(o["lsem"], total[o["lsem"]])]
     seen = {e: {} for e in queue}
+    known = {e: {} for e in queue}
     for i in order:
         o = ops[i]
         if o["e"] not in queue:
             continue
-        q = queue[o["e"]]
+        q, kn = queue[o["e"]], known[o["e"]]
         need = {}
         for j, how, k, wt in o["dep"]:
             if wt:
                 sm, c = ops[j]["t" + how][k]
-                need[sm] = max(need.get(sm, 0), c)
-        for sm, c in need.items():
-            if seen[o["e"]].get(sm, 0) < c:
+                if c > need.get(sm, (0, 0))[0]:
+                    need[sm] = (c, j)
+        for sm, (c, j) in sorted(need.items(), key=lambda x: -ops[x[1][1]]["at"]):
+            if kn.get(sm, 0) < c:
                 q.wait_ge(T.sem[sm], c)
-                seen[o["e"]][sm] = c
+                seen[o["e"]][sm] = kn[sm] = c
+                for x, y in ops[j].get("kn", {}).items():
+                    kn[x] = max(kn.get(x, 0), y)
+        if o["k"] == "c":
+            o["kn"] = dict(kn)
         for f in o["f"]:
             ins = f()
             if o["k"] == "c":

@@ -9,16 +9,16 @@ MAGIC = 12582912.0
 
 F32, BF, F16, I32, U16 = "float32", "bfloat16", "float16", "int32", "uint16"
 SB = {
-    BF: {"xA": W, "rep1": W, "rep2": W, "rep3": W, "near": W, "far": W, "xvc": RO * L, "xvq": 3 * L, "nxc": RO * L, "updin": 6 * L, "at1": L,
+    BF: {"xA": W, "rep1": W, "rep2": W, "rep3": W, "near": W, "far": W, "reps": 448 * 16, "xvc": RO * L, "xvq": 3 * L, "nxc": RO * L, "updin": 6 * L, "at1": L,
          "a2": L, "at3": 4 * L, "idrow": 64, "lanerow": L, "farp": L, "mvp": L, "xa": L, "mh": L, "free": RO * L, "hey": 128, "nhey": 128,
          "half": L, "z32": 144, "zm16": 144, "z16": 144, "eye": 128, "neye": 128, "bo": 128, "oh": 48, "rst": L},
-    F16: {"ownh": RO * L, "nown": RO * L, "alh": L, "selv": L, "zh": 144, "boh": 128, "bok": 432, "c128": 144, "eqd": 264,
+    F16: {"ownh": RO * L, "nown": RO * L, "ub": 64, "alh": L, "selv": L, "zh": 144, "boh": 128, "bok": 432, "c128": 144, "eqd": 264,
           "cvoid": 264, "nsc": 264},
-    I32: {"aqs": W, "aqr1": W, "aqr2": W, "aqr3": W, "tgs": L, "ki": 16, "kj": 16, "vi": 16, "vj": 16, "pi": 2, "ri": 2},
+    I32: {"aqs": W, "aqr1": W, "aqr2": W, "aqr3": W, "tgs": L, "ksc": L, "vsc": L, "kj": 16, "vj": 16, "pi": 2, "ri": 2},
     U16: {"tgu": L, "ownj": L, "ownu": RO * L, "alist": RO * 16, "alu": L, "plist": 16, "ku": 16, "vu": 16, "ulist": RO * 10, "tlist": 16, "soff": RO * 4,
-          "woff": RO * 4, "repl": WD // 16, "prm": RO * 16, "prr": RO * 16},
-    F32: {"stab": WD, "tw": WD, "yy": WD, "ymc": RO * L, "ymin": 6 * L, "ksc": L, "vsc": L, "rowpo": 96, "st1": 64, "zcol": 2, "asc": L,
-          "ub": 64, "bsc": 64, "ucol": 4, "tm": 64, "swp": 64, "vall": 3 * L, "nrow": L, "urow": RO * 64, "zr1": 32, "b2": L, "kcm": 4,
+          "wo1": RO * 34, "wo2": RO * 68, "zlist": 4, "repl": 448, "prm": RO * 16, "prr": RO * 16},
+    F32: {"stab": WD, "tw": WD, "ymc": RO * L, "ymin": 6 * L, "rowpo": 96, "st1": 64, "zcol": 2, "asc": L,
+          "bsc": 64, "ucol": 4, "kct": 4, "swp": 64, "vall": RO * L, "nrow": L, "urow": RO * 64, "zr1": 34, "cw1": 17, "b2": L, "kcm": 4,
           "cwave": 68, "eqw": 136, "wsc": 136, "col": 16, "idf": 4, "idcol": 4, "dum": 2, "nrm": 8, "cfz": L, "cmax": L, "cmin": L},
 }
 SCRATCH = {k: ("sbuf", [128, n], d) for d in SB for k, n in SB[d].items()}
@@ -32,12 +32,12 @@ SEMAPHORES = (["eV", "eS", "eP", "eG", "ldx", "ldt", "outs", "lsm"] + ["ldq%d" %
               + ["lx1", "lx2", "lq1", "rx1", "rx2", "rx3", "rq0", "rq1", "rq2", "rq3", "hq0", "hq1", "hl"] + ["u%s%d" % (a, k) for a in "xq" for k in range(len(UPD))])
 COSTS = [(1.56, 3.8, 0.5, 250.0, 3000.0, 2200.0, 1.0), (1.25, 2.5, 0.5, 220.0, 4200.0, 2800.0, 1.1), (1.8, 5.0, 0.5, 280.0, 3300.0, 2500.0, 1.3)]
 CFG = {
-    "cg": ["S32 S32 V32 S32 V32 S32 V32 S16 V16", "F96 S64 S64 S32", "F96 S64 S64 S32", "F48 S48 S64 S64 S32"],
-    "cn": ["M64 A64 M64 M64", "R96 M64 M96", "R96 M64 M96", "R48 M48 M64 M96"],
+    "cg": ["S32 S32 V32 S32 V32 S32 V32 S16 V16", ] + ["F48 F48 S32 S32 S32 S32 S32"] * 3,
+    "cn": ["M64 A64 M64 M64"] + ["R48 R48 M64 M96"] * 3,
     "parts": "P96 P64 P96", "clamp": 1, "split": 0, "per": 8, "late": [1, 2],
-    "vg": ["S64 S64 S64 S64"] * 3 + ["V64 S64 V64 V64"],
+    "vg": ["S32 " * 8] * 3 + ["V64 S64 V64 V64"],
     "yg": "SVSVSVSV", "xa": "S", "free": "V", "redo": 1, "reset": "V", "lists": "G", "renew": "GGGGGG",
-    "bonus": [0.0, 700.0, 1500.0, 3000.0], "lead": [0.0, 1000.0, 2000.0, 4000.0, 8000.0, 16000.0], "tries": 15000, "seed": 5, "temp": 50.0, "pull": 0.1, "turn": 100, "mg": 2, "near": 0.15,
+    "bonus": [0.0, 700.0, 1500.0, 3000.0], "lead": [0.0, 1000.0, 2000.0, 4000.0, 8000.0, 16000.0], "tries": 30000, "seed": 5, "temp": 50.0, "pull": 0.6, "tol": 60.0, "halves": 1, "inorder": 1, "mg": 2, "share": [0.2, 0.2, 0.2, 0.3, 0.1], "starts": 3, "fill": [0.0], "vb": ["B4", "B5", "B3"],
 }
 FIRST = 96
 
@@ -174,7 +174,7 @@ def build(g, T, topo, rank, cost):
         iota(prow[:, a:b], [[128, 16], [16, (b - a) // 32], [2048, 2]], a // 2, 0, b - a, ["prow%d" % a])
     iota(pf, [[1, 4], [16, 8], [2048, 2]], 0, 0, 64, ["pf"])
     iota(T.idrow[:], [[16, 2], [128, 32]], 48, 0, 64, ["idrow"])
-    iota(T.idf[:], [[16, 2], [2048, 2]], 48, 0, 4, ["idf"])
+    iota(T.idf[:], [[16, 2], [2048, 2]], 48 - 2048, 0, 4, ["idf"])
     for h in range(WD // L):
         op("S", [lambda h=h: S.activation(nt(T.stab, h), T.nrow[:], AF.Identity, bias=float(L * h))], L, ["nrow"], ["stab%d" % h])
     join(5)
@@ -210,6 +210,7 @@ def build(g, T, topo, rank, cost):
     ts(T.boh[:], g16, gc0, None, A.is_equal, None, 128, ["g16", "gc0"], ["boh"])
     ts(T.prm[:], pf, r128, None, A.add, None, 64, ["pf", "r128"], ["prm"])
     ts(T.kcm[:], T.nrow[:, 0:4], kc, None, A.subtract, None, 4, ["nrow", "kc"], ["kcm"])
+    ts(T.kct[:], T.nrow[:, 0:4], kc, None, A.add, None, 4, ["nrow", "kc"], ["kct"])
     if CFG["clamp"]:
         ts(T.nbo[:], g16, gc0, -KF, A.is_equal, A.mult, 128, ["g16", "gc0"], ["nbo"])
     for t in range(RO - 1):
@@ -222,6 +223,11 @@ def build(g, T, topo, rank, cost):
     tt(T.cfz[:, 0:16], T.cfz[:, 0:16], T.cfz[:, 16:32], A.add, 32, ["cfz", "cf2"], ["cfz"])
     for w in (16, 32, 64, 128):
         cp(T.cfz[:, w:2 * w], T.cfz[:, 0:w], w, ["cfz"], ["cfz"])
+    ts(T.cw1[:], T.nrow[:, 0:17], rc, -KF, A.is_equal, A.mult, 17, ["nrow", "rc"], ["cw1"])
+    ts(T.zr1[:, 0:17], T.nrow[:, 0:17], r1, KF, A.is_equal, A.mult, 17, ["nrow", "r1"], ["zr1"])
+    tt(T.cw1[:], T.cw1[:], T.zr1[:, 0:17], A.add, 34, ["cw1", "zr1"], ["cw1"])
+    ts(T.cw1[:, 16:17], T.cw1[:, 16:17], -KF, None, A.add, None, 1, ["cw1"], ["cw1"])
+    put(T.zr1[:], 34, 0.0, "zr1")
     put(T.rst[:], 128, 1.0, "rst")
     put(T.rst[:, 0:L:64], 4, 0.0, "rst")
     for c1 in range(2):
@@ -264,7 +270,7 @@ def build(g, T, topo, rank, cost):
             cp(nt(T.xvc, t), T.xA[:, t:W:16], 128, ["xA"], ["xvc%d" % t])
         else:
             gcp(nt(T.xvc, t), T.xA[:, t:W:16], L, ["xA"], ["xvc%d" % t])
-            gat("S", nt(T.xvq, t - 1), T.xA[:, 0:W], nt(T.prr, t, 16), L, ["xA", "prr%d" % t], ["xvq%d" % t])
+            gat("S", nt(T.xvq, t - 1), T.xA[:, 0:W], nt(T.prr, t, 16), L, ["xA", "prr%d" % t, AQ[-1]], ["xvq%d" % t])
         if t > 0 and CFG["lists"] == "G":
             for a, b, kind in parts:
                 nc = (b - a) // 16
@@ -285,33 +291,40 @@ def build(g, T, topo, rank, cost):
         ts(nt(T.nown, t), T.aqs[:, t:W:16], -2048.0, T.nrm[:, 4 + t:5 + t], A.add, A.mult, L, AQ + ["nrn"], ["nown%d" % t])
     (gcp if CFG["lists"] == "G" else cp)(T.tgu[:], T.tgs[:], L, ["tgs"], ["tgu"])
 
-    REP, YK, room = {}, {}, 0
-    for t in range(1, RO):
+    REP, room = {}, 0
+    for t in range(RO):
         for a, b, e in spans(CFG["cg"][t]):
             if e == "F":
-                REP[t, a] = T.yy[:, room:room + 16 * (b - a)]
-                ts(T.repl[:, room // 16:room // 16 + b - a], prow[:, a:b], float(t), None, A.add, None, b - a,
-                   ["prow%d" % x for x, y, z in parts], ["repl%d" % room])
-                gat("S", REP[t, a], T.xA[:, 0:W], T.repl[:, room // 16:room // 16 + b - a], 16 * (b - a), ["xA", "repl%d" % room], ["rep%d_%d" % (t, a)])
-                YK[t, a] = ["yy%d" % x for x in range(room // 512, (room + 16 * (b - a) - 1) // 512 + 1)]
+                REP[t, a] = T.reps[:, room:room + 16 * (b - a)]
+                ts(T.repl[:, room // 16:room // 16 + b - a], prow[:, a:b] if t else T.lanerow[:, a:b], float(t), None, A.add, None, b - a,
+                   ["prow%d" % x for x, y, z in parts] + ["lanerow"], ["repl%d" % room])
+                gat("S", REP[t, a], T.xA[:, 0:W], T.repl[:, room // 16:room // 16 + b - a], 16 * (b - a), ["xA", "repl%d" % room] + ([AQ[-1]] if t else []),
+                    ["rep%d_%d" % (t, a)])
                 room += 16 * (b - a)
 
     def gathers(tag, raw, win, wkey, lst, lkeys, who, t=0):
         for a, b, e in who:
-            wr = ["%sraw%d" % (tag, u) for u in range(a // 16, b // 16)]
+            wr = ["%sraw%d" % (tag, u) for u in range(a // 8, b // 8)]
             if e == "F":
                 tt(raw[:, 16 * a:16 * b], win.indirect(lst[:, a:b]), REP[t, a], A.subtract, 60 + GA * 16 * (b - a),
-                   [wkey, "rep%d_%d" % (t, a)] + YK[t, a] + lkeys(a, b), wr, [], True)
+                   [wkey, "rep%d_%d" % (t, a)] + lkeys(a, b), wr, [], True)
             else:
                 gat(e, raw[:, 16 * a:16 * b], win, lst[:, a:b], 16 * (b - a), [wkey] + lkeys(a, b), wr)
 
+    def add(lst, R, key, kb):
+        for i in range(0, len(lst), CFG["per"]):
+            part = lst[i:i + CFG["per"]]
+            if part[0][3] or part[-1][4]:
+                mm(part, R, [key], [kb], len(part), True)
+            else:
+                mm(part, R + [key], ["%s_%d" % (key, len(ops))], [kb], len(part), True)
+
     def scores(tag, raw, non, a, b, kind, xv, xkey, blocks, key, kb, first, last, diff, skip=-1, later=None):
-        rk = ["%sraw%d" % (tag, u) for u in range(a // 16, b // 16)]
+        rk = ["%sraw%d" % (tag, u) for u in range(a // 8, b // 8)]
         nk = ["%snon%d_%d" % (tag, u, k) for k in range(16) for u in range(a // 16, b // 16)]
         m = len(nk) // 16
         if kind in "MR":
-            mm([(o, Z(T.zm16, r), raw[:, 16 * i:16 * j], first and x == 0, False, n) for x, (r, o, i, j, st, n) in enumerate(blocks)],
-               rk + ["zm16"], [key], [kb], CFG["per"], True)
+            add([(o, Z(T.zm16, r), raw[:, 16 * i:16 * j], first and x == 0, False, n) for x, (r, o, i, j, st, n) in enumerate(blocks)], rk + ["zm16"], key, kb)
         if kind == "R":
             ts(non[:, a:b, :], raw[:, 16 * a:16 * b], 0.0, None, A.max, None, 8 * (b - a), rk, nk, [], True)
         elif kind == "M":
@@ -334,17 +347,16 @@ def build(g, T, topo, rank, cost):
                     ac(non[:, a:b, x:y], T[bn][:, w * (x - lo):w * (y - lo)], AF.Abs, w * (y - x), [bn], nk[m * x:m * y], [bn])
                 join(len(runs))
         z = T.z16 if kind == "A" else T.z32
-        total = lambda: mm([(o, Z(z, r), non[:, i:j:st, :], first and kind == "A" and x == 0, last and x == len(blocks) - 1, n)
-                            for x, (r, o, i, j, st, n) in enumerate(blocks)], nk + ["z32", "z16"], [key], [kb], CFG["per"], True)
+        total = lambda: add([(o, Z(z, r), non[:, i:j:st, :], first and kind == "A" and x == 0, last and x == len(blocks) - 1, n)
+                             for x, (r, o, i, j, st, n) in enumerate(blocks)], nk + ["z32", "z16"], key, kb)
         if later is None:
             total()
         else:
             later.append(total)
 
     def redirect(win, key, t, w, more=()):
-        o = 4 * t + 2 * (w - 1)
-        sca(win, T.woff[:, o:o + 2], T.urow[:, 64 * t + 32 * (w - 1):64 * t + 32 * w], 32,
-            ["woff%d" % o, "woff%d" % (o + 1), "urow%d" % t], [key] + list(more))
+        off = T.wo1[:, 34 * t + 32:34 * t + 34] if w == 1 else T.wo2[:, 68 * t + 66:68 * t + 68]
+        sca(win, off, T.urow[:, 64 * t + 32 * (w - 1):64 * t + 32 * w], 32, ["woff%d%d" % (w, t), "urow%d" % t], [key] + list(more))
 
     def night(t):
         s = str(t)
@@ -371,8 +383,7 @@ def build(g, T, topo, rank, cost):
         def best(a, b, kb, h):
             ca, cb = a // 16, b // 16
             scan(T.ksc[:, a:b], T.cmax[:, a:b], T[kb][:, a:b], A.add, A.max, b - a, ["cmax", kb + "lo"], ["ksc" + x for x in h], [kb])
-            cp(T.ki[:, ca:cb], T.ksc[:, a + 15:b:16], 16, ["ksc" + x for x in h], ["ki" + x for x in h])
-            ts(T.kj[:, ca:cb], T.ki[:, ca:cb], 15, None, A.bitwise_and, None, 16, ["ki" + x for x in h], ["kj" + x for x in h])
+            ts(T.kj[:, ca:cb], T.ksc[:, a + 15:b:16], 15, None, A.bitwise_and, None, 16, ["ksc" + x for x in h], ["kj" + x for x in h])
             if t == 0:
                 for x in range(2):
                     cp(T.ku[:, x:16:2], T.kj[:, 8 * x:8 * x + 8], 8, ["kjA"], [["kuA", "kuD"], ["kuB"]][x])
@@ -428,6 +439,7 @@ def build(g, T, topo, rank, cost):
         join(4)
         so = ["soff%d_%d" % (t, e) for e in range(4)]
         cp(T.ulist[:, 10 * t:10 * t + ul[0][1]], B3[:, ul[0][2]:ul[0][2] + ul[0][1]], 10, [wb + "md"], ["ulist" + s], [wb])
+        cp(T.zlist[:, 0:4:2], B3[:, ul[0][2] + uz[1]:ul[0][2] + uz[1] + 2], 2, [wb + "md"], ["zlist"], [wb])
         for c1 in range(2):
             ts(T.eqw[:, 34 * c1 + 1:34 * c1 + 33], B3[:, zo:zo + 32], lst(1, c1, 1), T.dum[:, c1:c1 + 1], A.is_equal, A.mult, 32,
                [wb + "md", "dum"], ["eqw%d" % c1], [wb])
@@ -435,12 +447,13 @@ def build(g, T, topo, rank, cost):
         scan(T.wsc[:, 0:68], T.cwave[:], T.eqw[:, 0:68], A.add, A.max, 68, ["cwave", "eqw0", "eqw1"], ["wsc0"])
         sca(T.stab[:, 0:WD], nt(T.soff, t, 4), T.rowpo[:, 32:96], 64, so + ["rowpo"] + STAB0, ["stab"])
         st = T.stab[:, 0:W]
-        gat("V", T.zr1[:], st, T.ulist[:, 10 * t + uz[1]:10 * t + uz[1] + 2], 32, ["stab", "ulist" + s], ["zr1"])
-        gat("V", nt(T.urow, t, 64), st, T.ulist[:, 10 * t:10 * t + 4], 64, ["stab", "ulist" + s], ["urow" + s])
-        scan(T.st1[:, 0:32], T.cfz[:, 0:32], T.zr1[:], A.add, A.max, 32, ["cfz", "zr1"], ["st10"])
         for c1 in range(2):
-            ts(T.woff[:, 4 * t + c1:4 * t + c1 + 1], T.st1[:, 16 * c1 + 15:16 * c1 + 16], kc, T.wsc[:, 34 * c1 + 33:34 * c1 + 34], A.subtract, A.max, 1,
-               ["st10", "kc", "wsc0"], ["woff%d" % (4 * t + c1)])
+            gat("V", T.zr1[:, 17 * c1:17 * c1 + 16], st, T.zlist[:, 2 * c1:2 * c1 + 1], 16, ["stab", "zlist"], ["zr1"], False)
+        join(2)
+        gat("V", nt(T.urow, t, 64), st, T.ulist[:, 10 * t:10 * t + 4], 64, ["stab", "ulist" + s], ["urow" + s])
+        for c1 in range(2):
+            op("V", [lambda c1=c1: V.tensor_tensor_scan(T.wo1[:, 34 * t + c1:34 * t + 34:2], T.cw1[:], nt(T.zr1, c1, 17), T.wsc[:, 34 * c1 + 32:34 * c1 + 33],
+                                                        A.add, A.max)], 64, ["cw1", "zr1", "wsc0"], ["woff1" + s])
         join(2)
         redo = CFG["redo"] and t > 0
 
@@ -468,15 +481,15 @@ def build(g, T, topo, rank, cost):
         redirect(T.tw[:, 0:WD], "tw", t, 1)
         zrow = T.tw[:, 32 + t:W:128]
         scan(T.st1[:, 32:64], T.cfz[:, 0:32], zrow, A.add, A.max, 32, ["cfz", "tw"], ["st11"])
-        for c1 in range(2):
-            ts(T.eqw[:, 68 + 34 * c1 + 1:68 + 34 * c1 + 33], zrow, kc, T.st1[:, 47 + 16 * c1:48 + 16 * c1], A.add, A.is_equal, 32,
-               ["tw", "st11", "kc"], ["eqw%d" % (2 + c1)])
+        ts(T.st1[:, 0:32], zrow, kc, None, A.add, None, 32, ["tw", "kc"], ["st11"])
         join(2)
-        ts(T.zcol[:], T.st1[:, 47:64:16], kc, None, A.subtract, None, 2, ["st11", "kc"], ["zcol"])
-        scan(T.wsc[:, 68:136], T.cwave[:], T.eqw[:, 68:136], A.add, A.max, 68, ["cwave", "eqw2", "eqw3"], ["wsc1"])
         for c1 in range(2):
-            ts(T.woff[:, 4 * t + 2 + c1:4 * t + 3 + c1], T.wsc[:, 101 + 34 * c1:102 + 34 * c1], T.dum[:, c1:c1 + 1], T.zcol[:, c1:c1 + 1],
-               A.mult, A.max, 1, ["wsc1", "dum", "zcol"], ["woff%d" % (4 * t + 2 + c1)])
+            ts(T.eqw[:, 68 + 34 * c1 + 1:68 + 34 * c1 + 33], T.st1[:, 0:32], T.st1[:, 47 + 16 * c1:48 + 16 * c1], T.dum[:, c1:c1 + 1], A.is_equal, A.mult, 32,
+               ["st11", "dum"], ["eqw%d" % (2 + c1)])
+        ts(T.eqw[:, 101:136:34], T.st1[:, 47:64:16], kc, None, A.subtract, None, 2, ["st11", "kc"], ["eqw2"])
+        join(3)
+        for c1 in range(2):
+            scan(T.wo2[:, 68 * t + c1:68 * t + 68:2], nt(T.cwave, c1, 34), nt(T.eqw, 2 + c1, 34), A.add, A.max, 34, ["cwave", "eqw2", "eqw3"], ["woff2" + s])
         join(2)
         if redo:
             rest()
@@ -484,18 +497,21 @@ def build(g, T, topo, rank, cost):
         redirect(T.tw[:, 0:WD], "tw", t, 2)
         scan(T.asc[:], T.cfz[:], T.tw[:, t:W:16], A.add, A.max, L, ["cfz", "tw"], ["asc"])
         ts(nt(T.alist, t, 16), T.asc[:, 15:L:16], kc, None, A.subtract, None, 16, ["asc", "kc"], ["alist" + s])
+        kt = T.kct[:, t:t + 1]
         for h in range(2):
-            ts(nt(T.ub, h, 32), T.tw[:, 16 * (3 + h) + t:W:128], float(-t), None, A.add, None, 32, ["tw"], ["ub%d" % h])
+            scan(nt(T.bsc, h, 32), T.cfz[:, 0:32], T.tw[:, 16 * (3 + h) + t:W:128], A.add, A.max, 32, ["cfz", "tw"], ["bsc"])
         join(2)
-        scan(T.bsc[:], T.cfz[:, 0:64], T.ub[:], A.add, A.max, 64, ["cfz", "ub0", "ub1"], ["bsc"])
+        for h in range(2):
+            ts(nt(T.ub, h, 32), T.tw[:, 16 * (3 + h) + t:W:128], -2048.0 - t, None, A.add, None, 32, ["tw"], ["ub"])
+        join(2)
+        mm([(B1[:, 0:64], T.eye[:], T.ub[:], True, False, 64)], ["eye", "ub"], ["B1lo"], ["B1"])
         for c in range(4):
-            ts(nt(T.at1, c, 64), T.idrow[:], kc, T.bsc[:, 16 * c + 15:16 * c + 16], A.add, A.is_equal, 64, ["idrow", "kc", "bsc"], ["at1%d" % c])
+            ts(nt(T.at1, c, 64), T.idrow[:], kt, T.bsc[:, 16 * c + 15:16 * c + 16], A.add, A.is_equal, 64, ["idrow", "kct", "bsc"], ["at1%d" % c])
         join(4)
-        ts(T.ucol[:], T.bsc[:, 15:64:16], kc, None, A.subtract, None, 4, ["bsc", "kc"], ["ucol"])
-        mm([(B1[:, 0:64], T.bo[:], nt(T.at1, c, 64), c == 0, c == 3, 64) for c in range(4)], ["bo", "at10"], ["B1lo"], ["B1"])
-        tt(T.tm[:], T.ub[:], B1[:, 0:64], A.add, 64, ["ub0", "ub1", "B1lo"], ["tm"], ["B1"])
+        ts(T.ucol[:], T.bsc[:, 15:64:16], kt, None, A.subtract, None, 4, ["bsc", "kct"], ["ucol"])
+        mm([(B1[:, 0:64], T.bo[:], nt(T.at1, c, 64), False, c == 3, 64) for c in range(4)], ["bo", "at10"], ["B1lo"], ["B1"])
         for c in range(4):
-            ts(nt(T.a2, c, 64), T.tm[:], T.idcol[:, c:c + 1], None, A.is_equal, None, 64, ["tm", "idcol"], ["a2%d" % c])
+            ts(nt(T.a2, c, 64), B1[:, 0:64], T.idcol[:, c:c + 1], None, A.is_equal, None, 64, ["B1lo", "idcol"], ["a2%d" % c], ["B1"])
         join(4)
         scan(T.b2[:], T.rst[:], T.a2[:], A.mult, A.max, L, ["rst"] + ["a2%d" % c for c in range(4)], ["b2"])
         d = 1 + t % 3
@@ -544,21 +560,26 @@ def build(g, T, topo, rank, cost):
         d = 1 + t % 3
         rep, rk, aqw, ak = T["rep%d" % d][:, 0:W], "rep%d" % d, T["aqr%d" % d][:, 0:W], "aqr%d" % d
         xv, al = nt(T.xvc, t), nt(T.alist, t, 16)
-        gat("V", T.alu[:], aqw, al, L, [ak, "aqr1b", "alist" + s], ["alu"], False)
-        gathers("v", T.far, rep, rk, T.alu, lambda a, b: ["alu"], spans(CFG["vg"][t]))
+        H = CFG["halves"]
+        hw = L // H
+        for h in range(H):
+            gat("V", nt(T.alu, h, hw), aqw, nt(al, h, hw // 16), hw, [ak, "aqr1b", "alist" + s], ["alu%d" % x for x in range(h * 2 // H, (h + 1) * 2 // H)], False)
+        gathers("v", T.far, rep, rk, T.alu, lambda a, b: ["alu%d" % x for x in range(a // 128, (b - 1) // 128 + 1)], spans(CFG["vg"][t]))
         later = []
         for a in range(0, L, 64):
             scores("v", T.far, T.mv, a, a + 64, "A", xv, "xvc" + s, [(r, T.B6[:, a:a + 64], a + r, a + 64, 16, 64) for r in range(16)],
-                   "B6lo", "B6", a == 0, a + 64 == L, ("B4", "B5"), t - 1, later if t in CFG["late"] else None)
+                   "B6lo", "B6", a == 0, a + 64 == L, [CFG["vb"][(a // 32 + x) % len(CFG["vb"])] for x in range(2)], t - 1, later if t in CFG["late"] else None)
         if t == 0:
-            ts(T.alh[:], T.alu[:], -2048.0, None, A.add, None, 128, ["alu"], ["alh"])
+            ts(T.alh[:], T.alu[:], -2048.0, None, A.add, None, 128, ["alu0", "alu1"], ["alh0", "alh1"])
         else:
             renew(t - 1, [d])
-            ts(T.alh[:], aqw.indirect(al), -2048.0, None, A.add, None, 60 + GA * L, [ak, "alist" + s], ["alh"])
+            for h in range(H):
+                ts(nt(T.alh, h, hw), aqw.indirect(nt(al, h, hw // 16)), -2048.0, None, A.add, None, 60 + GA * hw, [ak, "alist" + s],
+                   ["alh%d" % x for x in range(h * 2 // H, (h + 1) * 2 // H)])
             o = 144 * (t - 1) + 15
             mm([(T.B7[:, L:L + 16], T.boh[:], T.c128[:, 0:16], True, False, 16)]
                + [(T.B7[:, L:L + 16], T.bok[:, o - r:o + 128 - r], T.alh[:, r:L:16], False, r == 15, 16) for r in range(16)],
-               ["bok%d" % (t - 1), "alh", "boh", "c128"], ["B7hi"], ["B7"], 17)
+               ["bok%d" % (t - 1), "alh0", "alh1", "boh", "c128"], ["B7hi"], ["B7"], 17)
             cp(T.plist[:], T.B7[:, L:L + 16], 16, ["B7hi"], ["plist"], ["B7"])
             gat("S", T.farp[:], rep, T.plist[:], L, [rk, "plist"], ["farp"])
             mm([(T.B7[:, 0:L], T.eye[:], T.farp[:], True, False, L), (T.B7[:, 0:L], T.neye[:], xv, False, True, L)],
@@ -571,12 +592,14 @@ def build(g, T, topo, rank, cost):
                 ac(T.mvp[:], T.B7[:, 0:L], AF.Abs, L, ["B7lo"], ["mvp"], ["B7"], False)
                 mm([(T.B6[:, t - 1:L:16], Z(T.z16, r), T.mvp[:, r:L:16], r == 0, r == 15, 16) for r in range(16)], ["z16", "mvp"], ["B6lo"], ["B6"], 16)
         scan(T.vsc[:], T.cmin[:], T.B6[:, 0:L], A.add, A.min, L, ["cmin", "B6lo"], ["vsc"], ["B6"])
-        cp(T.vi[:], T.vsc[:, 15:L:16], 16, ["vsc"], ["vi"])
-        ts(T.vj[:], T.vi[:], 15, None, A.bitwise_and, None, 16, ["vi"], ["vj"])
+        ts(T.vj[:], T.vsc[:, 15:L:16], 15, None, A.bitwise_and, None, 16, ["vsc"], ["vj"])
         cp(T.vu[:], T.vj[:], 16, ["vj"], ["vu"])
         mm([(T.B6[:, L:2 * L], Z(T.zh, t), nt(T.nown, t), True, False, L)], ["zh", "nown" + s], ["B6hi"], ["B6"])
-        tt(T.selv[:], T.oh[:, 32:48].indirect(T.vu[:]), T.alh[:], A.mult, 60 + GA * L, ["vu", "oh2", "alh"], ["selv"])
-        mm([(T.B6[:, L:2 * L], Z(T.zh, t), T.selv[:], False, True, L)], ["zh", "selv"], ["B6hi"], ["B6"])
+        G = H if t < RO - 1 else 1
+        for h in range(G):
+            tt(nt(T.selv, h, L // G), T.oh[:, 32:48].indirect(nt(T.vu, h, 16 // G)), nt(T.alh, h, L // G), A.mult, 60 + GA * L // G,
+               ["vu", "oh2", "alh0", "alh1"], ["selv%d" % x for x in range(h * 2 // G, (h + 1) * 2 // G)])
+        mm([(T.B6[:, L:2 * L], Z(T.zh, t), T.selv[:], False, True, L)], ["zh", "selv0", "selv1"], ["B6hi"], ["B6"])
         tt(T.B7[:, L:2 * L], T.B6[:, L:2 * L], nt(T.free, t), A.mult, L, ["B6hi", "free" + s], ["B7hi"], ["B6", "B7"])
         tt(nt(T.ymc, t), T.aqs[:, t:W:16], T.B7[:, L:2 * L], A.add, L, AQ + ["B7hi"], ["ymc" + s] + TMP, ["B7"])
         ks = [k for k, (tu, du) in enumerate(UPD) if tu == t]
@@ -604,15 +627,16 @@ def build(g, T, topo, rank, cost):
             gat("S", nt(T.urow, t, 64), st, T.ulist[:, 10 * t:10 * t + 4], 64, ["stab", "ulist%d" % t], ["urow%d" % t])
         n8 = len(CFG["yg"])
         w = L // n8
+        gcp(nt(T.vall, RO - 1), T.tw[:, RO - 1:W:16], L, ["tw"], ["vall%d" % (RO - 1), "tw"])
         for n in range(n8):
-            gat(CFG["yg"][n], T.yy[:, 16 * w * n:16 * w * (n + 1)], st, T.tgu[:, w * n:w * (n + 1)], 16 * w, ["stab", "tgu"], ["yy%d" % x for x in range(n * 8 // n8, (n + 1) * 8 // n8)])
+            gat(CFG["yg"][n], T.tw[:, 16 * w * n:16 * w * (n + 1)], st, T.tgu[:, w * n:w * (n + 1)], 16 * w, ["stab", "tgu", "tw"], ["yy%d" % n])
         for t in range(RO):
-            redirect(T.yy[:, 0:WD], "yy", t, 1, ["yy%d" % n for n in range(9)] if t == 0 else [])
-            redirect(T.yy[:, 0:WD], "yy", t, 2)
-            o, a, key = (T.yy[:, t:W:16], nt(T.vall, t), "vall%d" % t) if t < RO - 1 else (T.yy[:, t:W:16], T.tw[:, t:W:16], "tw")
-            cp(o, a, L, [key], ["yy"])
+            redirect(T.tw[:, 0:WD], "yy", t, 1, ["yy%d" % n for n in range(n8)] if t == 0 else [])
+            redirect(T.tw[:, 0:WD], "yy", t, 2)
+            o, a = T.tw[:, t:W:16], nt(T.vall, t)
+            cp(o, a, L, ["vall%d" % t], ["yy"])
             ops[-1]["alt"] = {"V": (ops[-1]["f"], L), "S": ([lambda o=o, a=a: S.activation(o, a, AF.Copy)], L)}
-        dma(T.yt[:, :], T.yy[0:128:16, 0:W], "outs", ["yy"], [], 0.2)
+        dma(T.yt[:, :], T.tw[0:128:16, 0:W], "outs", ["yy"], [], 0.2)
 
     for t in range(RO):
         phase[0] = "n"
@@ -630,22 +654,22 @@ def depend(ops):
     for i, o in enumerate(ops):
         dep = {}
 
-        def add(j, how, key=None):
+        def add(j, how, key=None, reads=True):
             if key in ("ld", "rs", "hs"):
                 dep.setdefault((j, "o", None), False)
             elif how == "w" and ops[j]["k"] == "r":
                 dep[(j, how, ops[j]["W"].index(key))] = True
             else:
-                dep[(j, how, 0)] = not (o["e"] == "P" and ops[j]["e"] == "P")
+                dep[(j, "w" if ops[j]["k"] == "c" else how, 0)] = not (o["e"] == "P" and ops[j]["e"] == "P")
         for k in o["R"]:
             if k in last:
                 add(last[k], "w", k)
         for k in o["W"]:
             if k in last:
-                add(last[k], "w", k)
+                add(last[k], "w", k, False)
             for j in readers.get(k, []):
                 if j != i:
-                    add(j, "r", k)
+                    add(j, "r", k, False)
         for b in o["b"]:
             eng, cur, prev = epoch.get(b, (None, [], []))
             if eng == o["e"]:
@@ -663,51 +687,68 @@ def depend(ops):
         o["dep"] = [(j, how, n, wt) for (j, how, n), wt in dep.items()]
 
 
-def place(eng, dur, pred, prio, first=None):
-    n = len(eng)
-    p = list(prio)
-    for i in (range(n) if first is None else range(n - 1, -1, -1)):
+def place(eng, dur, pred, tail, p, order, k0, base):
+    rest = sorted(order[k0:])
+    for i in rest:
         for j, lt, dm in pred[i]:
             if p[j] >= p[i]:
                 p[i] = p[j] + 0.001
-    lo = {e: [] for e in "VSPGYH"}
-    hi = {e: [] for e in "VSPGYH"}
-    start = [0.0] * n
-    for i in sorted(range(n), key=lambda k: p[k]):
-        t = 0.0 if first is None else first[i]
+    fin, done = (list(base[2]), list(base[4])) if k0 else ([0.0] * len(eng), [0.0] * len(eng))
+    lo = {e: [-1.0] for e in "VSPGYH"}
+    hi = {e: [0.0] for e in "VSPGYH"}
+    for i in order[:k0]:
+        hi[eng[i]][0] = fin[i]
+    start, tol = {}, CFG["tol"]
+    rest.sort(key=lambda k: p[k])
+    for i in rest:
+        t = 0.0
         for j, lt, dm in pred[i]:
-            x = start[j] + dur[j] + lt + dm
+            x = (done[j] if dm else fin[j]) + lt
             if x > t:
                 t = x
         a, b, d = lo[eng[i]], hi[eng[i]], dur[i]
-        k = len(a)
-        while k > 0 and b[k - 1] > t:
+        k = n = len(a)
+        while k > 1 and b[k - 1] > t:
             k -= 1
-        while k < len(a) and a[k] < t + d:
-            t = max(t, b[k])
+        if b[k - 1] > t:
+            t = b[k - 1]
+        while k < n and a[k] < t + d - tol:
+            if b[k] > t:
+                t = b[k]
             k += 1
         a.insert(k, t)
         b.insert(k, t + d)
         start[i] = t
-    return start
+        fin[i] = t + d
+        done[i] = t + d + tail[i]
+    rest.sort(key=lambda k: start[k])
+    return order[:k0] + rest
 
 
-def replay(eng, dur, pred, move, lat, order):
+def replay(eng, dur, pred, move, lat, order, k0=0, base=None):
     n = len(eng)
-    fin, done, why, free, last = [0.0] * n, [0.0] * n, [None] * n, {e: 0.0 for e in "VSPGYH"}, {e: None for e in "VSPGYH"}
-    busy = {True: 0.0, False: 0.0}
-    for i in order:
-        t, w = free[eng[i]], (last[eng[i]], True)
+    fin, done, why = (list(base[2]), list(base[4]), list(base[1])) if k0 else ([0.0] * n, [0.0] * n, [None] * n)
+    free, last, busy = {e: 0.0 for e in "VSPGYH"}, {e: None for e in "VSPGYH"}, {True: 0.0, False: 0.0}
+    for i in order[:k0]:
+        last[eng[i]] = i
+        if move[i]:
+            busy[eng[i] == "H"] = done[i]
+    for e in last:
+        if last[e] is not None:
+            free[e] = fin[last[e]]
+    for i in order[k0:]:
+        e = eng[i]
+        t, w = free[e], (last[e], True)
         for j, lt, dm in pred[i]:
             x = (done[j] if dm else fin[j]) + lt
             if x >= t:
                 t, w = x, (j, False)
-        fin[i] = done[i] = free[eng[i]] = t + dur[i]
+        fin[i] = done[i] = free[e] = t + dur[i]
         if move[i]:
-            busy[eng[i] == "H"] = done[i] = max(fin[i] + lat, busy[eng[i] == "H"]) + move[i]
-        why[i], last[eng[i]] = w, i
-    i = max(range(n), key=lambda k: done[k])
-    return done[i], why, fin, i
+            busy[e == "H"] = done[i] = max(fin[i] + lat, busy[e == "H"]) + move[i]
+        why[i], last[e] = w, i
+    end = max(done)
+    return end, why, fin, done.index(end), done
 
 
 def neighbours(why, i):
@@ -756,23 +797,6 @@ def schedule(sets):
     group = np.array(group)
     rs = np.random.RandomState(CFG["seed"])
 
-    loose = [i for i, o in enumerate(ops) if "alt" in o]
-    marks = [i for i, o in enumerate(ops) if o["e"] == "V" and o["W"][0][:-1] in ("x", "alist", "ymc")]
-
-    def critical(res):
-        x = res[rs.randint(len(res))]
-        return neighbours(x[1], x[3] if rs.randint(2) else marks[rs.randint(len(marks))]) or neighbours(res[0][1], res[0][3])
-
-    def score(prio, eng, bound=1e18, order=None):
-        if order is None:
-            st = place(eng, durs[0], preds[0], prio)
-            order = sorted(range(n), key=lambda k: (st[k], k))
-        res = [replay(eng, durs[0], preds[0], moves[0], COSTS[0][5], order)]
-        if res[0][0] > bound:
-            return None
-        res += [replay(eng, durs[m], preds[m], moves[m], COSTS[m][5], order) for m in range(1, len(sets))]
-        return sum(x[0] + CFG["pull"] * sum(x[2][k] for k in marks) for x in res) / len(res), np.array(res[0][2]) - d0, order, res, eng
-
     def shift(order, a, b, ahead):
         i, j = order.index(a), order.index(b)
         mid = order[i:j + 1]
@@ -780,60 +804,93 @@ def schedule(sets):
         mask = (anc[x] if ahead else des[x]) | 1 << x
         took, left = [k for k in mid if mask >> k & 1], [k for k in mid if not mask >> k & 1]
         return order[:i] + (took + left if ahead else left + took) + order[j + 1:]
-    d0 = np.array(durs[0])
-    top = best = min((score([-(level[i] + (0.0 if ops[i]["bulk"] else x) + (y if ops[i]["ph"] == "n" else 0.0)) for i in range(n)], eng)
-                      for x in CFG["bonus"] for y in CFG["lead"]), key=lambda z: z[0])
-    succ = [[] for i in range(n)]
-    for i in range(n):
-        for j, lt, dm in preds[0][i]:
-            succ[j].append((i, lt, dm))
-    for it in range(CFG["tries"]):
-        p, eng, order = best[1].copy(), best[4], None
-        if rs.uniform() < CFG["near"]:
-            pairs = critical(best[3])
-            a, b = pairs[rs.randint(len(pairs))]
-            if rs.randint(3) == 0:
-                same = [k for k in best[2] if eng[k] == eng[a]]
-                x = same.index(a)
+
+    def search(m, aims, start, eng, since, tries):
+        d0, grp = np.array(durs[0][:m]), group[:m]
+
+        def value(x):
+            return sum(w * (x[0] if k is None else x[2][k]) for k, w in aims)
+
+        def score(p, eng, bound=1e18, order=None, old=None):
+            k0 = 0
+            if old is not None:
+                if order is None:
+                    ch = np.nonzero(p != old[1])[0]
+                    first = min([p[ch].min(), old[1][ch].min()] if len(ch) else [1e18])
+                    if eng is not old[4]:
+                        first = min([first] + [p[x] - 2000.0 for x in range(m) if eng[x] != old[4][x]])
+                    k0 = int(np.searchsorted(old[1][old[2]], first - 300.0))
+                elif eng is old[4]:
+                    while k0 < m and order[k0] == old[2][k0]:
+                        k0 += 1
+            if order is None:
+                order = place(eng, durs[0], preds[0], tail, list(p), old[2] if old else list(range(m)), k0, old[3][0] if old else None)
+            res = [replay(eng, durs[0], preds[0], moves[0], COSTS[0][5], order, k0, old[3][0] if old else None)]
+            if value(res[0]) > bound:
+                return None
+            res += [replay(eng, durs[c], preds[c], moves[c], COSTS[c][5], order, k0, old[3][c] if old else None) for c in range(1, len(sets))]
+            st = np.array(res[0][2]) - d0
+            return sum(value(x) for x in res) / len(res), st, sorted(order, key=lambda k: st[k]), res, eng
+
+        def critical(res, p):
+            x, k = res[rs.randint(len(res))], aims[0 if rs.randint(3) else rs.randint(len(aims))][0]
+            return [ab for ab in neighbours(x[1], x[3] if k is None else k) if p[ab[1]] >= since]
+        top = best = min((score(x, eng[:m]) for x in start), key=lambda z: z[0])
+        for it in range(tries):
+            p, eng, order = best[1].copy(), best[4], None
+            pairs = critical(best[3], p)
+            kind = rs.randint(16) if pairs else 15
+            if pairs:
+                a, b = pairs[rs.randint(len(pairs))]
+            if kind < 3:
+                order = shift(best[2], a, b, rs.randint(2))
+            elif kind < 5:
+                eng = list(eng)
+                loose = [x for x in range(m) if "alt" in ops[x] and p[x] >= since]
+                on = [x for ab in pairs for x in ab if "alt" in ops[x]]
+                a = on[rs.randint(len(on))] if on and rs.randint(2) else loose[rs.randint(len(loose))]
+                near = [x for x in loose if eng[x] != eng[a] and abs(p[x] - p[a]) < 2500]
+                for x in [a] + ([near[rs.randint(len(near))]] if near and rs.randint(2) else []):
+                    eng[x] = "S" if eng[x] == "V" else "V"
                 if rs.randint(2):
-                    a = same[max(0, x - rs.randint(1, 5))]
-                else:
-                    b = same[min(len(same) - 1, x + 1 + rs.randint(1, 5))]
-            order = shift(best[2], a, b, rs.randint(2))
-        elif it < 12 or it % CFG["turn"] == 0:
-            p = -np.array(place(eng, durs[0], succ, (-p - d0 + rs.normal(size=n) * rs.choice([0.0, 30.0, 100.0])).tolist(), tail)) - d0
-        elif it % 8 == 3:
-            eng = list(eng)
-            pairs = [x for ab in critical(best[3]) for x in ab if "alt" in ops[x]]
-            a = pairs[rs.randint(len(pairs))] if pairs and rs.randint(2) else loose[rs.randint(len(loose))]
-            near = [x for x in loose if eng[x] != eng[a] and abs(p[x] - p[a]) < 2500]
-            for x in [a] + ([near[rs.randint(len(near))]] if near and rs.randint(2) else []):
-                eng[x] = "S" if eng[x] == "V" else "V"
-            if rs.randint(2):
-                order = sorted(best[2], key=lambda k: p[k])
-        elif it % 4:
-            pairs = critical(best[3])
-            a, b = pairs[rs.randint(len(pairs))]
-            kind = rs.randint(4)
-            if kind == 0:
+                    order = sorted(best[2], key=lambda k: p[k])
+            elif kind < 8:
                 p[b] = p[a] - 1.0
-            elif kind == 1:
-                p[a] = p[b] + 1.0
-            elif kind == 2:
-                p[group == group[b]] -= p[b] - p[group == group[a]].min() + 1.0
+            elif kind < 10:
+                p[a] = p[b] + 1.0 + rs.choice([0.0, 300.0, 1500.0])
+            elif kind < 12:
+                p[grp == grp[b]] -= p[b] - p[grp == grp[a]].min() + 1.0
+            elif kind < 13:
+                p[grp == grp[a]] += p[grp == grp[b]].max() - p[a] + 1.0
             else:
-                p[group == group[a]] += p[group == group[b]].max() - p[a] + 1.0
-        else:
-            near = np.unique(group[np.abs(p - rs.uniform(6000, p.max())) < 3000])
-            if len(near) == 0:
-                continue
-            for x in rs.choice(near, rs.randint(1, 4)):
-                p[group == x] += rs.normal() * rs.choice([300.0, 1200.0, 4000.0])
-        cand = score(p.tolist(), eng, best[3][0][0] + 300.0, order)
-        if cand is not None and cand[0] <= best[0] + CFG["temp"] * (1.0 - it / CFG["tries"]) * rs.exponential():
-            best = cand
-        if best[0] < top[0]:
-            top = best
+                near = np.unique(grp[np.abs(p - rs.uniform(since, p.max())) < 3000])
+                if len(near) == 0:
+                    continue
+                for x in rs.choice(near, rs.randint(1, 4)):
+                    p[grp == x] += rs.normal() * rs.choice([300.0, 1200.0, 4000.0])
+            cand = score(p, eng, value(best[3][0]) + 300.0, order, best)
+            if cand is not None and cand[0] <= best[0] + CFG["temp"] * (1.0 - it / tries) * rs.exponential():
+                best = cand
+            if best[0] < top[0]:
+                top = best
+        return top
+    ends = [i for i, o in enumerate(ops) if o["e"] == "V" and o["W"][0] == "xA"]
+    seen = [i for i, o in enumerate(ops) if o["e"] == "V" and o["W"][0][:-1] == "ymc"]
+    cuts = [i for i in range(1, n) if ops[i]["ph"] == "v" and ops[i - 1]["ph"] == "n"] + [n, n]
+    top, done, since = None, 0, 0.0
+    for s, m in enumerate(cuts):
+        aims = [(ends[s], 1.0)] + ([(seen[s - 1], CFG["pull"])] if s else []) if s < len(ends) else [(None, 1.0)]
+        old = [] if top is None else top[1].tolist()
+        base = 0.0 if top is None else old[ends[min(s, len(ends)) - 1]] + level[ends[min(s, len(ends)) - 1]]
+        start = [old + [base - (level[i] + (0.0 if ops[i]["bulk"] else x) + (y if ops[i]["ph"] == "n" else 0.0)
+                                - (z if ops[i]["ph"] != "n" and eng[i] == "V" else 0.0)) for i in range(done, m)]
+                 for x in CFG["bonus"] for y in CFG["lead"] for z in CFG["fill"]] if m > done else [old]
+        k = CFG["starts"] if m > done else 1
+        top = min((search(m, aims, start[x::k], (list(top[4]) if top else []) + eng[done:], since if m > done else 0.0,
+                          int(CFG["tries"] * CFG["share"][s] / k)) for x in range(k)), key=lambda z: z[0])
+        done = m
+        if s < len(ends):
+            since = top[1][ends[s]] - 8000.0
     for i in range(n):
         ops[i]["t"] = top[3][0][2][i] - durs[0][i]
     return top[2], [x[0] for x in top[3]], top[4]

import numpy as np
from concourse.bass import DstId, RemoteDMATransfer
from concourse.mybir import AluOpType, ActivationFunctionType

W, L, RO, N = 4096, 256, 4, 4
WD = W + 256
KF = 8192.0
MAGIC = 12582912.0

F32, BF, F16, I32, U16 = "float32", "bfloat16", "float16", "int32", "uint16"
SB = {
    BF: {"xA": W, "rep1": W, "rep2": W, "rep3": W, "near": W, "far": W, "reps": 448 * 16, "xvc": RO * L, "xvq": 3 * L, "nxc": RO * L, "updin": 6 * L, "at1": L,
         "a2": L, "at3": 4 * L, "idrow": 64, "lanerow": L, "farp": L, "mvp": L, "xa": L, "mh": L, "free": RO * L, "hey": 128, "nhey": 128,
         "half": L, "z32": 144, "zm16": 144, "z16": 144, "eye": 128, "neye": 128, "bo": 128, "oh": 48, "rst": L},
    F16: {"ownh": RO * L, "nown": RO * L, "ub": 64, "alh": L, "selv": L, "zh": 144, "boh": 128, "bok": 432, "c128": 144, "eqd": 264,
          "cvoid": 264, "nsc": 264},
    I32: {"aqs": W, "aqr1": W, "aqr2": W, "aqr3": W, "tgs": L, "ksc": L, "vsc": L, "kj": 16, "vj": 16, "pi": 2, "ri": 2},
    U16: {"tgu": L, "ownj": L, "ownu": RO * L, "alist": RO * 16, "alu": L, "plist": 16, "ku": 16, "vu": 16, "ulist": RO * 10, "tlist": 16, "soff": RO * 4,
          "wo1": RO * 34, "wo2": RO * 68, "zlist": 4, "repl": 448, "prm": RO * 16, "prr": RO * 16},
    F32: {"stab": WD, "tw": WD, "ymc": RO * L, "ymin": 6 * L, "rowpo": 96, "st1": 64, "zcol": 2, "asc": L,
          "bsc": 64, "ucol": 4, "kct": 4, "swp": 64, "vall": RO * L, "nrow": L, "urow": RO * 64, "zr1": 34, "cw1": 17, "b2": L, "kcm": 4,
          "cwave": 68, "eqw": 136, "wsc": 136, "col": 16, "idf": 4, "idcol": 4, "dum": 2, "nrm": 8, "cfz": L, "cmax": L, "cmin": L},
}
SCRATCH = {k: ("sbuf", [128, n], d) for d in SB for k, n in SB[d].items()}
SCRATCH.update({k: ("sbuf", [128, L, 16], BF) for k in ("mc", "mv")})
SCRATCH["nbo"] = ("sbuf", [128, 128], BF)
SCRATCH["sel"] = ("sbuf", [128, 2, L], F16)
SCRATCH.update({"B%d" % b: ("psum", [128, 512], F32) for b in range(8)})
UPD = [(0, 2), (0, 3), (0, 1), (1, 3), (1, 1), (2, 1)]
PIECES = 8
SEMAPHORES = (["eV", "eS", "eP", "eG", "ldx", "ldt", "outs", "lsm"] + ["ldq%d" % p for p in range(PIECES)]
              + ["lx1", "lx2", "lq1", "rx1", "rx2", "rx3", "rq0", "rq1", "rq2", "rq3", "hq0", "hq1", "hl"] + ["u%s%d" % (a, k) for a in "xq" for k in range(len(UPD))])
COSTS = [(1.56, 3.8, 0.5, 250.0, 3000.0, 2200.0, 1.0), (1.25, 2.5, 0.5, 220.0, 4200.0, 2800.0, 1.1), (1.8, 5.0, 0.5, 280.0, 3300.0, 2500.0, 1.3)]
CFG = {
    "cg": ["S32 S32 V32 S32 V32 S32 V32 S16 V16", ] + ["F48 F48 S32 S32 S32 S32 S32"] * 3,
    "cn": ["M64 A64 M64 M64"] + ["R48 R48 M64 M96"] * 3,
    "parts": "P96 P64 P96", "clamp": 1, "split": 0, "per": 8, "late": [1, 2],
    "vg": ["S32 " * 8] * 3 + ["V64 S64 V64 V64"],
    "yg": "SVSVSVSV", "xa": "S", "free": "V", "redo": 1, "reset": "V", "lists": "G", "renew": "GGGGGG",
    "bonus": [0.0, 700.0, 1500.0, 3000.0], "lead": [0.0, 1000.0, 2000.0, 4000.0, 8000.0, 16000.0], "tries": 30000, "seed": 5, "temp": 50.0, "pull": 0.6, "tol": 60.0, "halves": 1, "inorder": 1, "mg": 2, "share": [0.2, 0.2, 0.2, 0.3, 0.1], "starts": 3, "fill": [0.0], "vb": ["B4", "B5", "B3"],
}
FIRST = 96


def spans(word):
    out, a = [], 0
    for w in word.split():
        out.append((a, a + int(w[1:]), w[0]))
        a = out[-1][1]
    return out


A = AluOpType
AF = ActivationFunctionType


def helpers(T, topo):
    out = []
    for c in T.cores:
        out.append([x for x in topo.cores_of(c) if x not in T.cores and x not in out and topo.die(x) == topo.die(c)][0])
    return out


def build(g, T, topo, rank, cost):
    ops, phase = [], ["s"]
    V, S, P = g.vector, g.scalar, g.tensor
    core, helper = T.cores[rank], helpers(T, topo)[rank]
    GA, SCA, PE = cost[:3]

    def op(eng, fns, dur, R, Wr, banks=(), kind="c", sem=None, lsem=None, cnt=0, mib=0.0, hint=0.0, bulk=False):
        ops.append(dict(e=eng, f=fns, d=float(dur), R=list(R), W=list(Wr), b=list(banks), k=kind, sem=sem, lsem=lsem,
                        cnt=cnt, mib=mib, hint=hint, bulk=bulk, ph=phase[0]))

    def join(k):
        last = ops[-k:]
        del ops[-k:]
        op(last[0]["e"], [f for o in last for f in o["f"]], sum(o["d"] for o in last), sorted({x for o in last for x in o["R"]}),
           sorted({x for o in last for x in o["W"]}), last[0]["b"], bulk=last[0]["bulk"])

    def ts(out, in0, s1, s2, o0, o1, n, R, Wr, banks=(), bulk=False):
        if o1 is None:
            op("V", [lambda: V.tensor_scalar(out, in0, s1, None, o0)], max(64, n), R, Wr, banks, bulk=bulk)
        else:
            op("V", [lambda: V.tensor_scalar(out, in0, s1, s2, o0, o1)], max(64, n), R, Wr, banks, bulk=bulk)

    def fill(out, n, c, R, Wr):
        ts(out, T.nrow[:, 0:n], 0.0, c, A.mult, A.add, n, ["nrow"] + R, Wr)

    def put(out, n, c, key):
        op("V", [lambda: V.memset(out, c)], max(64, n), [], [key])

    def tt(out, a, b, o, n, R, Wr, banks=(), bulk=False):
        op("V", [lambda: V.tensor_tensor(out, a, b, o)], max(64, n), R, Wr, banks, bulk=bulk)

    def cp(out, a, n, R, Wr, banks=(), eng="V"):
        if eng == "V":
            op("V", [lambda: V.tensor_copy(out, a)], max(64, n), R, Wr, banks)
        else:
            ac(out, a, AF.Copy, n, R, Wr, banks, False)

    def ac(out, a, fn, n, R, Wr, banks=(), bulk=True):
        op("S", [lambda: S.activation(out, a, fn)], max(64, n), R, Wr, banks, bulk=bulk)

    def gcp(out, a, n, R, Wr):
        op("G", [lambda: g.affine_select(out, a, [[0, n]], A.is_gt, 0.0, 1, 0)], 205 + 2 * n, R, Wr)

    def scan(out, d0, d1, o0, o1, n, R, Wr, banks=()):
        op("V", [lambda: V.tensor_tensor_scan(out, d0, d1, 0.0, o0, o1)], max(64, n), R, Wr, banks)

    def mm(lst, R, Wr, banks, per=4, bulk=False):
        for i in range(0, len(lst), per):
            part = lst[i:i + per]
            op("P", [(lambda m=m: P.matmul(m[0], m[1], m[2], m[3], m[4])) for m in part], sum(max(64, m[5]) for m in part) * PE + 15,
               R, Wr, banks, bulk=bulk)

    def gat(eng, out, win, off, n, R, Wr, free=True):
        both = {"V": ([lambda: V.tensor_copy(out, win.indirect(off))], 60 + GA * n), "S": ([lambda: S.activation(out, win.indirect(off), AF.Copy)], 80 + GA * n)}
        op(eng, both[eng][0], both[eng][1], R, Wr, bulk=n > 256)
        if free:
            ops[-1]["alt"] = both

    def sca(win, off, a, n, R, Wr):
        op("V", [lambda: V.tensor_copy(win.indirect(off), a)], 60 + SCA * n, R, Wr)

    def iota(out, pat, base, cm, n, Wr, fl=True):
        if fl:
            op("G", [lambda: g.iota(out, pat, base, cm, allow_small_or_imprecise_dtypes=True)], 160 + 2 * n, [], Wr)
        else:
            op("G", [lambda: g.iota(out, pat, base, cm)], 160 + 2 * n, [], Wr)

    def dma(out, a, sem, R, Wr, mib, hint=0.0):
        op("Y", [lambda: g.sync.dma_start(out, a)], 100, R, Wr, kind="d", sem=[sem], cnt=16, mib=mib, hint=hint)

    def send(items, lsem, R, Wr, mib, hint=0.0, by="G"):
        trs, per = [], 0
        for i, (dist, out, a, sem) in enumerate(items):
            dst = helper if dist is None else T.cores[(rank - dist) % N]
            rid, pid, _ = topo.addr(dst)
            eng = topo.engines(core if by == "G" else helper, dst)
            per = len(eng) // (1 if len(items) == 1 else 2 if len(items) == 2 else 4)
            mask = sum(1 << e for e in eng[i * per:(i + 1) * per])
            trs.append((out, a, T.sem[sem], pid, rid, mask))
        if len(items) == 1:
            o, a, sm, pid, rid, mask = trs[0]
            fn = lambda: g.remote_dma(o, a, sm, T.sem[lsem], pid, rid, mask)
        else:
            fn = lambda: g.remote_dma_fused([RemoteDMATransfer(dst_ids=[DstId(rid=rid, pnc=pid)], dma_engine_mask=mask, remote_sem=sm, src=a, dst=o)
                                             for o, a, sm, pid, rid, mask in trs], local_sem=T.sem[lsem])
        op(by, [fn], 600, R, Wr, kind="r", sem=[x[3] for x in items], lsem=lsem, cnt=per, mib=mib, hint=hint)

    def nt(buf, t, w=L):
        return buf[:, t * w:(t + 1) * w]

    q = W // PIECES
    AQ = ["aq%d" % p for p in range(PIECES)]
    aqw = T.aqs[:, 0:W]
    dma(T.xA[:], T.x[:], "ldx", ["ld"], ["xA", "ld"], 1.0)
    for p in range(PIECES):
        dma(T.aqs[:, p * q:(p + 1) * q], T.aq[:, p * q:(p + 1) * q], "ldq%d" % p, ["ld"], [AQ[p], "ld"], 2.0 / PIECES, 2900 + 5900 * p / PIECES)
    dma(T.tgs[:], T.tg[:], "ldt", ["ld"], ["tgs", "ld"], 0.125, 9000)

    col = T.col
    rc, pc, gc15, gc0, r128, kc, r1, c15, cu, cv, t0, r4 = [col[:, i:i + 1] for i in range(12)]
    iota(T.pi[:], [[0, 2]], 0, 1, 2, ["pi"], False)
    iota(T.nrow[:], [[1, L]], 0, 0, L, ["nrow"])
    ina, g16, vw, inw = T.ymc[:, 0:264], T.ymc[:, 272:400], T.ymc[:, 400:464], T.ymc[:, 464:532]
    prow, psc, pf = T.vall[:, 0:L], T.vall[:, L:2 * L], T.vall[:, 2 * L:2 * L + 64]
    iota(g16, [[16, 8], [0, 16]], 0, 0, 128, ["g16"])
    iota(T.asc[:], [[-16, 2], [0, 4], [1, 32]], 0, 0, L, ["asc"])
    iota(vw, [[-16, 2], [1, 32]], 0, 0, 64, ["vw"])
    iota(T.lanerow[:], [[16, L]], 0, 0, L, ["lanerow"])
    parts = spans(CFG["parts"])
    for a, b, kind in parts:
        iota(prow[:, a:b], [[128, 16], [16, (b - a) // 32], [2048, 2]], a // 2, 0, b - a, ["prow%d" % a])
    iota(pf, [[1, 4], [16, 8], [2048, 2]], 0, 0, 64, ["pf"])
    iota(T.idrow[:], [[16, 2], [128, 32]], 48, 0, 64, ["idrow"])
    iota(T.idf[:], [[16, 2], [2048, 2]], 48 - 2048, 0, 4, ["idf"])
    for h in range(WD // L):
        op("S", [lambda h=h: S.activation(nt(T.stab, h), T.nrow[:], AF.Identity, bias=float(L * h))], L, ["nrow"], ["stab%d" % h])
    join(5)
    STAB0 = ["stab%d" % h for h in range(WD // L)]
    ts(T.ri[:], T.pi[:], 15, None, A.bitwise_and, None, 2, ["pi"], ["ri"])
    cp(rc, T.ri[:, 0:1], 1, ["ri"], ["rc"])
    cp(pc, T.pi[:, 0:1], 1, ["pi"], ["pc"])
    tt(gc0, pc, rc, A.subtract, 1, ["pc", "rc"], ["gc0"])
    ts(gc15, gc0, 15.0, None, A.add, None, 1, ["gc0"], ["gc15"])
    ts(r128, rc, 128.0, None, A.mult, None, 1, ["rc"], ["r128"])
    ts(T.idcol[:], T.idf[:], r128, None, A.add, None, 4, ["idf", "r128"], ["idcol"])
    ts(kc, rc, 15.0, KF, A.is_lt, A.mult, 1, ["rc"], ["kc"])
    ts(T.nrm[:, 0:4], T.nrow[:, 0:4], rc, None, A.is_equal, None, 4, ["nrow", "rc"], ["nrm"])
    ts(T.nrm[:, 4:8], T.nrow[:, 0:4], rc, -1.0, A.is_equal, A.mult, 4, ["nrow", "rc"], ["nrn"])
    ts(r1, rc, 1.0, None, A.add, None, 1, ["rc"], ["r1"])
    ts(c15, rc, -1.0, 15.0, A.mult, A.add, 1, ["rc"], ["c15"])
    ts(t0, rc, 0.0, -16.0, A.is_equal, A.mult, 1, ["rc"], ["t0"])
    ts(cu, c15, 1.0, t0, A.add, A.add, 1, ["c15", "t0"], ["cu"])
    ts(cv, rc, 15.0, r1, A.is_lt, A.mult, 1, ["rc", "r1"], ["cv"])
    ts(r4, rc, 4.0, W + 128.0, A.mult, A.add, 1, ["rc"], ["r4"])
    ts(T.dum[:], T.nrow[:, 0:128:64], r4, None, A.add, None, 2, ["nrow", "r4"], ["dum"])
    for i, (c, key) in enumerate(((c15, "c15"), (cu, "cu"), (cv, "cv"))):
        ts(T.oh[:, 16 * i:16 * i + 16], T.nrow[:, 0:16], c, None, A.is_equal, None, 16, ["nrow", key], ["oh%d" % i])
    ts(T.zh[:], T.nrow[:, 0:144], gc15, None, A.is_equal, None, 144, ["nrow", "gc15"], ["zh"])
    ts(T.eye[:], T.nrow[:, 0:128], pc, None, A.is_equal, None, 128, ["nrow", "pc"], ["eye"])
    for buf, sc, key in ((T.z32, 32.0, "z32"), (T.zm16, -16.0, "zm16"), (T.z16, 16.0, "z16")):
        ts(buf[:], T.zh[:], sc, None, A.mult, None, 72, ["zh"], [key])
    for buf, sc, key in ((T.neye, -1.0, "neye"), (T.hey, 0.5, "hey"), (T.nhey, -0.5, "nhey")):
        ts(buf[:], T.eye[:], sc, None, A.mult, None, 64, ["eye"], [key])
    put(T.half[:], 128, 0.5, "half")
    fill(T.c128[:], 144, 128.0, [], ["c128"])
    ts(T.bo[:], g16, gc0, KF, A.is_equal, A.mult, 128, ["g16", "gc0"], ["bo"])
    ts(T.boh[:], g16, gc0, None, A.is_equal, None, 128, ["g16", "gc0"], ["boh"])
    ts(T.prm[:], pf, r128, None, A.add, None, 64, ["pf", "r128"], ["prm"])
    ts(T.kcm[:], T.nrow[:, 0:4], kc, None, A.subtract, None, 4, ["nrow", "kc"], ["kcm"])
    ts(T.kct[:], T.nrow[:, 0:4], kc, None, A.add, None, 4, ["nrow", "kc"], ["kct"])
    if CFG["clamp"]:
        ts(T.nbo[:], g16, gc0, -KF, A.is_equal, A.mult, 128, ["g16", "gc0"], ["nbo"])
    for t in range(RO - 1):
        ts(nt(T.bok, t, 144), T.zh[:], T.nrm[:, t:t + 1], None, A.mult, None, 72, ["zh", "nrm"], ["bok%d" % t])
    for buf, sc, key in ((T.cmax, 1.0, "cmax"), (T.cmin, -1.0, "cmin")):
        put(buf[:], L, sc, key)
        put(buf[:, 0:L:16], 16, -1000000.0 * sc, key)
    ts(T.cfz[:, 0:16], T.nrow[:, 0:16], rc, -20000.0, A.is_equal, A.mult, 16, ["nrow", "rc"], ["cfz"])
    ts(T.cfz[:, 16:32], T.nrow[:, 0:16], r1, KF, A.is_equal, A.mult, 16, ["nrow", "r1"], ["cf2"])
    tt(T.cfz[:, 0:16], T.cfz[:, 0:16], T.cfz[:, 16:32], A.add, 32, ["cfz", "cf2"], ["cfz"])
    for w in (16, 32, 64, 128):
        cp(T.cfz[:, w:2 * w], T.cfz[:, 0:w], w, ["cfz"], ["cfz"])
    ts(T.cw1[:], T.nrow[:, 0:17], rc, -KF, A.is_equal, A.mult, 17, ["nrow", "rc"], ["cw1"])
    ts(T.zr1[:, 0:17], T.nrow[:, 0:17], r1, KF, A.is_equal, A.mult, 17, ["nrow", "r1"], ["zr1"])
    tt(T.cw1[:], T.cw1[:], T.zr1[:, 0:17], A.add, 34, ["cw1", "zr1"], ["cw1"])
    ts(T.cw1[:, 16:17], T.cw1[:, 16:17], -KF, None, A.add, None, 1, ["cw1"], ["cw1"])
    put(T.zr1[:], 34, 0.0, "zr1")
    put(T.rst[:], 128, 1.0, "rst")
    put(T.rst[:, 0:L:64], 4, 0.0, "rst")
    for c1 in range(2):
        a = 128 * c1 + 32
        ts(T.asc[:, a:a + 32], T.asc[:, a:a + 32], -1.0, None, A.add, None, 32, ["asc"], ["asc"])
    put(ina, 264, 0.0, "ina")
    for h in range(2):
        fill(nt(T.eqd, h, 132), 132, 0.0, [], ["eqd0", "eqd1", "eqd2", "eqd3"])
        ts(ina[:, 132 * h + 2:132 * h + 130], nt(T.asc, h, 128), rc, KF, A.is_ge, A.mult, 128, ["asc", "rc"], ["ina"])
    tt(T.cvoid[:, 1:264], ina[:, 1:264], ina[:, 0:263], A.subtract, 528, ["ina"], ["cvoid"])
    fill(T.cvoid[:, 0:264:132], 2, -30000.0, ["cvoid"], ["cvoid"])
    fill(T.cvoid[:, 131:264:132], 2, -128.0, ["cvoid"], ["cvoid"])
    put(inw, 68, 0.0, "inw")
    fill(T.eqw[:], 136, 0.0, [], ["eqw0", "eqw1", "eqw2", "eqw3"])
    for h in range(2):
        ts(inw[:, 34 * h + 1:34 * h + 33], nt(vw, h, 32), rc, KF, A.is_ge, A.mult, 32, ["vw", "rc"], ["inw"])
    tt(T.cwave[:, 1:68], inw[:, 1:68], inw[:, 0:67], A.subtract, 136, ["inw"], ["cwave"])
    fill(T.cwave[:, 0:68:34], 2, -30000.0, ["cwave"], ["cwave"])
    scan(psc, T.cfz[:], prow, A.add, A.max, L, ["cfz"] + ["prow%d" % a for a, b, kind in parts], ["psc"])
    for t in range(1, RO):
        ts(nt(T.prr, t, 16), psc[:, 15:L:16], T.kcm[:, t:t + 1], None, A.add, None, 16, ["psc", "kcm"], ["prr%d" % t])
    TMP = ["ina", "g16", "vw", "inw", "psc", "pf"] + ["prow%d" % a for a, b, kind in parts]

    def Z(buf, r):
        return buf[:, 15 - r:143 - r]

    lo, hi = nt(T.aqs, 0, W // 2), nt(T.aqs, 1, W // 2)
    send([(None, lo, lo, "hq0")], "lq1", AQ[:PIECES * 3 // 4] + ["rs"], ["hq0", "rs"], 1.0)
    send([(1, T.rep1[:], T.xA[:], "rx1")], "lx1", ["xA", "rs"], ["rep1", "rs"], 1.0, 2400)
    send([(1, nt(T.aqr1, 1, W // 2), hi, "rq1")], "lq1", AQ + ["rs"], ["aqr1b", "rs"], 1.0, 4800)
    send([(None, hi, hi, "hq1")], "lq1", AQ + ["rs"], ["hq1", "rs"], 1.0, 7200)
    send([(1, T.rep2[:], T.rep1[:], "rx2")], "lx2", ["rep1", "rs"], ["rep2", "rs"], 1.0, 5400)
    send([(1, nt(T.aqr1, 0, W // 2), lo, "rq0")], "hl", ["hq0", "hs"], ["aqr1", "hs"], 1.0, by="H")
    send([(2, T.aqr2[:], T.aqs[:], "rq2")], "hl", ["hq0", "hq1", "hs"], ["aqr2", "hs"], 2.0, by="H")
    send([(3, T.aqr3[:], T.aqs[:], "rq3")], "hl", ["hq0", "hq1", "hs"], ["aqr3", "hs"], 2.0, 5400, by="H")
    for t in range(RO):
        if t == 0:
            for p in range(PIECES):
                cp(T.ownu[:, p * q // 16:(p + 1) * q // 16], T.aqs[:, p * q:(p + 1) * q:16], q // 16, [AQ[p]], ["ownu0_%d" % p])
            cp(nt(T.xvc, t), T.xA[:, t:W:16], 128, ["xA"], ["xvc%d" % t])
        else:
            gcp(nt(T.xvc, t), T.xA[:, t:W:16], L, ["xA"], ["xvc%d" % t])
            gat("S", nt(T.xvq, t - 1), T.xA[:, 0:W], nt(T.prr, t, 16), L, ["xA", "prr%d" % t, AQ[-1]], ["xvq%d" % t])
        if t > 0 and CFG["lists"] == "G":
            for a, b, kind in parts:
                nc = (b - a) // 16
                for c in range(nc):
                    o = 2048 * (c % 2) + a // 2 + 16 * (c // 2) + t
                    gcp(T.ownu[:, t * L + a + c:t * L + b:nc], T.aqs[:, o:o + 1921:128], 16, AQ, ["ownu%d_%d" % (t, c)])
                join(nc)
                ops[-1]["W"] = ["ownu%d_%d" % (t, p) for p in range(PIECES)]
            for role in range(8):
                gcp(T.ownj[:, 32 * role:32 * role + 32], T.aqs[:, 16 * role + t:W:128], 32, AQ, ["ownj"])
                if role % 4 == 3:
                    join(4)
            ts(nt(T.ownh, t), T.ownj[:], -2048.0, None, A.add, None, 128, ["ownj"], ["ownh%d" % t])
        else:
            if t > 0:
                gat("V", nt(T.ownu, t), aqw, nt(T.prr, t, 16), L, AQ + ["prr%d" % t], ["ownu%d_%d" % (t, p) for p in range(PIECES)], False)
            ts(nt(T.ownh, t), aqw.indirect(nt(T.prm, t, 16)), -2048.0, None, A.add, None, 60 + GA * L, AQ + ["prm"], ["ownh%d" % t])
        ts(nt(T.nown, t), T.aqs[:, t:W:16], -2048.0, T.nrm[:, 4 + t:5 + t], A.add, A.mult, L, AQ + ["nrn"], ["nown%d" % t])
    (gcp if CFG["lists"] == "G" else cp)(T.tgu[:], T.tgs[:], L, ["tgs"], ["tgu"])

    REP, room = {}, 0
    for t in range(RO):
        for a, b, e in spans(CFG["cg"][t]):
            if e == "F":
                REP[t, a] = T.reps[:, room:room + 16 * (b - a)]
                ts(T.repl[:, room // 16:room // 16 + b - a], prow[:, a:b] if t else T.lanerow[:, a:b], float(t), None, A.add, None, b - a,
                   ["prow%d" % x for x, y, z in parts] + ["lanerow"], ["repl%d" % room])
                gat("S", REP[t, a], T.xA[:, 0:W], T.repl[:, room // 16:room // 16 + b - a], 16 * (b - a), ["xA", "repl%d" % room] + ([AQ[-1]] if t else []),
                    ["rep%d_%d" % (t, a)])
                room += 16 * (b - a)

    def gathers(tag, raw, win, wkey, lst, lkeys, who, t=0):
        for a, b, e in who:
            wr = ["%sraw%d" % (tag, u) for u in range(a // 8, b // 8)]
            if e == "F":
                tt(raw[:, 16 * a:16 * b], win.indirect(lst[:, a:b]), REP[t, a], A.subtract, 60 + GA * 16 * (b - a),
                   [wkey, "rep%d_%d" % (t, a)] + lkeys(a, b), wr, [], True)
            else:
                gat(e, raw[:, 16 * a:16 * b], win, lst[:, a:b], 16 * (b - a), [wkey] + lkeys(a, b), wr)

    def add(lst, R, key, kb):
        for i in range(0, len(lst), CFG["per"]):
            part = lst[i:i + CFG["per"]]
            if part[0][3] or part[-1][4]:
                mm(part, R, [key], [kb], len(part), True)
            else:
                mm(part, R + [key], ["%s_%d" % (key, len(ops))], [kb], len(part), True)

    def scores(tag, raw, non, a, b, kind, xv, xkey, blocks, key, kb, first, last, diff, skip=-1, later=None):
        rk = ["%sraw%d" % (tag, u) for u in range(a // 8, b // 8)]
        nk = ["%snon%d_%d" % (tag, u, k) for k in range(16) for u in range(a // 16, b // 16)]
        m = len(nk) // 16
        if kind in "MR":
            add([(o, Z(T.zm16, r), raw[:, 16 * i:16 * j], first and x == 0, False, n) for x, (r, o, i, j, st, n) in enumerate(blocks)], rk + ["zm16"], key, kb)
        if kind == "R":
            ts(non[:, a:b, :], raw[:, 16 * a:16 * b], 0.0, None, A.max, None, 8 * (b - a), rk, nk, [], True)
        elif kind == "M":
            for k in range(16):
                tt(non[:, a:b, k], raw[:, 16 * a + k:16 * b:16], T.B0[:, a:b], A.max, b - a, rk + ["B0lo"], nk[m * k:m * k + m], ["B0"], True)
                if k % CFG["mg"] == CFG["mg"] - 1:
                    join(CFG["mg"])
        else:
            for kh in range(2):
                bn = diff[kh]
                lo, hi = 8 * kh, 8 * kh + 8
                runs = [(x, y) for x, y in (((lo, skip), (skip + 1, hi)) if lo <= skip < hi else ((lo, hi),)) if x < y]
                lst, w = [], b - a
                for x, y in runs:
                    for k in range(x, y):
                        o = T[bn][:, w * (x - lo) + k - x:w * (y - lo):y - x]
                        lst += [(o, T.eye[:], raw[:, 16 * a + k:16 * b:16], not lst, False, w), (o, T.neye[:], xv[:, a:b], False, k == hi - 1, w)]
                mm(lst, rk + ["eye", "neye", xkey], [bn], [bn], CFG["per"], True)
                for x, y in runs:
                    ac(non[:, a:b, x:y], T[bn][:, w * (x - lo):w * (y - lo)], AF.Abs, w * (y - x), [bn], nk[m * x:m * y], [bn])
                join(len(runs))
        z = T.z16 if kind == "A" else T.z32
        total = lambda: add([(o, Z(z, r), non[:, i:j:st, :], first and kind == "A" and x == 0, last and x == len(blocks) - 1, n)
                             for x, (r, o, i, j, st, n) in enumerate(blocks)], nk + ["z32", "z16"], key, kb)
        if later is None:
            total()
        else:
            later.append(total)

    def redirect(win, key, t, w, more=()):
        off = T.wo1[:, 34 * t + 32:34 * t + 34] if w == 1 else T.wo2[:, 68 * t + 66:68 * t + 68]
        sca(win, off, T.urow[:, 64 * t + 32 * (w - 1):64 * t + 32 * w], 32, ["woff%d%d" % (w, t), "urow%d" % t], [key] + list(more))

    def night(t):
        s = str(t)
        xv = nt(T.xvc, t)
        B0, B1, B2 = T.B0, T.B1, T.B2
        xq, qk = (xv, "xvc0") if t == 0 else (nt(T.xvq, t - 1), "xvq" + s)
        how = spans(CFG["cn"][t])
        mm([(B0[:, 0:L], T.eye[:], xq, True, True, L)], ["eye", qk], ["B0lo"], ["B0"])
        DR = 32 if CFG["split"] and t > 0 else FIRST
        bank = lambda b: "B2" if t == 0 or b > FIRST else "B1" if b <= DR else "B3"
        gathers("c", T.near, T.xA[:, 0:W], "xA", nt(T.ownu, t), lambda a, b: ["ownu%d_%d" % (t, p) for p in range(a * PIECES // L, (b - 1) * PIECES // L + 1)],
                spans(CFG["cg"][t]), t)

        def part(a, b, kind):
            if t == 0:
                blocks = [((i // 8) % 16, B2[:, i // 128 * 128:i // 128 * 128 + 128], i, i + 8, 1, 128) for i in range(a, b, 8)]
            else:
                x, y = [(x, y) for x, y, z in parts if x <= a < y][0]
                nc = (y - x) // 16
                blocks = [(r, T[bank(b)][:, x:y], x + r * nc, x + (r + 1) * nc, 1, y - x) for r in range((a - x) // nc, (b - x) // nc)]
            scores("c", T.near, T.mc, a, b, kind, xq, qk, blocks, bank(b) + "lo", bank(b), a == 0 or (t > 0 and a in (DR, FIRST)),
                   b == L or (t > 0 and b in (DR, FIRST)), ("B3", "B1" if t == 0 else "B3"))

        def best(a, b, kb, h):
            ca, cb = a // 16, b // 16
            scan(T.ksc[:, a:b], T.cmax[:, a:b], T[kb][:, a:b], A.add, A.max, b - a, ["cmax", kb + "lo"], ["ksc" + x for x in h], [kb])
            ts(T.kj[:, ca:cb], T.ksc[:, a + 15:b:16], 15, None, A.bitwise_and, None, 16, ["ksc" + x for x in h], ["kj" + x for x in h])
            if t == 0:
                for x in range(2):
                    cp(T.ku[:, x:16:2], T.kj[:, 8 * x:8 * x + 8], 8, ["kjA"], [["kuA", "kuD"], ["kuB"]][x])
            else:
                cp(T.ku[:, ca:cb], T.kj[:, ca:cb], 16, ["kj" + h], ["ku" + h])

        def pick(u, a, b, h):
            tt(T.sel[:, u, a:b], T.oh[:, 16 - 16 * u:32 - 16 * u].indirect(T.ku[:, a // 16:b // 16]), T.ownh[:, t * L + a:t * L + b], A.mult,
               60 + GA * (b - a), (["kuA", "kuB"] if t == 0 else ["ku" + h]) + ["oh%d" % (1 - u), "ownh" + s], ["sel%s%d" % (h, u)])
        for a, b, kind in how:
            if t == 0 or b <= FIRST:
                part(a, b, kind)
        if t == 0:
            best(0, L, "B2", "DAB")
        else:
            best(0, DR, "B1", "D")
            if DR < FIRST:
                best(DR, FIRST, "B3", "A")
        for a, b, h in ((0, DR, "D"), (DR, FIRST, "A")):
            if a < b:
                pick(1, a, b, h)
                pick(0, a, b, h)
        o = FIRST
        rows = [(B1[:, o + 16:o + 80], T.boh[:], T.sel[:, :, 0:32], False, False, 64), (B1[:, o + 80:o + 112], T.boh[:], T.sel[:, 0, 0:32], False, DR < FIRST, 32)]
        mm([(B1[:, o:o + 144], T.boh[:], T.c128[:], True, False, 144)], ["boh", "c128"], ["B1md"], ["B1"])
        if DR < FIRST:
            B3, wb, zo = T.B3, "B3", o + 16
            lst = lambda u, c1, role: B1[:, o + 2 * u + c1:o + 2 * u + c1 + 1] if role == 0 else B3[:, o + 4 + c1:o + 5 + c1]
            mm([(B1[:, o:o + 4], Z(T.zh, r), T.sel[:, :, r:32:16], False, False, 4) for r in range(16)] + rows, ["selD0", "selD1", "zh", "boh"], ["B1md"], ["B1"], 18)
            mm([(B3[:, o:o + 48], T.boh[:], T.c128[:, 0:48], True, False, 48)], ["boh", "c128"], ["B3md"], ["B3"])
            mm([(B3[:, o:o + 8], Z(T.zh, r), T.sel[:, :, 32 + r:FIRST:16], False, False, 8) for r in range(16)]
               + [(B3[:, o + 16:o + 48], T.boh[:], T.sel[:, 1, 32:64], False, True, 32)], ["selA0", "selA1", "zh", "boh"], ["B3md"], ["B3"], 17)
            ul, uz = [(0, 8, o)], (0, 4, 6)
        else:
            B3, wb, zo = B1, "B1", o + 112
            lst = lambda u, c1, role: B1[:, o + 6 * u + 2 * role + c1:o + 6 * u + 2 * role + c1 + 1]
            mm([(B1[:, o:o + 12], Z(T.zh, r), T.sel[:, :, r:FIRST:16], False, False, 12) for r in range(16)] + rows
               + [(B1[:, zo:zo + 32], T.boh[:], T.sel[:, 1, 32:64], False, True, 32)], ["selD0", "selD1", "zh", "boh"], ["B1md"], ["B1"], 19)
            ul, uz = [(0, 10, o + 2)], (0, 6, 8)
        for c1 in range(2):
            for po in range(2):
                e = 132 * c1 + 2 + 64 * po
                ts(T.eqd[:, e:e + 64], B1[:, o + 16:o + 80], lst(po, c1, 0), T.dum[:, c1:c1 + 1], A.is_equal, A.mult, 64,
                   ["B1md", "dum"], ["eqd%d" % (2 * c1 + po)], ["B1"])
        join(4)
        scan(T.nsc[:], T.cvoid[:], T.eqd[:], A.add, A.max, 132, ["cvoid", "eqd0", "eqd1", "eqd2", "eqd3"], ["nsc"])
        cp(T.rowpo[:], B1[:, o + 16:o + 112], 96, ["B1md"], ["rowpo"], ["B1"])
        for po in range(2):
            for c1 in range(2):
                e = 2 * po + c1
                ts(T.soff[:, 4 * t + e:4 * t + e + 1], T.nsc[:, 132 * c1 + 130 + po:132 * c1 + 131 + po], lst(po, c1, 0), None, A.max, None, 1,
                   ["nsc", "B1md"], ["soff%d_%d" % (t, e)], ["B1"])
        join(4)
        so = ["soff%d_%d" % (t, e) for e in range(4)]
        cp(T.ulist[:, 10 * t:10 * t + ul[0][1]], B3[:, ul[0][2]:ul[0][2] + ul[0][1]], 10, [wb + "md"], ["ulist" + s], [wb])
        cp(T.zlist[:, 0:4:2], B3[:, ul[0][2] + uz[1]:ul[0][2] + uz[1] + 2], 2, [wb + "md"], ["zlist"], [wb])
        for c1 in range(2):
            ts(T.eqw[:, 34 * c1 + 1:34 * c1 + 33], B3[:, zo:zo + 32], lst(1, c1, 1), T.dum[:, c1:c1 + 1], A.is_equal, A.mult, 32,
               [wb + "md", "dum"], ["eqw%d" % c1], [wb])
        join(2)
        scan(T.wsc[:, 0:68], T.cwave[:], T.eqw[:, 0:68], A.add, A.max, 68, ["cwave", "eqw0", "eqw1"], ["wsc0"])
        sca(T.stab[:, 0:WD], nt(T.soff, t, 4), T.rowpo[:, 32:96], 64, so + ["rowpo"] + STAB0, ["stab"])
        st = T.stab[:, 0:W]
        for c1 in range(2):
            gat("V", T.zr1[:, 17 * c1:17 * c1 + 16], st, T.zlist[:, 2 * c1:2 * c1 + 1], 16, ["stab", "zlist"], ["zr1"], False)
        join(2)
        gat("V", nt(T.urow, t, 64), st, T.ulist[:, 10 * t:10 * t + 4], 64, ["stab", "ulist" + s], ["urow" + s])
        for c1 in range(2):
            op("V", [lambda c1=c1: V.tensor_tensor_scan(T.wo1[:, 34 * t + c1:34 * t + 34:2], T.cw1[:], nt(T.zr1, c1, 17), T.wsc[:, 34 * c1 + 32:34 * c1 + 33],
                                                        A.add, A.max)], 64, ["cw1", "zr1", "wsc0"], ["woff1" + s])
        join(2)
        redo = CFG["redo"] and t > 0

        def rest():
            if t > 0:
                for a, b, kind in how:
                    if b > FIRST:
                        part(a, b, kind)
                best(FIRST, L, "B2", "B")
            pick(1, FIRST, L, "B")
            mm([(B0[:, L:L + 16], T.boh[:], T.c128[:, 0:16], True, False, 16)]
               + [(B0[:, L:L + 16], Z(T.zh, r), T.sel[:, 1, 32 * (r % 8) + r // 8:32 * (r % 8) + 32:2], False, r == 15, 16) for r in range(16)],
               ["selD1", "selA1", "selB1", "zh", "boh", "c128"], ["B0hi"], ["B0"], 17)
            cp(T.tlist[:], B0[:, L:L + 16], 16, ["B0hi"], ["tlist"], ["B0"])
            gat("V", T.tw[:, t:W:16], st, T.tlist[:], L, ["stab", "tlist"], ["tw"])
            if t < RO - 1 and CFG["reset"] == "G":
                for h in range(8):
                    iota(nt(T.stab, h, 512), [[1, 512]], 512 * h, 0, 512, ["stab"])
            elif t < RO - 1:
                sca(T.stab[:, 0:WD], nt(T.soff, t, 4), T.rowpo[:, 0:64], 64, so + ["rowpo"], ["stab"])
        if redo:
            gat("V", T.tw[:, 32 + t:W:128], st, T.ulist[:, 10 * t + uz[2]:10 * t + uz[2] + 2], 32, ["stab", "ulist" + s], ["tw"])
        else:
            rest()
        redirect(T.tw[:, 0:WD], "tw", t, 1)
        zrow = T.tw[:, 32 + t:W:128]
        scan(T.st1[:, 32:64], T.cfz[:, 0:32], zrow, A.add, A.max, 32, ["cfz", "tw"], ["st11"])
        ts(T.st1[:, 0:32], zrow, kc, None, A.add, None, 32, ["tw", "kc"], ["st11"])
        join(2)
        for c1 in range(2):
            ts(T.eqw[:, 68 + 34 * c1 + 1:68 + 34 * c1 + 33], T.st1[:, 0:32], T.st1[:, 47 + 16 * c1:48 + 16 * c1], T.dum[:, c1:c1 + 1], A.is_equal, A.mult, 32,
               ["st11", "dum"], ["eqw%d" % (2 + c1)])
        ts(T.eqw[:, 101:136:34], T.st1[:, 47:64:16], kc, None, A.subtract, None, 2, ["st11", "kc"], ["eqw2"])
        join(3)
        for c1 in range(2):
            scan(T.wo2[:, 68 * t + c1:68 * t + 68:2], nt(T.cwave, c1, 34), nt(T.eqw, 2 + c1, 34), A.add, A.max, 34, ["cwave", "eqw2", "eqw3"], ["woff2" + s])
        join(2)
        if redo:
            rest()
            redirect(T.tw[:, 0:WD], "tw", t, 1)
        redirect(T.tw[:, 0:WD], "tw", t, 2)
        scan(T.asc[:], T.cfz[:], T.tw[:, t:W:16], A.add, A.max, L, ["cfz", "tw"], ["asc"])
        ts(nt(T.alist, t, 16), T.asc[:, 15:L:16], kc, None, A.subtract, None, 16, ["asc", "kc"], ["alist" + s])
        kt = T.kct[:, t:t + 1]
        for h in range(2):
            scan(nt(T.bsc, h, 32), T.cfz[:, 0:32], T.tw[:, 16 * (3 + h) + t:W:128], A.add, A.max, 32, ["cfz", "tw"], ["bsc"])
        join(2)
        for h in range(2):
            ts(nt(T.ub, h, 32), T.tw[:, 16 * (3 + h) + t:W:128], -2048.0 - t, None, A.add, None, 32, ["tw"], ["ub"])
        join(2)
        mm([(B1[:, 0:64], T.eye[:], T.ub[:], True, False, 64)], ["eye", "ub"], ["B1lo"], ["B1"])
        for c in range(4):
            ts(nt(T.at1, c, 64), T.idrow[:], kt, T.bsc[:, 16 * c + 15:16 * c + 16], A.add, A.is_equal, 64, ["idrow", "kct", "bsc"], ["at1%d" % c])
        join(4)
        ts(T.ucol[:], T.bsc[:, 15:64:16], kt, None, A.subtract, None, 4, ["bsc", "kct"], ["ucol"])
        mm([(B1[:, 0:64], T.bo[:], nt(T.at1, c, 64), False, c == 3, 64) for c in range(4)], ["bo", "at10"], ["B1lo"], ["B1"])
        for c in range(4):
            ts(nt(T.a2, c, 64), B1[:, 0:64], T.idcol[:, c:c + 1], None, A.is_equal, None, 64, ["B1lo", "idcol"], ["a2%d" % c], ["B1"])
        join(4)
        scan(T.b2[:], T.rst[:], T.a2[:], A.mult, A.max, L, ["rst"] + ["a2%d" % c for c in range(4)], ["b2"])
        d = 1 + t % 3
        gat(CFG["xa"], T.xa[:], T["rep%d" % d][:, 0:W], nt(T.alist, t, 16), L, ["rep%d" % d, "alist" + s], ["xa"])
        free, fk = nt(T.free, t), "free" + s
        new, nk = (T.xA[:, t:W:16], "xA") if t < RO - 1 else (nt(T.nxc, t), "nxc" + s)
        clamp = CFG["clamp"]
        if clamp:
            mm([(B2[:, 0:L], T.hey[:], xv, True, False, L), (B2[:, 0:L], T.nhey[:], T.half[:], False, False, L)], ["hey", "nhey", "half", "xvc" + s], ["B2lo"], ["B2"])
            mm([(B2[:, 0:L], T.hey[:], T.xa[:], False, True, L)], ["hey", "xa"], ["B2lo"], ["B2"])
            ts(T.mh[:], B2[:, 0:L], MAGIC, -MAGIC, A.add, A.add, L, ["B2lo"], ["mh"], ["B2"])
            mm([(B1[:, L:2 * L], T.eye[:], T.mh[:], True, False, L)], ["eye", "mh"], ["B1hi"], ["B1"])
            mm([(B0[:, 0:L], T.eye[:], T.mh[:], True, False, L)], ["eye", "mh"], ["B0lo"], ["B0"])
        else:
            mm([(B0[:, 0:L], T.eye[:], xv, True, False, L), (B0[:, 0:L], T.nhey[:], T.half[:], False, False, L)], ["eye", "nhey", "half", "xvc" + s], ["B0lo"], ["B0"])
            mm([(B2[:, 0:L], T.nhey[:], xv, True, False, L)], ["nhey", "xvc" + s], ["B2lo"], ["B2"])
            mm([(B2[:, 0:L], T.hey[:], T.xa[:], False, True, L)], ["hey", "xa"], ["B2lo"], ["B2"])
        for c in range(4):
            ts(nt(T.at3, c), T.lanerow[:], T.ucol[:, c:c + 1], T.b2[:, 64 * c + 63:64 * c + 64], A.is_equal, A.is_gt, 128,
               ["lanerow", "ucol", "b2"], ["at3%d" % c])
            mm([(B1[:, L:2 * L], T.bo[:], nt(T.at3, c), c == 0 and not clamp, c == 3, L)], ["bo", "at3%d" % c], ["B1hi"], ["B1"])
            if clamp:
                mm([(B0[:, 0:L], T.nbo[:], nt(T.at3, c), False, c == 3, L)], ["nbo", "at3%d" % c], ["B0lo"], ["B0"])
        if clamp:
            tt(T.xa[:], xv, B1[:, L:2 * L], A.min, L, ["B1hi", "xvc" + s], ["xa"], ["B1"])
            tt(new, T.xa[:], B0[:, 0:L], A.max, L, ["B0lo", "xa"], [nk], ["B0"])
            ts(free, B1[:, L:2 * L], KF / 2, None, A.is_lt, None, L, ["B1hi"], [fk], ["B1"])
        else:
            if CFG["free"] == "S":
                op("S", [lambda: S.activation(free, B1[:, L:2 * L], AF.Relu, bias=1.0, scale=-1.0)], L, ["B1hi"], [fk], ["B1"])
            else:
                ts(free, B1[:, L:2 * L], 0.0, None, A.is_equal, None, L, ["B1hi"], [fk], ["B1"])
            tt(T.mh[:], B2[:, 0:L], free, A.mult, L, ["B2lo", fk], ["mh"], ["B2"])
            mm([(B0[:, 0:L], T.eye[:], T.mh[:], False, True, L)], ["eye", "mh"], ["B0lo"], ["B0"])
            ts(new, B0[:, 0:L], MAGIC, -MAGIC, A.add, A.add, L, ["B0lo"], [nk], ["B0"])
        if t < RO - 1:
            gcp(nt(T.nxc, t), T.xA[:, t:W:16], L, ["xA"], ["nxc" + s])
            ks = [k for k, (tu, du) in enumerate(UPD) if tu == t]
            send([(UPD[k][1], nt(T.updin, k), nt(T.nxc, t), "ux%d" % k) for k in ks], "lsm", ["nxc" + s, "rs"], ["updin%d" % k for k in ks] + ["rs"], 0.1 * len(ks))
        if t == 0:
            send([(2, T.rep3[:], T.rep1[:], "rx3")], "lx2", ["rep1", "rs"], ["rep3", "rs"], 1.0)
        dma(T.yx[:, t * L:(t + 1) * L], nt(T.nxc, t), "outs", ["nxc" + s], [], 0.1)

    def visit(t):
        s = str(t)
        d = 1 + t % 3
        rep, rk, aqw, ak = T["rep%d" % d][:, 0:W], "rep%d" % d, T["aqr%d" % d][:, 0:W], "aqr%d" % d
        xv, al = nt(T.xvc, t), nt(T.alist, t, 16)
        H = CFG["halves"]
        hw = L // H
        for h in range(H):
            gat("V", nt(T.alu, h, hw), aqw, nt(al, h, hw // 16), hw, [ak, "aqr1b", "alist" + s], ["alu%d" % x for x in range(h * 2 // H, (h + 1) * 2 // H)], False)
        gathers("v", T.far, rep, rk, T.alu, lambda a, b: ["alu%d" % x for x in range(a // 128, (b - 1) // 128 + 1)], spans(CFG["vg"][t]))
        later = []
        for a in range(0, L, 64):
            scores("v", T.far, T.mv, a, a + 64, "A", xv, "xvc" + s, [(r, T.B6[:, a:a + 64], a + r, a + 64, 16, 64) for r in range(16)],
                   "B6lo", "B6", a == 0, a + 64 == L, [CFG["vb"][(a // 32 + x) % len(CFG["vb"])] for x in range(2)], t - 1, later if t in CFG["late"] else None)
        if t == 0:
            ts(T.alh[:], T.alu[:], -2048.0, None, A.add, None, 128, ["alu0", "alu1"], ["alh0", "alh1"])
        else:
            renew(t - 1, [d])
            for h in range(H):
                ts(nt(T.alh, h, hw), aqw.indirect(nt(al, h, hw // 16)), -2048.0, None, A.add, None, 60 + GA * hw, [ak, "alist" + s],
                   ["alh%d" % x for x in range(h * 2 // H, (h + 1) * 2 // H)])
            o = 144 * (t - 1) + 15
            mm([(T.B7[:, L:L + 16], T.boh[:], T.c128[:, 0:16], True, False, 16)]
               + [(T.B7[:, L:L + 16], T.bok[:, o - r:o + 128 - r], T.alh[:, r:L:16], False, r == 15, 16) for r in range(16)],
               ["bok%d" % (t - 1), "alh0", "alh1", "boh", "c128"], ["B7hi"], ["B7"], 17)
            cp(T.plist[:], T.B7[:, L:L + 16], 16, ["B7hi"], ["plist"], ["B7"])
            gat("S", T.farp[:], rep, T.plist[:], L, [rk, "plist"], ["farp"])
            mm([(T.B7[:, 0:L], T.eye[:], T.farp[:], True, False, L), (T.B7[:, 0:L], T.neye[:], xv, False, True, L)],
               ["farp", "eye", "neye", "xvc" + s], ["B7lo"], ["B7"])
            if later:
                ac(T.mv[:, :, t - 1], T.B7[:, 0:L], AF.Abs, L, ["B7lo"], ["vnon%d_%d" % (u, t - 1) for u in range(16)], ["B7"], False)
                for total in later:
                    total()
            else:
                ac(T.mvp[:], T.B7[:, 0:L], AF.Abs, L, ["B7lo"], ["mvp"], ["B7"], False)
                mm([(T.B6[:, t - 1:L:16], Z(T.z16, r), T.mvp[:, r:L:16], r == 0, r == 15, 16) for r in range(16)], ["z16", "mvp"], ["B6lo"], ["B6"], 16)
        scan(T.vsc[:], T.cmin[:], T.B6[:, 0:L], A.add, A.min, L, ["cmin", "B6lo"], ["vsc"], ["B6"])
        ts(T.vj[:], T.vsc[:, 15:L:16], 15, None, A.bitwise_and, None, 16, ["vsc"], ["vj"])
        cp(T.vu[:], T.vj[:], 16, ["vj"], ["vu"])
        mm([(T.B6[:, L:2 * L], Z(T.zh, t), nt(T.nown, t), True, False, L)], ["zh", "nown" + s], ["B6hi"], ["B6"])
        G = H if t < RO - 1 else 1
        for h in range(G):
            tt(nt(T.selv, h, L // G), T.oh[:, 32:48].indirect(nt(T.vu, h, 16 // G)), nt(T.alh, h, L // G), A.mult, 60 + GA * L // G,
               ["vu", "oh2", "alh0", "alh1"], ["selv%d" % x for x in range(h * 2 // G, (h + 1) * 2 // G)])
        mm([(T.B6[:, L:2 * L], Z(T.zh, t), T.selv[:], False, True, L)], ["zh", "selv0", "selv1"], ["B6hi"], ["B6"])
        tt(T.B7[:, L:2 * L], T.B6[:, L:2 * L], nt(T.free, t), A.mult, L, ["B6hi", "free" + s], ["B7hi"], ["B6", "B7"])
        tt(nt(T.ymc, t), T.aqs[:, t:W:16], T.B7[:, L:2 * L], A.add, L, AQ + ["B7hi"], ["ymc" + s] + TMP, ["B7"])
        ks = [k for k, (tu, du) in enumerate(UPD) if tu == t]
        if ks:
            send([(UPD[k][1], nt(T.ymin, k), nt(T.ymc, t), "uq%d" % k) for k in ks], "lsm", ["ymc" + s, "rs"], ["ymin%d" % k for k in ks] + ["rs"], 0.16 * len(ks))
        dma(T.ym[:, t * L:(t + 1) * L], T.ymc[t:128:16, t * L:(t + 1) * L], "outs", ["ymc" + s], [], 0.05)
        for k in ks:
            gcp(T["rep%d" % UPD[k][1]][:, t:W:16], nt(T.updin, k), L, ["updin%d" % k], ["rep%d" % UPD[k][1]])
        if t > 0:
            renew(t - 1, [x for x in (1, 2, 3) if x != d])

    def renew(t, dists):
        for k, (tu, du) in enumerate(UPD):
            if tu == t and du in dists:
                (gcp if CFG["renew"][k] == "G" else cp)(T["aqr%d" % du][:, t:W:16], nt(T.ymin, k), L, ["ymin%d" % k], ["aqr%d" % du])

    def targets():
        st = T.stab[:, 0:WD]
        for t in (2, 1, 0):
            so = ["soff%d_%d" % (t, e) for e in range(4)]
            gat("S", nt(T.vall, t), st, nt(T.alist, t, 16), L, ["stab", "alist%d" % t, "ymc0"], ["vall%d" % t])
            gat("V", T.swp[:, 0:32], st, T.soff[:, 4 * t + 2:4 * t + 4], 32, ["stab"] + so, ["swp0"])
            gat("V", T.swp[:, 32:64], st, T.soff[:, 4 * t:4 * t + 2], 32, ["stab"] + so, ["swp1"])
            sca(st, nt(T.soff, t, 4), T.swp[:], 64, so + ["swp0", "swp1"], ["stab"])
            gat("S", nt(T.urow, t, 64), st, T.ulist[:, 10 * t:10 * t + 4], 64, ["stab", "ulist%d" % t], ["urow%d" % t])
        n8 = len(CFG["yg"])
        w = L // n8
        gcp(nt(T.vall, RO - 1), T.tw[:, RO - 1:W:16], L, ["tw"], ["vall%d" % (RO - 1), "tw"])
        for n in range(n8):
            gat(CFG["yg"][n], T.tw[:, 16 * w * n:16 * w * (n + 1)], st, T.tgu[:, w * n:w * (n + 1)], 16 * w, ["stab", "tgu", "tw"], ["yy%d" % n])
        for t in range(RO):
            redirect(T.tw[:, 0:WD], "yy", t, 1, ["yy%d" % n for n in range(n8)] if t == 0 else [])
            redirect(T.tw[:, 0:WD], "yy", t, 2)
            o, a = T.tw[:, t:W:16], nt(T.vall, t)
            cp(o, a, L, ["vall%d" % t], ["yy"])
            ops[-1]["alt"] = {"V": (ops[-1]["f"], L), "S": ([lambda o=o, a=a: S.activation(o, a, AF.Copy)], L)}
        dma(T.yt[:, :], T.tw[0:128:16, 0:W], "outs", ["yy"], [], 0.2)

    for t in range(RO):
        phase[0] = "n"
        night(t)
        if t == RO - 1:
            phase[0] = "t"
            targets()
        phase[0] = "v"
        visit(t)
    return ops


def depend(ops):
    last, readers, epoch = {}, {}, {}
    for i, o in enumerate(ops):
        dep = {}

        def add(j, how, key=None, reads=True):
            if key in ("ld", "rs", "hs"):
                dep.setdefault((j, "o", None), False)
            elif how == "w" and ops[j]["k"] == "r":
                dep[(j, how, ops[j]["W"].index(key))] = True
            else:
                dep[(j, "w" if ops[j]["k"] == "c" else how, 0)] = not (o["e"] == "P" and ops[j]["e"] == "P")
        for k in o["R"]:
            if k in last:
                add(last[k], "w", k)
        for k in o["W"]:
            if k in last:
                add(last[k], "w", k, False)
            for j in readers.get(k, []):
                if j != i:
                    add(j, "r", k, False)
        for b in o["b"]:
            eng, cur, prev = epoch.get(b, (None, [], []))
            if eng == o["e"]:
                cur.append(i)
            else:
                eng, cur, prev = o["e"], [i], cur
            for j in prev:
                add(j, "w")
            epoch[b] = (eng, cur, prev)
        for k in o["R"]:
            readers.setdefault(k, []).append(i)
        for k in o["W"]:
            last[k] = i
            readers[k] = []
        o["dep"] = [(j, how, n, wt) for (j, how, n), wt in dep.items()]


def place(eng, dur, pred, tail, p, order, k0, base):
    rest = sorted(order[k0:])
    for i in rest:
        for j, lt, dm in pred[i]:
            if p[j] >= p[i]:
                p[i] = p[j] + 0.001
    fin, done = (list(base[2]), list(base[4])) if k0 else ([0.0] * len(eng), [0.0] * len(eng))
    lo = {e: [-1.0] for e in "VSPGYH"}
    hi = {e: [0.0] for e in "VSPGYH"}
    for i in order[:k0]:
        hi[eng[i]][0] = fin[i]
    start, tol = {}, CFG["tol"]
    rest.sort(key=lambda k: p[k])
    for i in rest:
        t = 0.0
        for j, lt, dm in pred[i]:
            x = (done[j] if dm else fin[j]) + lt
            if x > t:
                t = x
        a, b, d = lo[eng[i]], hi[eng[i]], dur[i]
        k = n = len(a)
        while k > 1 and b[k - 1] > t:
            k -= 1
        if b[k - 1] > t:
            t = b[k - 1]
        while k < n and a[k] < t + d - tol:
            if b[k] > t:
                t = b[k]
            k += 1
        a.insert(k, t)
        b.insert(k, t + d)
        start[i] = t
        fin[i] = t + d
        done[i] = t + d + tail[i]
    rest.sort(key=lambda k: start[k])
    return order[:k0] + rest


def replay(eng, dur, pred, move, lat, order, k0=0, base=None):
    n = len(eng)
    fin, done, why = (list(base[2]), list(base[4]), list(base[1])) if k0 else ([0.0] * n, [0.0] * n, [None] * n)
    free, last, busy = {e: 0.0 for e in "VSPGYH"}, {e: None for e in "VSPGYH"}, {True: 0.0, False: 0.0}
    for i in order[:k0]:
        last[eng[i]] = i
        if move[i]:
            busy[eng[i] == "H"] = done[i]
    for e in last:
        if last[e] is not None:
            free[e] = fin[last[e]]
    for i in order[k0:]:
        e = eng[i]
        t, w = free[e], (last[e], True)
        for j, lt, dm in pred[i]:
            x = (done[j] if dm else fin[j]) + lt
            if x >= t:
                t, w = x, (j, False)
        fin[i] = done[i] = free[e] = t + dur[i]
        if move[i]:
            busy[e == "H"] = done[i] = max(fin[i] + lat, busy[e == "H"]) + move[i]
        why[i], last[e] = w, i
    end = max(done)
    return end, why, fin, done.index(end), done


def neighbours(why, i):
    pairs = []
    while i is not None:
        if why[i][1] and why[i][0] is not None:
            pairs.append((why[i][0], i))
        i = why[i][0]
    return pairs


def schedule(sets):
    ops = sets[0]
    n = len(ops)
    eng = [o["e"] for o in ops]
    durs = [[o["d"] * (c[6] if o["k"] == "c" else 1.0) for o in s] for s, c in zip(sets, COSTS)]
    moves = [[o["mib"] * c[4] for o in ops] for c in COSTS]
    tail = [(COSTS[0][5] + moves[0][i] + o["hint"]) if o["mib"] else 0.0 for i, o in enumerate(ops)]
    preds = [[[(j, c[3] if wt else 0.0, 0.0 if how == "o" else tail[j]) for j, how, k, wt in o["dep"]] for o in ops] for c in COSTS]
    anc, des = [0] * n, [0] * n
    for i in range(n):
        for j, lt, dm in preds[0][i]:
            anc[i] |= anc[j] | 1 << j
    for i in range(n - 1, -1, -1):
        for j, lt, dm in preds[0][i]:
            des[j] |= des[i] | 1 << i
    for pred in preds:
        for i in range(n):
            far = 0
            for j, lt, dm in pred[i]:
                if lt:
                    far |= anc[j]
            pred[i] = [x for x in pred[i] if ops[x[0]]["k"] != "c" or ops[x[0]]["e"] == "P" or not far >> x[0] & 1]
    level = [durs[0][i] + tail[i] for i in range(n)]
    for i in range(n - 1, -1, -1):
        for j, lt, dm in preds[0][i]:
            level[j] = max(level[j], durs[0][j] + lt + dm + level[i])
    group, names, count = [], {}, 0
    for i, o in enumerate(ops):
        key = (o["e"], (o["W"] + ["-"])[0].split("_")[0])
        if key not in names or names[key][1] < i - 40:
            names[key] = [count, i]
            count += 1
        names[key][1] = i
        group.append(names[key][0])
    group = np.array(group)
    rs = np.random.RandomState(CFG["seed"])

    def shift(order, a, b, ahead):
        i, j = order.index(a), order.index(b)
        mid = order[i:j + 1]
        x = b if ahead else a
        mask = (anc[x] if ahead else des[x]) | 1 << x
        took, left = [k for k in mid if mask >> k & 1], [k for k in mid if not mask >> k & 1]
        return order[:i] + (took + left if ahead else left + took) + order[j + 1:]

    def search(m, aims, start, eng, since, tries):
        d0, grp = np.array(durs[0][:m]), group[:m]

        def value(x):
            return sum(w * (x[0] if k is None else x[2][k]) for k, w in aims)

        def score(p, eng, bound=1e18, order=None, old=None):
            k0 = 0
            if old is not None:
                if order is None:
                    ch = np.nonzero(p != old[1])[0]
                    first = min([p[ch].min(), old[1][ch].min()] if len(ch) else [1e18])
                    if eng is not old[4]:
                        first = min([first] + [p[x] - 2000.0 for x in range(m) if eng[x] != old[4][x]])
                    k0 = int(np.searchsorted(old[1][old[2]], first - 300.0))
                elif eng is old[4]:
                    while k0 < m and order[k0] == old[2][k0]:
                        k0 += 1
            if order is None:
                order = place(eng, durs[0], preds[0], tail, list(p), old[2] if old else list(range(m)), k0, old[3][0] if old else None)
            res = [replay(eng, durs[0], preds[0], moves[0], COSTS[0][5], order, k0, old[3][0] if old else None)]
            if value(res[0]) > bound:
                return None
            res += [replay(eng, durs[c], preds[c], moves[c], COSTS[c][5], order, k0, old[3][c] if old else None) for c in range(1, len(sets))]
            st = np.array(res[0][2]) - d0
            return sum(value(x) for x in res) / len(res), st, sorted(order, key=lambda k: st[k]), res, eng

        def critical(res, p):
            x, k = res[rs.randint(len(res))], aims[0 if rs.randint(3) else rs.randint(len(aims))][0]
            return [ab for ab in neighbours(x[1], x[3] if k is None else k) if p[ab[1]] >= since]
        top = best = min((score(x, eng[:m]) for x in start), key=lambda z: z[0])
        for it in range(tries):
            p, eng, order = best[1].copy(), best[4], None
            pairs = critical(best[3], p)
            kind = rs.randint(16) if pairs else 15
            if pairs:
                a, b = pairs[rs.randint(len(pairs))]
            if kind < 3:
                order = shift(best[2], a, b, rs.randint(2))
            elif kind < 5:
                eng = list(eng)
                loose = [x for x in range(m) if "alt" in ops[x] and p[x] >= since]
                on = [x for ab in pairs for x in ab if "alt" in ops[x]]
                a = on[rs.randint(len(on))] if on and rs.randint(2) else loose[rs.randint(len(loose))]
                near = [x for x in loose if eng[x] != eng[a] and abs(p[x] - p[a]) < 2500]
                for x in [a] + ([near[rs.randint(len(near))]] if near and rs.randint(2) else []):
                    eng[x] = "S" if eng[x] == "V" else "V"
                if rs.randint(2):
                    order = sorted(best[2], key=lambda k: p[k])
            elif kind < 8:
                p[b] = p[a] - 1.0
            elif kind < 10:
                p[a] = p[b] + 1.0 + rs.choice([0.0, 300.0, 1500.0])
            elif kind < 12:
                p[grp == grp[b]] -= p[b] - p[grp == grp[a]].min() + 1.0
            elif kind < 13:
                p[grp == grp[a]] += p[grp == grp[b]].max() - p[a] + 1.0
            else:
                near = np.unique(grp[np.abs(p - rs.uniform(since, p.max())) < 3000])
                if len(near) == 0:
                    continue
                for x in rs.choice(near, rs.randint(1, 4)):
                    p[grp == x] += rs.normal() * rs.choice([300.0, 1200.0, 4000.0])
            cand = score(p, eng, value(best[3][0]) + 300.0, order, best)
            if cand is not None and cand[0] <= best[0] + CFG["temp"] * (1.0 - it / tries) * rs.exponential():
                best = cand
            if best[0] < top[0]:
                top = best
        return top
    ends = [i for i, o in enumerate(ops) if o["e"] == "V" and o["W"][0] == "xA"]
    seen = [i for i, o in enumerate(ops) if o["e"] == "V" and o["W"][0][:-1] == "ymc"]
    cuts = [i for i in range(1, n) if ops[i]["ph"] == "v" and ops[i - 1]["ph"] == "n"] + [n, n]
    top, done, since = None, 0, 0.0
    for s, m in enumerate(cuts):
        aims = [(ends[s], 1.0)] + ([(seen[s - 1], CFG["pull"])] if s else []) if s < len(ends) else [(None, 1.0)]
        old = [] if top is None else top[1].tolist()
        base = 0.0 if top is None else old[ends[min(s, len(ends)) - 1]] + level[ends[min(s, len(ends)) - 1]]
        start = [old + [base - (level[i] + (0.0 if ops[i]["bulk"] else x) + (y if ops[i]["ph"] == "n" else 0.0)
                                - (z if ops[i]["ph"] != "n" and eng[i] == "V" else 0.0)) for i in range(done, m)]
                 for x in CFG["bonus"] for y in CFG["lead"] for z in CFG["fill"]] if m > done else [old]
        k = CFG["starts"] if m > done else 1
        top = min((search(m, aims, start[x::k], (list(top[4]) if top else []) + eng[done:], since if m > done else 0.0,
                          int(CFG["tries"] * CFG["share"][s] / k)) for x in range(k)), key=lambda z: z[0])
        done = m
        if s < len(ends):
            since = top[1][ends[s]] - 8000.0
    for i in range(n):
        ops[i]["t"] = top[3][0][2][i] - durs[0][i]
    return top[2], [x[0] for x in top[3]], top[4]


MEMO = {}


def rank_program(g, core, T, topo):
    rank, helping = T.rank_of(core), core in helpers(T, topo)
    if helping:
        rank = helpers(T, topo).index(core)
    if rank is None:
        return
    sets = [build(g, T, topo, rank, c) for c in (COSTS if "order" not in MEMO else COSTS[:1])]
    ops = sets[0]
    depend(ops)
    if "order" not in MEMO:
        MEMO["order"] = schedule(sets)
    order, ends, eng = MEMO["order"]
    for o, e in zip(ops, eng):
        if e != o["e"]:
            o["e"], o["f"] = e, o["alt"][e][0]
    queue = {"H": g} if helping else {"V": g.vector, "S": g.scalar, "P": g.tensor, "G": g, "Y": g.sync}
    total = {}
    for at, i in enumerate(order):
        o = ops[i]
        o["at"] = at
        if o["k"] == "c":
            sm = "e" + o["e"]
            total[sm] = total.get(sm, 0) + len(o["f"])
            o["tw"] = o["tr"] = [(sm, total[sm])]
        else:
            for sm in o["sem"]:
                total[sm] = total.get(sm, 0) + o["cnt"]
            o["tw"] = o["tr"] = [(sm, total[sm]) for sm in o["sem"]]
            if o["k"] == "r":
                total[o["lsem"]] = total.get(o["lsem"], 0) + o["cnt"] * len(o["sem"])
                o["tr"] = [(o["lsem"], total[o["lsem"]])]
    seen = {e: {} for e in queue}
    known = {e: {} for e in queue}
    for i in order:
        o = ops[i]
        if o["e"] not in queue:
            continue
        q, kn = queue[o["e"]], known[o["e"]]
        need = {}
        for j, how, k, wt in o["dep"]:
            if wt:
                sm, c = ops[j]["t" + how][k]
                if c > need.get(sm, (0, 0))[0]:
                    need[sm] = (c, j)
        for sm, (c, j) in sorted(need.items(), key=lambda x: -ops[x[1][1]]["at"]):
            if kn.get(sm, 0) < c:
                q.wait_ge(T.sem[sm], c)
                seen[o["e"]][sm] = kn[sm] = c
                for x, y in ops[j].get("kn", {}).items():
                    kn[x] = max(kn.get(x, 0), y)
        if o["k"] == "c":
            o["kn"] = dict(kn)
        for f in o["f"]:
            ins = f()
            if o["k"] == "c":
                ins.then_inc(T.sem["e" + o["e"]], 1)
            elif o["k"] == "d":
                ins.then_inc(T.sem[o["sem"][0]], 16)
    for sm, c in total.items():
        if (sm[0] == "h") == helping and max(seen[e].get(sm, 0) for e in seen) < c:
            g.wait_ge(T.sem[sm], c)
